import numpy as np, ml_dtypes
CORES = [23,119,17,113]
N = 4
BF = ml_dtypes.bfloat16
def gentries(a):
    return np.ascontiguousarray(a.reshape(8, 16, -1).transpose(0, 2, 1)).reshape(8, -1)
def gtable(e):
    e = np.asarray(e); return np.ascontiguousarray(e.reshape(8, -1, 16).transpose(0, 2, 1)).reshape(128, -1).astype(np.int32)
W, L, RO = 3072, 256, 4
NONE = W - 1
def link(rng, n, m, share):
    q, g, k, c = np.nonzero((m != NONE) & (rng.random(m.shape) < share))
    n[q, g, rng.integers(0, 16, len(q)), m[q, g, k, c]] = c
def world(rng, fill, stray, share):
    s = (N, 8, 16, W)
    m = np.where(rng.random(s) < fill, rng.integers(0, NONE, s), NONE); n = np.where(rng.random(s) < stray, rng.integers(0, NONE, s), NONE)
    link(rng, n, m, share)
    return n, m
def words(rng):
    pool = rng.integers(0, NONE, (N, 8, 40)); a = np.take_along_axis(pool, rng.integers(0, 40, (N, 8, L)), 2)
    return np.where(rng.random((N, 8, L)) < 0.5, a, rng.integers(0, NONE, (N, 8, L)))
def pack(x, n, m, w, z, th):
    x[..., NONE] = 255; n[..., NONE] = NONE; m[..., NONE] = NONE
    return {"x": x.reshape(N, 128, W).astype(np.float32).astype(BF), "nm": np.ascontiguousarray((n + 4096 * m).reshape(N, 128, W)).astype(np.int32),
            "w": np.stack([gtable(a) for a in w]), "z": z.reshape(N, 128, L).astype(np.float32).astype(BF),
            "th": np.repeat(th, 16, axis=1).reshape(N, 128, 1).astype(np.int32)}
def setup_inputs(rng):
    n, m = world(rng, rng.choice(np.array([0.0, 0.1, 0.4, 0.8, 1.0]), (N, 8, 1, W)), 0.3, 0.75)
    return pack(rng.integers(0, 16, (N, 8, 16, W)), n, m, words(rng), rng.integers(0, 16, (N, 8, 16, L)), rng.integers(55, 86, (N, 8)))
def setup_inputs_crowd(rng):
    n, m = world(rng, 0.7, 0.3, 0.7); x = rng.integers(0, 16, (N, 8, 16, W)); z = rng.integers(0, 16, (N, 8, 16, L)); w = np.zeros((N, 8, L), np.int64)
    for g in range(8):
        pw = rng.permutation(NONE)[:12]; po = rng.permutation(NONE)[:6]
        for q in range(N):
            mm = po[rng.integers(0, 6, (16, 12))]; mm[rng.random((16, 12)) < 0.3] = NONE; mm[:, 0] = NONE; mm[0, 0] = po[0]
            m[q, g][:, pw] = mm; n[q, g][:, po] = NONE
            k, c = np.nonzero(mm != NONE); n[q, g][rng.integers(0, 16, len(k)), mm[k, c]] = pw[c]
            n[q, g][0, po[0]] = pw[0]
            v = int(rng.integers(1, 13)); w[q, g] = pw[rng.integers(0, v, L)]; w[q, g, 0] = pw[0]; w[q, g, L - 1] = pw[0]
            near = np.clip(x[q, g][:, po[rng.integers(0, 6, L)]] + rng.integers(-1, 2, (16, L)), 0, 15)
            z[q, g] = np.where(rng.random(L) < 0.5, near, z[q, g])
            a = x[q, g][:, po[0]].copy(); far = np.where(a < 8, 15, 0)
            z[q, g][:, 0] = far if g % 2 == 0 else a
            z[q, g][:, L - 1] = a if g % 2 == 0 else far
    return pack(x, n, m, w, z, rng.integers(20, 91, (N, 8)))
def setup_inputs_ties(rng):
    proto = rng.integers(0, 12, (8, 16, 4)); kind = rng.integers(0, 4, (N, 8, W))
    x = np.stack([np.take_along_axis(proto, kind[q][:, None, :], 2) for q in range(N)])
    m = np.take_along_axis(rng.integers(0, NONE, (N, 8, 4, W)), rng.integers(0, 4, (N, 8, 16, W)), 2)
    n = np.full((N, 8, 16, W), NONE, np.int64); link(rng, n, m, 0.6)
    w = words(rng); one = np.take_along_axis(m, w[:, :, None, :], 3)[:, :, :1]
    z = np.take_along_axis(x, one, 3) + 2; z[:, :, 0] += rng.integers(-1, 2, (N, 8, L))
    return pack(x, n, m, w, z, np.full((N, 8), 32, np.int64))
def setup_inputs_hollow(rng):
    n, m = world(rng, 0.6, 0.2, 0.7); w = words(rng)
    n[:, 0::4] = NONE
    for g in (0, 4):
        o = rng.permutation(NONE); a, b = o[:L // 2], o[L // 2:]
        for q in range(N):
            if q % 2 == 0:
                m[q, g][:, a] = NONE; w[q, g, rng.permutation(L)[:L // 2]] = a
            else:
                m[q, g][:, a] = rng.integers(0, NONE, (16, L // 2))
                w[q, g] = np.where(rng.random(L) < 0.5, b[rng.integers(0, 40, L)], b[rng.integers(0, len(b), L)])
    m[:, 1::4] = np.where(rng.random((N, 2, 1, W)) < 0.8, NONE, m[:, 1::4])
    m[:, 2::4] = np.where(rng.random((N, 2, 16, W)) < 0.9, NONE, m[:, 2::4]); n[:, 2::4] = np.where(rng.random((N, 2, 16, W)) < 0.8, rng.integers(0, NONE, (N, 2, 16, W)), n[:, 2::4])
    for c in (0, NONE - 1):
        m[:, 3::4, :, c] = rng.choice(np.array([0, NONE - 1, NONE]), (N, 2, 16)); n[:, 3::4, :, c] = rng.choice(np.array([0, NONE - 1, NONE]), (N, 2, 16))
    w[:, 3::4] = rng.choice(np.array([0, NONE - 1]), (N, 2, L))
    return pack(rng.integers(0, 16, (N, 8, 16, W)), n, m, w, rng.integers(0, 16, (N, 8, 16, L)), rng.choice(np.array([0, 1, 90, 255]), (N, 8)))
def setup_inputs_mutual(rng):
    n = np.full((N, 8, 16, W), NONE, np.int64); m = np.full((N, 8, 16, W), NONE, np.int64); i = np.arange(NONE)[None, :]
    for q in range(N):
        for g in range(8):
            ob = rng.permutation(NONE); wo = rng.permutation(NONE); s = rng.permutation(NONE)[:16]; s2 = rng.permutation(s)
            m[q, g][:, wo] = ob[(i + s[:, None]) % NONE]; n[q, g][:, ob] = wo[(i - s2[:, None]) % NONE]
    th = rng.integers(40, 80, (N, 8)); th[:, ::2] = 255
    x = rng.integers(0, 16, (N, 8, 16, W)); w = words(rng); z = rng.integers(0, 16, (N, 8, 16, L))
    r = int(rng.integers(0, N)); r1, r2, r3 = (r - 1) % N, (r - 2) % N, (r - 3) % N
    th[r] = rng.permutation(np.array([241, 244, 247, 250, 253, 254, 255, 255])); won = int(rng.integers(3, 16)); h = int(rng.integers(0, 8))
    for g in range(8):
        pw = rng.permutation(np.setdiff1d(np.arange(NONE), w[[r, r1, r2], g]))[:33]; ob = rng.permutation(NONE)[:33]; tb = rng.permutation(NONE)[:32]
        m[r, g][np.isin(m[r, g], ob)] = NONE; m[r, g][:, pw] = ob; n[r, g][0::2][:, ob] = pw; x[r, g][:, ob] = 15
        m[r2, g][np.isin(m[r2, g], tb)] = NONE; m[r2, g][:, pw[:32]] = tb; n[r2, g][:, tb] = pw[:32]
        x[r2, g][:, tb] = (np.arange(32)[None, :] + rng.permutation(16)[:, None]) // 16
        p = rng.permutation(L); w[r1, g, p[:32]] = pw[:32]; w[r3, g, rng.permutation(L)[:32]] = pw[:32]
        if g == h: w[r1, g, p[32:32 + won]] = pw[32]
        m[r1, g][:, w[r1, g]] = NONE; m[r3, g][:, pw[:32]] = NONE
        if g == h:
            c = int(rng.integers(0, NONE)); m[r1, g][:, pw[32]] = c; n[r1, g][:, c] = pw[32]
    return pack(x, n, m, w, z, th)
def setup_inputs_spread(rng):
    n, m = world(rng, rng.random((N, 8, 1, W)), rng.random((N, 8, 1, W)), 0.7)
    x = rng.integers(0, 16, (N, 8, 16, W)) >> rng.integers(0, 5, (N, 8, 1, W)); z = rng.integers(0, 16, (N, 8, 16, L)) >> rng.integers(0, 5, (N, 8, 1, L))
    th = rng.integers(0, 256, (N, 8)); th[0, 0] = 0; th[1, 1] = 255
    return pack(x, n, m, words(rng), z, th)
def check_inputs(d):
    bad = []; x = np.asarray(d["x"]).astype(np.float32); z = np.asarray(d["z"]).astype(np.float32); p = np.asarray(d["nm"]).astype(np.int64); th = np.asarray(d["th"])
    if not np.all((x[..., :NONE] >= 0) & (x[..., :NONE] <= 15) & (np.floor(x[..., :NONE]) == x[..., :NONE])): bad.append("range of x")
    if not np.all(x[..., NONE] == 255): bad.append("last column of x")
    if not np.all((p >= 0) & ((p & 4095) <= NONE) & ((p >> 12) <= NONE)): bad.append("range of nm")
    if not np.all(p[..., NONE] == NONE + 4096 * NONE): bad.append("last column of nm")
    if np.min(d["w"]) < 0 or np.max(d["w"]) > NONE - 1: bad.append("range of w")
    if not np.all((z >= 0) & (z <= 15) & (np.floor(z) == z)): bad.append("range of z")
    if np.min(th) < 0 or np.max(th) > 255: bad.append("range of th")
    if not np.all(th.reshape(N, 8, 16) == th.reshape(N, 8, 16)[:, :, :1]): bad.append("th alike in a group")
    return bad
def reference(x, nm, w, z, th):
    X = x.astype(np.float32).astype(np.int32).reshape(N, 8, 16, W); P = nm.astype(np.int32).reshape(N, 8, 16, W); NA = P & 4095; MA = P >> 12
    wl = np.stack([gentries(a) for a in w]).astype(np.int32); zl = z.astype(np.float32).astype(np.int32).reshape(N, 8, 16, L)
    t0 = th.astype(np.int32).reshape(N, 8, 16)[:, :, :1]; wins = [0] * N
    lane = np.arange(L); earlier = lane[None, :] < lane[:, None]; rows = np.arange(16)[:, None]
    for t in range(RO):
        nw, nz, cnt = [], [], []
        for a in range(N):
            n, m, xx, ww, zz = NA[a], MA[a], X[a], wl[a], zl[a]
            e = np.take_along_axis(m, ww[:, None, :], 2); ef = e.reshape(8, 1, 16 * L)
            D = np.add.reduce(np.abs(zz[:, :, None, :] - np.take_along_axis(xx, ef, 2).reshape(8, 16, 16, L)), axis=1)
            real = np.any(np.take_along_axis(n, ef, 2).reshape(8, 16, 16, L) == ww[:, None, None, :], axis=1)
            key = np.where(real, D, D + 8192); k = np.argmin(key, axis=1)[:, None, :]
            o = np.take_along_axis(e, k, 1)[:, 0]; hit = np.take_along_axis(key, k, 1)[:, 0] < t0[a] + (wins[a] & 31)
            no = np.take_along_axis(n, o[:, None, :], 2); xo = np.take_along_axis(xx, o[:, None, :], 2)
            mn = np.take_along_axis(m, no.reshape(8, 1, 16 * L), 2).reshape(8, 16, 16, L)
            cand = np.any(mn == o[:, None, None, :], axis=1) & (no != NONE)
            few = np.where(cand, np.add.reduce((mn != NONE).astype(np.int32), axis=1), 17); j = np.argmin(few, axis=1)[:, None, :]
            nw.append(np.where(np.any(cand, axis=1), np.take_along_axis(no, j, 1)[:, 0], ww)); nz.append(xo); cnt.append(int(np.count_nonzero(hit)))
            h = hit[:, None, :]
            n2 = np.where(h, np.where(no == ww[:, None, :], no, NONE), np.where(rows == ((lane + t) & 15), ww[:, None, :], no))
            x2 = np.where(h, xo, xo + np.clip(zz - xo, -2, 2)); m2 = np.where(e == o[:, None, :], e, NONE)
            go = ~np.any((o[:, :, None] == o[:, None, :]) & earlier, axis=2) & (o != NONE)
            gw = ~np.any((ww[:, :, None] == ww[:, None, :]) & earlier, axis=2) & hit
            for g in range(8):
                c = o[g][go[g]]; n[g][:, c] = n2[g][:, go[g]]; xx[g][:, c] = x2[g][:, go[g]]
                m[g][:, ww[g][gw[g]]] = m2[g][:, gw[g]]
        d = 1 + t % (N - 1); wins = cnt
        wl = np.stack([nw[(a - d) % N] for a in range(N)]).astype(np.int32); zl = np.stack([nz[(a - d) % N] for a in range(N)])
    return {"ynm": (NA + 4096 * MA).reshape(N, 128, W).astype(np.float32), "yw": np.stack([gtable(a) for a in wl]).astype(np.float32), "yz": zl.reshape(N, 128, L).astype(np.float32).astype(BF)}

@@ -1,0 +1,592 @@
+import numpy as np
+from concourse.mybir import AluOpType, ActivationFunctionType, AxisListType
+
+W, L, RO = 3072, 256, 4
+NONE = W - 1
+WP = W + 16
+MOFF = 2 ** 23 + 1
+NCH = 6
+OCH = 6
+DUP = 2
+NV = 2
+NBK = 4
+TRIES = 4000
+SEED = 0
+C = {"cyc": 0.83, "g": 1.56, "s": 3.8, "tt": 2.0, "v": 50, "a": 65, "pe": 0.55, "pf": 10, "lat": 120,
+     "dma": 2000, "bw": 180.0, "rem": 2500, "look": 120}
+
+F, B, I32, U16 = "float32", "bfloat16", "int32", "uint16"
+SIZE = {F: 4, B: 2, I32: 4, U16: 2}
+SCRATCH = {}
+PLACE = {}
+
+
+def _own(name, cols, d):
+    SCRATCH[name] = ("sbuf", [128, cols], d)
+    PLACE[name] = (name, 0, cols, d)
+
+
+def _pool(name, cols, d):
+    p = "pool_" + d
+    at = SCRATCH[p][1][1] if p in SCRATCH else 0
+    SCRATCH[p] = ("sbuf", [128, at + (cols + 15) // 16 * 16], d)
+    PLACE[name] = (p, at, cols, d)
+
+
+for _n, _c, _d in [("NMI", W, I32), ("F1", W, F), ("NT", WP, F), ("MT", WP, F), ("M4", WP, F), ("XT", WP, B),
+                   ("XG", 4096, B), ("AB", 4096, B), ("EQ", 4096, B), ("EQ2", 4096, B), ("CN", 4096, B),
+                   ("WIN", 16, I32), ("THI", 16, I32), ("WF", 16, F), ("WFS", 16, F)]:
+    _own(_n, _c, _d)
+for _t in range(RO + 1):
+    _own("Z%d" % _t, 256, B)
+for _t in range(RO):
+    _own("WU%d" % _t, 16, U16)
+    _own("XO%d" % _t, 256, B)
+    _own("WS%d" % _t, 16, U16)
+for _d, _l in [
+    (F, "EP 288 NP 288 TR 544 TR2 544 EF 256 UL 256 WB0 %d WB1 %d OB %d RR 256 RW0 256 RW1 256 RUN 128 CH0 128 CH1 128 "
+        "FO1 64 WL 16 OL 16 OLM 16 OH 16 HL 16 RS 64 RS2 64 SF1 32 AL 16 AL2 16 DEw 256 DSw 256 DDw 16 DMw 16 DEo 256 "
+        "DSo 256 DDo 16 DMo 16 NE 256 C1 256 Q1 256 B1 256 NE2 256 C2 256 THF 1 THR 1 SC1 1 PF 16 ZT 144 G32 128 ID32 128 "
+        "PRM 512 PL 4 DG 272 NDG 272 HZ 256 HS 16 BI 16" % ((256 * DUP,) * 3)),
+    (B, "HI 256 LO 256 TT 256 TT2 256 RH 256 HLB 16 X1 256 X2 256 ZS 144 G2 128 GM2 128 G3K 128 GM1 128 G23 128 ID 128 "
+        "IDM 128 ID22 128 ID23 128 IM64 128 ONES 128 DGB 256 KC 256 KC2 256"),
+    (I32, "ENDI 32 ANDI 32 WI 16 WA 16 SC2 1 SC3 1 PI 1 PJ 4 CI 272 CJ 272 CK 256 PK 4"),
+    (U16, "OFF 256 OF2 256 OU 16 SW 32 SO 32 EXO 16 TRO 16"),
+]:
+    for _n, _c in zip(_l.split()[0::2], _l.split()[1::2]):
+        _pool(_n, int(_c), _d)
+PSUM = ("PD0", "PD1", "PD2", "PA0", "PA1", "PB0", "PB1", "PM")
+for _n in PSUM:
+    SCRATCH[_n] = ("psum", [128, 512], F)
+    PLACE[_n] = (_n, 0, 512, F)
+
+SEMAPHORES = (["cv", "cs", "cp", "cg", "sent"] + ["d%d" % i for i in range(NCH + OCH + 8)]
+              + ["az%d" % t for t in range(RO)] + ["aw%d" % t for t in range(RO)])
+
+A = AluOpType
+AF = ActivationFunctionType
+
+
+def build(g, core, T, topo):
+    ops = []
+    rank = T.rank_of(core)
+    n = len(T.cores)
+    V, S, P = g.vector, g.scalar, g.tensor
+    phase, rnd = ["0"], [0]
+
+    def v(name, a=0, b=None, s=1):
+        buf, at, cols, d = PLACE[name]
+        b = cols if b is None else b
+        ap = T[buf][:, at + a:at + b] if s == 1 else T[buf][:, at + a:at + b:s]
+        return {"ap": ap, "n": len(range(a, b, s)), "rg": [(buf, at + a, at + b)], "two": SIZE[d] == 2, "ps": buf in PSUM,
+                "ind": False, "off": [], "lab": name}
+
+    def ind(win, off):
+        return {"ap": win["ap"].indirect(off["ap"]), "n": 16 * off["n"], "rg": win["rg"], "off": off["rg"], "two": False,
+                "ps": False, "ind": True, "lab": win["lab"]}
+
+    def ext(ap, key, a=0, b=1):
+        return {"ap": ap, "n": b - a, "rg": [(key, a, b)], "off": [], "ind": False, "lab": key}
+
+    def add(q, fn, out, ins, dur, kind="c", sem=None, cnt=0):
+        r, w = [], []
+        for x in ins:
+            if isinstance(x, dict):
+                r += x["rg"] + x["off"]
+        if out is not None:
+            w += out["rg"]
+            r += out["off"]
+        ops.append({"q": q, "fn": fn, "r": r, "w": w, "kind": kind, "sem": sem, "cnt": cnt, "dur": dur,
+                    "lab": (q or "x") + (out["lab"] if out else "send") + phase[0], "rnd": rnd[0]})
+
+    def cost(q, out, a, base):
+        fx = C["v"] if q == "v" else C["a"]
+        rate = C["s"] if out["ind"] else C["g"] if a["ind"] else base
+        return fx + max(20, a["n"] * rate) * C["cyc"]
+
+    def ap(x):
+        return x["ap"] if isinstance(x, dict) else x
+
+    def ts(out, a, s1, s2, o0, o1=None):
+        d = cost("v", out, a, 0.5 if out["two"] and a["two"] else 1)
+        if o1 is None:
+            add("v", lambda: V.tensor_scalar(ap(out), ap(a), ap(s1), None, o0), out, [a, s1], d)
+        else:
+            add("v", lambda: V.tensor_scalar(ap(out), ap(a), ap(s1), ap(s2), o0, o1), out, [a, s1, s2], d)
+
+    def tt(out, a, b, op):
+        add("v", lambda: V.tensor_tensor(ap(out), ap(a), ap(b), op), out, [a, b],
+            cost("v", out, a, 1 if a["ps"] or b["ps"] else C["tt"]))
+
+    def cp(out, a):
+        add("v", lambda: V.tensor_copy(ap(out), ap(a)), out, [a], cost("v", out, a, 0.5 if out["two"] and a["two"] else 1))
+
+    def ms(out, c):
+        add("v", lambda: V.memset(ap(out), c), out, [], cost("v", out, out, 1))
+
+    def scan(out, a, b):
+        add("v", lambda: V.tensor_tensor_scan(ap(out), ap(a), ap(b), 0.0, A.mult, A.add), out, [a, b], cost("v", out, a, 1))
+
+    def tr(out, a):
+        add("v", lambda: V.transpose(ap(out), ap(a)), out, [a], cost("v", out, a, 1))
+
+    def act(out, a, f, scale=None, bias=None):
+        d = cost("s", out, a, 1)
+        if bias is not None:
+            add("s", lambda: S.activation(ap(out), ap(a), f, bias=ap(bias), scale=scale), out, [a, bias], d)
+        elif scale is not None:
+            add("s", lambda: S.activation(ap(out), ap(a), f, scale=scale), out, [a], d)
+        else:
+            add("s", lambda: S.activation(ap(out), ap(a), f), out, [a], d)
+
+    def mm(out, lt, rhs, st, sp):
+        add("p", lambda: P.matmul(ap(out), ap(lt), ap(rhs), st, sp), out, [lt, rhs],
+            C["pf"] + max(64, rhs["n"]) * C["pe"] * (1 if rhs["two"] else 4))
+
+    def merge(k):
+        l = ops[-k:]
+        del ops[-k:]
+        fns = [o["fn"] for o in l]
+        o = dict(l[0])
+        o.update({"fn": lambda: [f() for f in fns][-1], "r": [x for y in l for x in y["r"]],
+                  "w": [x for y in l for x in y["w"]], "dur": sum(y["dur"] for y in l)})
+        ops.append(o)
+
+    nd = [0]
+
+    def dma(q, out, src, nbytes):
+        s = "d%d" % nd[0]
+        nd[0] += 1
+        e = {"y": g.sync, "s": g.scalar}[q]
+        add(q, lambda: e.dma_start(ap(out), ap(src)), out, [src], nbytes / C["bw"], "dma", s, 16)
+
+    sent = [0]
+
+    def move(t, out, src, sem):
+        dst = T.cores[(rank + 1 + t % (n - 1)) % n]
+        frm = T.cores[(rank - 1 - t % (n - 1)) % n]
+        eng = topo.engines(core, dst)[:8]
+        m = sum(1 << e for e in eng)
+        rid, pid, _ = topo.addr(dst)
+        sent[0] += len(eng)
+        add("g", lambda: g.remote_dma(ap(out), ap(src), T.sem[sem], T.sem.sent, pid, rid, m), None, [src],
+            C["rem"] + src["n"] * 5, "rem")
+        add(None, None, out, [], 0, "ext", sem, len(topo.engines(frm, core)[:8]))
+
+    cw = W // NCH
+    dma("s", v("WIN"), ext(T.w[:], "w"), 8192)
+    for c in range(NCH):
+        dma("y", v("NMI", c * cw, (c + 1) * cw), ext(T.nm[:, c * cw:(c + 1) * cw], "nm"), 512 * cw)
+    dma("s", v("Z0"), ext(T.z[:], "z"), 65536)
+    dma("s", v("THI", 0, 1), ext(T.th[:], "th"), 4096)
+    add("g", lambda: g.iota(ap(v("PI")), [[1, 1]], 0, 1), v("PI"), [], 140)
+    add("g", lambda: g.iota(ap(v("CI")), [[1, 272]], 0, 0), v("CI"), [], 600)
+    dma("y", v("XT", 0, W), ext(T.x[:], "x"), 256 * W)
+    bias = {}
+    for j, x in enumerate([2.0 ** 23 - 0.5, float(MOFF), 1.0, -32.0 * (MOFF + NONE - 1), -4096.0 * MOFF, -float(MOFF),
+                           128.0, 8224.0, 61440.0, 2.0 ** 21]):
+        ms(v("BI", j, j + 1), x)
+        bias[x] = v("BI", j, j + 1)
+    pi = v("PI")
+    ts(v("PJ", 0, 1), pi, 112, None, A.bitwise_and)
+    ts(v("PJ", 1, 2), pi, 15, None, A.bitwise_and)
+    ts(v("PJ", 2, 3), pi, 1, None, A.bitwise_and)
+    ts(v("PJ", 3, 4), pi, 4, 1, A.logical_shift_right, A.bitwise_and)
+    cp(v("PF", 0, 4), v("PJ"))
+    cp(v("PF", 4, 5), pi)
+    pf = lambda j: v("PF", j, j + 1)
+    g16, acol, pcol = pf(0), pf(1), pf(4)
+    ts(v("CJ"), v("CI"), 15, None, A.bitwise_and)
+    ts(v("DG"), v("CJ"), acol, None, A.is_equal)
+    cp(v("EXO"), v("CI", 0, 16))
+    tt(pf(5), pf(2), pf(3), A.not_equal)
+    ts(pf(6), acol, 16.0, None, A.mult)
+    ts(pf(7), pf(5), 272.0, pf(6), A.mult, A.add)
+    ts(v("TRO"), v("CI", 0, 16), pf(7), None, A.add)
+    act(v("NDG"), v("DG"), AF.Identity, -1.0, bias[1.0])
+    act(v("DGB"), v("DG", 0, 256), AF.Identity)
+    ts(pf(8), acol, float(W), None, A.add)
+    ts(v("HZ"), v("CJ", 0, 256), 0.0, 2.0, A.not_equal, A.mult)
+    scan(v("HS"), v("HZ", 0, 16), v("DG", 0, 16))
+    ts(pf(9), v("HS", 15, 16), 2.0, None, A.mult)
+    ts(v("ZT"), v("CI", 0, 144), g16, 15.0, A.subtract, A.is_equal)
+    act(v("ZS"), v("ZT"), AF.Identity, 2048.0)
+    ts(v("ID32"), v("CI", 0, 128), pcol, None, A.is_equal)
+    for nm_, x in [("ID", 1.0), ("IDM", -1.0), ("ID22", 2.0 ** 22), ("ID23", 2.0 ** 23), ("IM64", -64.0)]:
+        act(v(nm_), v("ID32"), AF.Identity, x)
+    ts(v("CK"), v("CI", 0, 256), 240, None, A.bitwise_and)
+    ts(v("KC"), v("CK"), 8.0, None, A.mult)
+    act(v("KC2"), v("KC"), AF.Identity, -32.0, bias[61440.0])
+    ts(v("G32"), v("CK", 0, 128), g16, None, A.is_equal)
+    for nm_, x in [("G2", 2.0), ("GM2", -2.0), ("G3K", 3072.0), ("GM1", -1.0), ("G23", 2.0 ** 23)]:
+        act(v(nm_), v("G32"), AF.Identity, x)
+    ms(v("ONES"), 1.0)
+    ts(v("PK"), v("CI", 0, 4), pcol, None, A.add)
+    ts(v("PK"), v("PK"), 15, None, A.bitwise_and)
+    ts(v("PL"), v("PK"), g16, None, A.add)
+    for t in range(RO):
+        ts(v("PRM", 128 * t, 128 * t + 128), v("CI", 0, 128), v("PL", t, t + 1), None, A.is_equal)
+    for nm_ in ("EP", "NP"):
+        ms(v(nm_, 0, 16), 0.0)
+        ms(v(nm_, 272, 288), 0.0)
+    ms(v("RS"), 0.0)
+    for nm_ in ("NT", "MT", "XT"):
+        ms(v(nm_, W, WP), 0.0)
+    for c in range(NCH):
+        a, b = c * cw, (c + 1) * cw
+        ts(v("F1", a, b), v("NMI", a, b), 4097.0, None, A.add)
+        act(v("MT", a, b), v("F1", a, b), AF.Identity, 2.0 ** -12, bias[2.0 ** 23 - 0.5])
+        ts(v("NMI", a, b), v("NMI", a, b), 4095, None, A.bitwise_and)
+        cp(v("NT", a, b), v("NMI", a, b))
+    cp(v("WU0"), v("WIN"))
+    cp(v("THF"), v("THI", 0, 1))
+    ts(v("THR"), v("THF"), 2048.0, None, A.mult)
+
+    Nw, Mw, Xw = v("NT", 0, W), v("MT", 0, W), v("XT", 0, W)
+    kb = 16 // NBK
+    m = 16 * kb
+
+    def turn(src, dst):
+        tr(v(dst, 0, 256), v(src, 16, 272))
+        tr(v(dst, 256, 544), v(src))
+
+    def spread(src, tmp, dst, bi):
+        tt(v(tmp), ind(v(src), v("EXO")), v("DG", 0, 256), A.mult)
+        mm(v("PM", 0, 256), v("G32"), v(tmp), True, True)
+        for d in range(DUP):
+            act(v(dst, 256 * d, 256 * d + 256), v("PM", 0, 256), AF.Identity, None if bi is None else 1.0, bi)
+
+    def first_of(vl, vb, pl, s, out):
+        tt(v("DE" + s), ind(v(vl), v("EXO")), v(vb, 0, 256), A.is_equal)
+        scan(v("DS" + s), v("HZ"), v("DE" + s))
+        ts(v("DD" + s), v("DS" + s, 15, 256, 16), pf(9), pf(8), A.is_ge, A.mult)
+        tt(v("DM" + s), v("DD" + s), v(pl), A.max)
+        cp(v(out, 0, 32, 2), v("DM" + s))
+
+    def reduce16(out, src, c, st, sp):
+        for a in range(16):
+            mm(out, v("ZS", 15 - a, 143 - a), v(src, c * kb * 256 + a, (c + 1) * kb * 256, 16), st and a == 0, sp and a == 15)
+        merge(16)
+
+    def lx(name, c):
+        return v(name, 16 * kb * c, 16 * kb * (c + 1))
+
+    for t in range(RO):
+        last = t == RO - 1
+        rnd[0] = t
+        wu, z, wb, rw, xo = v("WU%d" % t), v("Z%d" % t), "WB%d" % (t % 2), "RW%d" % (t % 2), v("XO%d" % t)
+        if last:
+            dma("y", v("M4"), v("MT"), 512 * WP)
+        phase[0] = "l"
+        act(v("EP", 16, 272), ind(Mw, wu), AF.Identity)
+        cp(v("WL"), wu)
+        spread("WL", rw, wb, None)
+        turn("EP", "TR")
+        ts(v("OFF"), ind(v("TR"), v("TRO")), float(MOFF), None, A.subtract)
+        first_of("WL", wb, "WL", "w", "SW")
+        for k in range(0, 16, DUP):
+            tt(v("EQ", 256 * k, 256 * (k + DUP)), ind(Nw, v("OFF", 16 * k, 16 * (k + DUP))), v(wb), A.is_equal)
+        for i in range(8):
+            xg, ab, pd = v("XG", 512 * i, 512 * i + 512), v("AB", 512 * i, 512 * i + 512), "PD%d" % (i % 3)
+            if i >= 8 - NV:
+                for k in (2 * i, 2 * i + 1):
+                    tt(v("XG", 256 * k, 256 * k + 256), ind(Xw, v("OFF", 16 * k, 16 * k + 16)), z, A.subtract)
+                act(ab, xg, AF.Abs)
+                continue
+            act(xg, ind(Xw, v("OFF", 32 * i, 32 * i + 32)), AF.Identity)
+            for h in range(2):
+                o = v(pd, 256 * h, 256 * h + 256)
+                mm(o, v("ID"), v("XG", 512 * i + 256 * h, 512 * i + 256 * h + 256), True, False)
+                mm(o, v("IDM"), z, False, True)
+            merge(4)
+            act(ab, v(pd), AF.Abs)
+        act(v("EF"), ind(v("TR"), v("TRO")), AF.Identity, 1.0, bias[-float(MOFF)])
+        act(v("HI"), v("EF"), AF.Identity, 2.0 ** -6, bias[128.0])
+        mm(v("PM", 256, 512), v("ID32"), v("EF"), True, False)
+        mm(v("PM", 256, 512), v("IM64"), v("HI"), False, True)
+        act(v("LO"), v("PM", 256, 512), AF.Identity, 1.0, bias[8224.0])
+        for c in range(NBK):
+            pa, pb = v("PA%d" % (c % 2), 0, m), v("PB%d" % (c % 2), 0, m)
+            mm(pa, v("ID"), lx("KC", c), True, False)
+            reduce16(pa, "AB", c, False, False)
+            reduce16(pb, "EQ", c, True, True)
+            act(lx("TT", c), pb, AF.Relu, -1.0, bias[1.0])
+            mm(pa, v("ID23"), lx("TT", c), False, True)
+            dst = "RUN" if c == 0 else "CH%d" % (c % 2)
+            tt(v(dst, 0, 2 * m, 2), pa, lx("HI", c), A.add)
+            tt(v(dst, 1, 2 * m, 2), pa, lx("LO", c), A.add)
+            if c > 0:
+                tt(v("RUN"), v("RUN"), v(dst), A.min)
+        tt(v("FO1"), v("RUN", 0, 64), v("RUN", 64, 128), A.min)
+        tt(v("ENDI"), v("FO1", 0, 32), v("FO1", 32, 64), A.min)
+        ts(v("ANDI"), v("ENDI"), 127, None, A.bitwise_and)
+        ts(v("OH"), v("ANDI", 0, 32, 2), 64.0, -32.0, A.mult, A.add)
+        tt(v("OL"), v("OH"), v("ANDI", 1, 32, 2), A.add)
+        cp(v("OU"), v("OL"))
+        phase[0] = "s"
+        act(v("NP", 16, 272), ind(Nw, v("OU")), AF.Identity)
+        spread("OL", "RR", "OB", bias[float(MOFF)])
+        act(xo, ind(Xw, v("OU")), AF.Identity)
+        move(t, v("Z%d" % (t + 1)), xo, "az%d" % t)
+        turn("NP", "TR2")
+        cp(v("OF2"), ind(v("TR2"), v("TRO")))
+        act(v("UL"), ind(v("TR2"), v("TRO")), AF.Identity)
+        ts(v("AL"), v("OL"), float(NONE), 2.0 ** 23, A.is_equal, A.mult)
+        act(v("AL2"), v("WL"), AF.Identity, 1.0, bias[2.0 ** 21])
+        tt(v("RS", 0, 16), v("AL"), v("AL2"), A.add)
+        for c in range(NBK):
+            for k in range(c * kb, (c + 1) * kb, DUP):
+                tt(v("EQ2", 256 * k, 256 * (k + DUP)), ind(Mw, v("OF2", 16 * k, 16 * (k + DUP))), v("OB"), A.is_equal)
+            for k in range(c * kb, (c + 1) * kb, 2):
+                act(v("CN", 256 * k, 256 * (k + 2)), ind(Mw, v("OF2", 16 * k, 16 * (k + 2))), AF.Relu, 32.0,
+                    bias[-32.0 * (MOFF + NONE - 1)])
+            pa, pb = v("PA%d" % (c % 2), 0, m), v("PB%d" % (c % 2), 0, m)
+            mm(pa, v("ID32"), lx("UL", c), True, False)
+            mm(pa, v("ID"), lx("KC2", c), False, False)
+            reduce16(pa, "CN", c, False, False)
+            reduce16(pb, "EQ2", c, True, True)
+            act(lx("TT2", c), pb, AF.Sign)
+            mm(pa, v("ID22"), lx("TT2", c), False, True)
+            tt(v("RS2"), pa, v("RS" if c == 0 else "RS2"), A.max)
+        tt(v("SF1"), v("RS2", 0, 32), v("RS2", 32, 64), A.max)
+        tt(v("WI"), v("SF1", 0, 16), v("SF1", 16, 32), A.max)
+        ts(v("WA"), v("WI"), 4095, None, A.bitwise_and)
+        if last:
+            cp(v("WFS"), v("WA"))
+            move(t, v("WF"), v("WFS"), "aw%d" % t)
+        else:
+            cp(v("WS%d" % t), v("WA"))
+            move(t, v("WU%d" % (t + 1)), v("WS%d" % t), "aw%d" % t)
+        phase[0] = "z" if last else "w"
+        ts(v("HL"), v("ENDI", 1, 32, 2), v("THR"), None, A.is_lt)
+        tt(v("RH"), ind(v("HL"), v("EXO")), v("DG", 0, 256), A.mult)
+        mm(v("PD0", 0, 256), v("G23"), v("RH"), True, False)
+        mm(v("PD0", 0, 256), v("G3K"), v("RH"), False, True)
+        mm(v("PD2", 0, 256), v("G3K"), v("RH"), True, False)
+        mm(v("PD2", 0, 256), v("GM1"), v("RH"), False, True)
+        ts(v("OLM"), v("OL"), float(MOFF), None, A.add)
+        first_of("OLM", "OB", "OL", "o", "SO")
+        tt(v("NE2"), ind(Mw, wu), v("OB", 0, 256), A.not_equal)
+        tt(v("C2"), v("NE2"), v("PD0", 0, 256), A.mult)
+        mm(v("PD0", 256, 512), v("G32"), v(rw), True, True)
+        mm(v("PD2", 256, 512), v("PRM", 128 * t, 128 * t + 128), v(rw), True, True)
+        tt(v("NE"), v("NP", 16, 272), v("PD0", 256, 512), A.not_equal)
+        tt(v("B1"), ind(Nw, v("OU")), v("NDG", t, t + 256), A.mult)
+        tt(v("C1"), v("NE"), v("PD2", 0, 256), A.mult)
+        tt(v("Q1"), v("C1"), v("PD2", 256, 512), A.max)
+        if not last:
+            for h, (ga, gb) in enumerate((("G2", "GM2"), ("GM2", "G2"))):
+                o = v("PD1", 256 * h, 256 * h + 256)
+                mm(o, v("ID"), xo, True, False)
+                mm(o, v(ga), v("RH"), False, False)
+                mm(o, v(gb), v("DGB"), False, True)
+            tt(v("X1"), z, v("PD1", 0, 256), A.max)
+            tt(v("X2"), v("X1"), v("PD1", 256, 512), A.min)
+            act(v("HLB"), v("HL"), AF.Identity)
+            mm(v("PM", 16, 32), v("ONES"), v("HLB"), True, True)
+            o, a = v("SC1"), v("PM", 16, 32)
+            add("v", lambda o=o, a=a: V.tensor_reduce(ap(o), ap(a), AxisListType.X, A.add), o, [a], 70)
+            cp(v("SC2"), v("SC1"))
+            ts(v("SC3"), v("SC2"), 31, None, A.bitwise_and)
+            ts(v("THR"), v("SC3"), v("THF"), 2048.0, A.add, A.mult)
+        for b in range(15, -1, -1):
+            so, sw = v("SO", 2 * b, 2 * b + 1), v("SW", 2 * b, 2 * b + 1)
+            l0, l1 = 16 * b, 16 * b + 16
+            tt(ind(v("M4" if last else "MT"), sw), v("EP", 16 + l0, 16 + l1), v("C2", l0, l1), A.max)
+            if not last:
+                cp(ind(v("XT"), so), v("X2", l0, l1))
+            tt(ind(v("NT"), so), v("B1", l0, l1), v("Q1", l0, l1), A.max)
+        ms(v("NT", NONE, W), float(NONE))
+        if not last:
+            ms(v("XT", NONE, W), 255.0)
+    ow = W // OCH
+    for c in range(OCH):
+        a, b = c * ow, (c + 1) * ow
+        pd = v("PD%d" % (c % 3), 0, ow)
+        act(pd, v("M4", a, b), AF.Identity, 4096.0, bias[-4096.0 * MOFF])
+        tt(v("F1", a, b), v("NT", a, b), pd, A.add)
+        dma("y", ext(T.ynm[:, a:b], "ynm", a, b), v("F1", a, b), 512 * ow)
+    dma("y", ext(T.yz[:], "yz"), v("Z%d" % RO), 65536)
+    dma("y", ext(T.yw[:], "yw"), v("WF"), 8192)
+    return ops, sent[0]
+
+
+def hazards(ops):
+    acc = {}
+    for i, o in enumerate(ops):
+        pre = {}
+        both = [(x, False) for x in sorted(set(o["r"]))] + [(x, True) for x in sorted(set(o["w"]))]
+        for (buf, a, b), wr in both:
+            bank = buf in PSUM
+            for (j, a2, b2, w2) in acc.get(buf, []):
+                hit = a < b2 and a2 < b and (wr or w2)
+                if hit or bank:
+                    pre[j] = pre.get(j, False) or hit or ops[j]["q"] != o["q"]
+        for (buf, a, b), wr in both:
+            l = acc.setdefault(buf, [])
+            if buf in PSUM:
+                l[:] = [e for e in l if ops[e[0]]["q"] == o["q"]][-6:]
+            elif wr:
+                l[:] = [e for e in l if not (a <= e[1] and e[2] <= b)]
+            l.append((i, a, b, wr))
+        if o["kind"] == "ext":
+            pre = {i - 1: False}
+        if o["kind"] == "dma" and o["q"] == "y" and not pre:
+            pre = {j: False for j in range(i) if ops[j]["q"] == "y"}
+        o["pre"] = {j: w for j, w in pre.items() if ops[j]["kind"] != "rem" or o["kind"] == "ext"}
+
+
+def one_pass(res, dur, nxt, npre, prio, ready0):
+    n = len(res)
+    left, ready, start = list(npre), list(ready0), [0.0] * n
+    free = {q: 0.0 for q in ("v", "s", "p", "g", "D", None)}
+    cand = {q: [] for q in free}
+    for i in range(n):
+        if left[i] == 0:
+            cand[res[i]].append(i)
+    order = []
+    while len(order) < n:
+        pick = None
+        for q, l in cand.items():
+            if l:
+                t0 = max(free[q], min(ready[i] for i in l))
+                if pick is None or t0 < pick[0]:
+                    pick = (t0, q)
+        t0, q = pick
+        l = cand[q]
+        best = max((i for i in l if ready[i] <= t0 + C["look"]), key=lambda i: prio[i])
+        if ready[best] > t0:
+            fit = [i for i in l if ready[i] <= t0 and t0 + dur[i] <= ready[best] + 30]
+            if fit:
+                best = max(fit, key=lambda i: prio[i])
+        l.remove(best)
+        start[best] = max(t0, ready[best])
+        end = start[best] + dur[best]
+        free[q] = end
+        order.append(best)
+        for s, la in nxt[best]:
+            ready[s] = max(ready[s], end + la)
+            left[s] -= 1
+            if left[s] == 0:
+                cand[res[s]].append(s)
+    return order, start
+
+
+def schedule(ops):
+    n = len(ops)
+    res = ["D" if o["kind"] == "dma" else o["q"] for o in ops]
+    dur = [500 if o["kind"] == "rem" else o["dur"] for o in ops]
+    succ, pred = [[] for _ in ops], [[] for _ in ops]
+    for i, o in enumerate(ops):
+        for j, w in sorted(o["pre"].items()):
+            p = ops[j]
+            la = 0 if (p["q"] == "p" and o["q"] == "p") or not w else C["lat"]
+            la += C["dma"] if o["kind"] == "dma" and w else 0
+            la += p["dur"] - 500 if p["kind"] == "rem" else 0
+            succ[j].append((i, la))
+            pred[i].append((j, la))
+    prio = [0.0] * n
+    for i in range(n - 1, -1, -1):
+        prio[i] = dur[i] + max([la + prio[s] for s, la in succ[i]], default=0.0)
+    npre, nsucc = [len(p) for p in pred], [len(p) for p in succ]
+    r0 = [C["dma"] if res[i] == "D" else 0.0 for i in range(n)]
+
+    def forward(pr):
+        order, st = one_pass(res, dur, succ, npre, pr, r0)
+        return max(st[i] + dur[i] for i in range(n)), order, st
+
+    def justified(st):
+        _, sb = one_pass(res, dur, pred, nsucc, [st[i] + dur[i] for i in range(n)], [0.0] * n)
+        return [sb[i] + dur[i] for i in range(n)]
+
+    groups = {}
+    for i, o in enumerate(ops):
+        groups.setdefault(o["lab"], []).append(i)
+        groups.setdefault((o["lab"], o["rnd"]), []).append(i)
+    groups = list(groups.values())
+    rng = np.random.RandomState(SEED)
+    best = forward(prio)
+    for it in range(TRIES):
+        if it % 200 == 0:
+            pr = justified(best[2])
+        else:
+            pr = list(prio)
+            for _ in range(int(rng.randint(1, 4))):
+                grp = groups[int(rng.randint(len(groups)))]
+                if rng.rand() < 0.3:
+                    grp = grp[int(rng.randint(len(grp))):]
+                d = float(rng.choice([-1, 1]) * rng.choice([200, 600, 2000, 6000]))
+                for i in grp:
+                    pr[i] += d
+        got = forward(pr)
+        if got[0] <= best[0]:
+            best, prio = got, pr
+    order = best[1]
+    first = [i for i in order if ops[i]["kind"] == "dma" and not any(ops[i]["pre"].values())]
+    return first + [i for i in order if i not in set(first)]
+
+
+def emit(g, T, ops, order, sent):
+    Q = {"v": g.vector, "s": g.scalar, "p": g.tensor, "g": g, "y": g.sync}
+    at = {i: k for k, i in enumerate(order)}
+    known = {q: {} for q in Q}
+
+    def sem_of(p):
+        return p["sem"] if p["kind"] != "c" else "c" + p["q"]
+
+    for i in order:
+        o = ops[i]
+        if o["kind"] == "ext":
+            o["clock"] = {o["sem"]: at[i]}
+            continue
+        kn = known[o["q"]]
+        waits = {}
+        need = [j for j, w in o["pre"].items() if w and not (ops[j]["q"] == "p" and o["q"] == "p")]
+        for j in sorted(need, key=lambda j: -at[j]):
+            p = ops[j]
+            if kn.get(sem_of(p), -1) >= at[j]:
+                continue
+            waits[sem_of(p)] = j
+            p["mark"] = True
+            for s2, k2 in p["clock"].items():
+                kn[s2] = max(kn.get(s2, -1), k2)
+        o["waits"] = waits
+        o["clock"] = dict(kn)
+        if o["kind"] != "rem":
+            o["clock"][sem_of(o)] = at[i]
+    count = {}
+    for i in order:
+        o = ops[i]
+        if o["kind"] == "c" and o.get("mark"):
+            count[o["q"]] = count.get(o["q"], 0) + 1
+            o["val"] = count[o["q"]]
+        elif o["kind"] != "c":
+            o["val"] = o["cnt"]
+    for i in order:
+        o = ops[i]
+        if o["kind"] == "ext":
+            continue
+        for s, j in o["waits"].items():
+            Q[o["q"]].wait_ge(T.sem[s], ops[j]["val"])
+        ins = o["fn"]()
+        if o["kind"] == "dma":
+            ins.then_inc(T.sem[o["sem"]], 16)
+        elif o["kind"] == "c" and o.get("mark"):
+            ins.then_inc(T.sem["c" + o["q"]], 1)
+    g.wait_ge(T.sem.sent, sent)
+    for o in ops:
+        if o["kind"] == "dma" and not o.get("mark"):
+            g.wait_ge(T.sem[o["sem"]], 16)
+
+
+ORDER = []
+
+
+def rank_program(g, core, T, topo):
+    if T.rank_of(core) is None:
+        return
+    ops, sent = build(g, core, T, topo)
+    hazards(ops)
+    if not ORDER:
+        ORDER.extend(schedule(ops))
+    emit(g, T, ops, ORDER, sent)

@@ -4,19 +4,31 @@ from concourse.mybir import AluOpType, ActivationFunctionType, AxisListType
 W, L, RO = 3072, 256, 4
 NONE = W - 1
 WP = W + 16
-MOFF = 2 ** 23 + 1
+CM = 1.5 * 2 ** 35
+HALF = 1536
+BIG = 8192.0
 NCH = 6
 OCH = 6
-DUP = 2
-NV = 2
-NBK = 4
-TRIES = 4000
+NV = (0, 1)
+GW = 1
+TRIES = 12000
+STEPS = 8000
 SEED = 0
-C = {"cyc": 0.83, "g": 1.56, "s": 3.8, "tt": 2.0, "v": 50, "a": 65, "pe": 0.55, "pf": 10, "lat": 120,
-     "dma": 2000, "bw": 180.0, "rem": 2500, "look": 120}
+HEAT = 100
+C = {"cyc": 0.83, "g": 1.56, "s": 3.8, "tt": 2.0, "v": 50, "a": 65, "pe": 0.5, "pf": 10, "lat": 120,
+     "dma": 2000, "bw": 180.0, "rem": 2500}
+START, PERIOD = 12.5, 23.5
+PLAN = {"sNElA": (0.1, 0), "sWBlA": (-1.0, 0.2), "sXGlA": (1.1, 1.1), "sABlA": (2.6, 1.3), "sEFlA": (3.8, 0),
+        "sHIlA": (5.7, 0), "sNElB": (5.0, 0), "sWBlB": (5.9, 0.2), "sTTlA": (6.9, 0), "sXGlB": (7.1, 1.0),
+        "sDClA": (7.85, 0), "sABlB": (8.75, 1.0), "sNEsA": (9.8, 0), "sOBsA": (10.6, 0.2), "sEFlB": (12.0, 0),
+        "sHIlB": (12.2, 0), "sTTlB": (12.4, 0), "sXOsA": (12.6, 0), "sDClB": (12.9, 0), "sULsA": (16.0, 0),
+        "sCNsA": (13.1, 1.1), "sNEsB": (14.6, 0), "sXOsB": (15.8, 0), "sHBsB": (15.5, 0), "sOBsB": (15.75, 0.15),
+        "sVAw": (14.0, 0), "sULsB": (18.5, 0), "sCNsB": (18.2, 0.8), "vEQlA": (1.2, 0.4), "vEQlB": (6.4, 0.4),
+        "vXGlA": (4.3, 0.2), "vXGlB": (5.8, 0.2), "vEQ2sA": (11.0, 0.4), "vEQ2sB": (17.0, 0.6), "vTBw": (17.4, 0.4),
+        "pPQw": (9.0, None), "pPD0sB": (13.0, None)}
 
-F, B, I32, U16 = "float32", "bfloat16", "int32", "uint16"
-SIZE = {F: 4, B: 2, I32: 4, U16: 2}
+F, B, H, I32, U16 = "float32", "bfloat16", "float16", "int32", "uint16"
+SIZE = {F: 4, B: 2, H: 2, I32: 4, U16: 2}
 SCRATCH = {}
 PLACE = {}
 
@@ -33,10 +45,15 @@ def _pool(name, cols, d):
     PLACE[name] = (p, at, cols, d)
 
 
-for _n, _c, _d in [("NMI", W, I32), ("F1", W, F), ("NT", WP, F), ("MT", WP, F), ("M4", WP, F), ("XT", WP, B),
+for _n, _c, _d in [("NMI", W, I32), ("F1", W, F), ("TB", 4 * WP, F), ("XB", W, B),
                    ("XG", 4096, B), ("AB", 4096, B), ("EQ", 4096, B), ("EQ2", 4096, B), ("CN", 4096, B),
                    ("WIN", 16, I32), ("THI", 16, I32), ("WF", 16, F), ("WFS", 16, F)]:
     _own(_n, _c, _d)
+TABLES = ("M1", "XT", "NT", "M0")
+for _j, _n in enumerate(TABLES):
+    PLACE[_n] = ("TB", _j * WP, WP, F)
+for _n in ("VA", "VB"):
+    SCRATCH[_n] = ("sbuf", [128, 16, 48], F)
 for _t in range(RO + 1):
     _own("Z%d" % _t, 256, B)
 for _t in range(RO):
@@ -44,24 +61,25 @@ for _t in range(RO):
     _own("XO%d" % _t, 256, B)
     _own("WS%d" % _t, 16, U16)
 for _d, _l in [
-    (F, "EP 288 NP 288 TR 544 TR2 544 EF 256 UL 256 WB0 %d WB1 %d OB %d RR 256 RW0 256 RW1 256 RUN 128 CH0 128 CH1 128 "
-        "FO1 64 WL 16 OL 16 OLM 16 OH 16 HL 16 RS 64 RS2 64 SF1 32 AL 16 AL2 16 DEw 256 DSw 256 DDw 16 DMw 16 DEo 256 "
-        "DSo 256 DDo 16 DMo 16 NE 256 C1 256 Q1 256 B1 256 NE2 256 C2 256 THF 1 THR 1 SC1 1 PF 16 ZT 144 G32 128 ID32 128 "
-        "PRM 512 PL 4 DG 272 NDG 272 HZ 256 HS 16 BI 16" % ((256 * DUP,) * 3)),
-    (B, "HI 256 LO 256 TT 256 TT2 256 RH 256 HLB 16 X1 256 X2 256 ZS 144 G2 128 GM2 128 G3K 128 GM1 128 G23 128 ID 128 "
-        "IDM 128 ID22 128 ID23 128 IM64 128 ONES 128 DGB 256 KC 256 KC2 256"),
-    (I32, "ENDI 32 ANDI 32 WI 16 WA 16 SC2 1 SC3 1 PI 1 PJ 4 CI 272 CJ 272 CK 256 PK 4"),
-    (U16, "OFF 256 OF2 256 OU 16 SW 32 SO 32 EXO 16 TRO 16"),
+    (F, "NE 544 TR0 288 TR1 288 TS0 288 TS1 288 WB 512 OB 512 EF 256 UL 256 DC 256 SC2 256 RS 16 SP 4 OH 16 RST 256 "
+        "RS0 128 DG 272 PM32 256 ID32 128 THF 1 THR 1 S1 1 PF 16 BI 16 T3 8 T4 8 T5 8 SHT 8 RTT 8"),
+    (B, "HI 256 TT 256 CB 256 SG 256 EW 512 EE 288 HB 256 SEL 2048 ONE 512 CIB 128 ID 128 IDM 128 IM64 128 I16K 128 "
+        "IM8K 128 I8K 128 IH 128 IHM 128 I1536 128 I2 128 PMT 256 P4K 128 P22 128 GS 8 CP 272 CQ 272 CIR 1024 RT 1024"),
+    (H, "VW0 48 VW1 48 KN 32"),
+    (I32, "SC 512 AN 32 WI 16 WA 16 S2 1 S3 1 PI 1 PJ 8 CI 272 CJ 272 C16 8 T1 8 T2 8"),
+    (U16, "OFF 256 OF2 256 OU 16 SO 64 TRK 8 TRB 8"),
 ]:
     for _n, _c in zip(_l.split()[0::2], _l.split()[1::2]):
         _pool(_n, int(_c), _d)
-PSUM = ("PD0", "PD1", "PD2", "PA0", "PA1", "PB0", "PB1", "PM")
+PSUM = ("PD0", "PD1", "PR", "PE", "PK0", "PK1", "PS", "PQ")
 for _n in PSUM:
     SCRATCH[_n] = ("psum", [128, 512], F)
     PLACE[_n] = (_n, 0, 512, F)
 
-SEMAPHORES = (["cv", "cs", "cp", "cg", "sent"] + ["d%d" % i for i in range(NCH + OCH + 8)]
-              + ["az%d" % t for t in range(RO)] + ["aw%d" % t for t in range(RO)])
+MOVES = ["az%d" % t for t in range(RO)] + ["aw%d_%d" % (t, h) for t in range(RO) for h in range(2)]
+SEMAPHORES = (["cv", "cs", "cp", "cg"] + ["d%d" % i for i in range(NCH + OCH + 10)] + MOVES + ["l" + m for m in MOVES])
+
+SAME = {x: x for x in ("XO", "WS", "WU", "VW", "WF")}
 
 A = AluOpType
 AF = ActivationFunctionType
@@ -74,19 +92,29 @@ def build(g, core, T, topo):
     V, S, P = g.vector, g.scalar, g.tensor
     phase, rnd = ["0"], [0]
 
+    def view(ap_, cols, rg, two, ps, lab):
+        return {"ap": ap_, "n": cols, "rg": [rg], "two": two, "ps": ps, "ind": False, "off": [], "lab": lab}
+
     def v(name, a=0, b=None, s=1):
         buf, at, cols, d = PLACE[name]
         b = cols if b is None else b
-        ap = T[buf][:, at + a:at + b] if s == 1 else T[buf][:, at + a:at + b:s]
-        return {"ap": ap, "n": len(range(a, b, s)), "rg": [(buf, at + a, at + b)], "two": SIZE[d] == 2, "ps": buf in PSUM,
-                "ind": False, "off": [], "lab": name}
+        ap_ = T[buf][:, at + a:at + b] if s == 1 else T[buf][:, at + a:at + b:s]
+        return view(ap_, len(range(a, b, s)), (buf, at + a, at + b), SIZE[d] == 2, buf in PSUM, name)
+
+    def part(name, j):
+        return view(T[name][:, :, 16 * j:16 * j + 16], 256, (name + str(j), 0, 16), False, False, name)
+
+    def col(name, b, k):
+        r = view(T[name][:, b, 0:16 * k], 16 * k, None, False, False, name)
+        r["rg"] = [(name + str(j), b, b + 1) for j in range(k)]
+        return r
 
     def ind(win, off):
         return {"ap": win["ap"].indirect(off["ap"]), "n": 16 * off["n"], "rg": win["rg"], "off": off["rg"], "two": False,
                 "ps": False, "ind": True, "lab": win["lab"]}
 
-    def ext(ap, key, a=0, b=1):
-        return {"ap": ap, "n": b - a, "rg": [(key, a, b)], "off": [], "ind": False, "lab": key}
+    def ext(ap_, key, a=0, b=1):
+        return {"ap": ap_, "n": b - a, "rg": [(key, a, b)], "off": [], "ind": False, "lab": key}
 
     def add(q, fn, out, ins, dur, kind="c", sem=None, cnt=0):
         r, w = [], []
@@ -96,8 +124,9 @@ def build(g, core, T, topo):
         if out is not None:
             w += out["rg"]
             r += out["off"]
+        lab = out["lab"] if out else "send"
         ops.append({"q": q, "fn": fn, "r": r, "w": w, "kind": kind, "sem": sem, "cnt": cnt, "dur": dur,
-                    "lab": (q or "x") + (out["lab"] if out else "send") + phase[0], "rnd": rnd[0]})
+                    "lab": (q or "x") + SAME.get(lab[:2], lab) + phase[0], "rnd": rnd[0]})
 
     def cost(q, out, a, base):
         fx = C["v"] if q == "v" else C["a"]
@@ -122,15 +151,15 @@ def build(g, core, T, topo):
         add("v", lambda: V.tensor_copy(ap(out), ap(a)), out, [a], cost("v", out, a, 0.5 if out["two"] and a["two"] else 1))
 
     def ms(out, c):
-        add("v", lambda: V.memset(ap(out), c), out, [], cost("v", out, out, 1))
+        add("v", lambda: V.memset(ap(out), c), out, [], cost("v", out, out, 0.5 if out["two"] else 1))
 
-    def scan(out, a, b):
-        add("v", lambda: V.tensor_tensor_scan(ap(out), ap(a), ap(b), 0.0, A.mult, A.add), out, [a, b], cost("v", out, a, 1))
+    def scan(out, a, b, o0, o1):
+        add("v", lambda: V.tensor_tensor_scan(ap(out), ap(a), ap(b), 0.0, o0, o1), out, [a, b], cost("v", out, a, 1))
 
     def tr(out, a):
         add("v", lambda: V.transpose(ap(out), ap(a)), out, [a], cost("v", out, a, 1))
 
-    def act(out, a, f, scale=None, bias=None):
+    def act(out, a, f=AF.Identity, scale=None, bias=None):
         d = cost("s", out, a, 1)
         if bias is not None:
             add("s", lambda: S.activation(ap(out), ap(a), f, bias=ap(bias), scale=scale), out, [a, bias], d)
@@ -139,9 +168,13 @@ def build(g, core, T, topo):
         else:
             add("s", lambda: S.activation(ap(out), ap(a), f), out, [a], d)
 
-    def mm(out, lt, rhs, st, sp):
+    def mm(out, lt, rhs, st=True, sp=True):
         add("p", lambda: P.matmul(ap(out), ap(lt), ap(rhs), st, sp), out, [lt, rhs],
             C["pf"] + max(64, rhs["n"]) * C["pe"] * (1 if rhs["two"] else 4))
+
+    def group(*terms):
+        for j, (o, lt, rhs) in enumerate(terms):
+            mm(o, lt, rhs, j == 0, j == len(terms) - 1)
 
     def merge(k):
         l = ops[-k:]
@@ -152,15 +185,23 @@ def build(g, core, T, topo):
                   "w": [x for y in l for x in y["w"]], "dur": sum(y["dur"] for y in l)})
         ops.append(o)
 
+    def iota(out, pat):
+        cm = 1 if out["n"] == 1 else 0
+        if out["two"]:
+            add("g", lambda: g.iota(ap(out), pat, 0, cm, allow_small_or_imprecise_dtypes=True), out, [], 130 + 1.7 * out["n"])
+        else:
+            add("g", lambda: g.iota(ap(out), pat, 0, cm), out, [], 130 + 1.7 * out["n"])
+
+    def select(out, a, pat, op, fill):
+        add("g", lambda: g.affine_select(ap(out), ap(a), pat, op, fill, 0, 1), out, [a], 170 + 1.7 * out["n"])
+
     nd = [0]
 
-    def dma(q, out, src, nbytes):
+    def dma(q, out, src, nbytes, after=None):
         s = "d%d" % nd[0]
         nd[0] += 1
-        e = {"y": g.sync, "s": g.scalar}[q]
-        add(q, lambda: e.dma_start(ap(out), ap(src)), out, [src], nbytes / C["bw"], "dma", s, 16)
-
-    sent = [0]
+        e = {"y": g.sync, "s": g.scalar, "g": g}[q]
+        add(q, lambda: e.dma_start(ap(out), ap(src)), out, [src, after], nbytes / C["bw"], "dma", s, 16)
 
     def move(t, out, src, sem):
         dst = T.cores[(rank + 1 + t % (n - 1)) % n]
@@ -168,10 +209,12 @@ def build(g, core, T, topo):
         eng = topo.engines(core, dst)[:8]
         m = sum(1 << e for e in eng)
         rid, pid, _ = topo.addr(dst)
-        sent[0] += len(eng)
-        add("g", lambda: g.remote_dma(ap(out), ap(src), T.sem[sem], T.sem.sent, pid, rid, m), None, [src],
+        add("g", lambda: g.remote_dma(ap(out), ap(src), T.sem[sem], T.sem["l" + sem], pid, rid, m), None, [src],
             C["rem"] + src["n"] * 5, "rem")
+        k = len(ops) - 1
         add(None, None, out, [], 0, "ext", sem, len(topo.engines(frm, core)[:8]))
+        add(None, None, ext(None, "l" + sem), [], 0, "ext", "l" + sem, len(eng))
+        ops[-1]["from"] = ops[-2]["from"] = k
 
     cw = W // NCH
     dma("s", v("WIN"), ext(T.w[:], "w"), 8192)
@@ -179,236 +222,272 @@ def build(g, core, T, topo):
         dma("y", v("NMI", c * cw, (c + 1) * cw), ext(T.nm[:, c * cw:(c + 1) * cw], "nm"), 512 * cw)
     dma("s", v("Z0"), ext(T.z[:], "z"), 65536)
     dma("s", v("THI", 0, 1), ext(T.th[:], "th"), 4096)
-    add("g", lambda: g.iota(ap(v("PI")), [[1, 1]], 0, 1), v("PI"), [], 140)
-    add("g", lambda: g.iota(ap(v("CI")), [[1, 272]], 0, 0), v("CI"), [], 600)
-    dma("y", v("XT", 0, W), ext(T.x[:], "x"), 256 * W)
+    iota(v("PI"), [[1, 1]])
+    iota(v("CI"), [[1, 272]])
+    iota(v("CIB"), [[1, 128]])
+    iota(v("C16"), [[16, 8]])
+    dma("y", v("XB"), ext(T.x[:], "x"), 256 * W)
     bias = {}
-    for j, x in enumerate([2.0 ** 23 - 0.5, float(MOFF), 1.0, -32.0 * (MOFF + NONE - 1), -4096.0 * MOFF, -float(MOFF),
-                           128.0, 8224.0, 61440.0, 2.0 ** 21]):
-        ms(v("BI", j, j + 1), x)
+    for j, x in enumerate([-CM / 4096, NONE, HALF, 1, -0.5, 8224, 1 - NONE, 4096, HALF - BIG, -2, -HALF]):
+        ms(v("BI", j, j + 1), float(x))
         bias[x] = v("BI", j, j + 1)
+    ms(v("SEL"), 1.0)
+    ms(v("ONE"), 1.0)
+    select(v("SEL"), v("SEL"), [[-1, 16], [-16, 8], [0, 16]], A.is_equal, 0.0)
+    select(v("PM32"), v("ONE", 0, 256), [[0, 2], [-1, 8], [-8, 16]], A.is_equal, 0.0)
     pi = v("PI")
-    ts(v("PJ", 0, 1), pi, 112, None, A.bitwise_and)
-    ts(v("PJ", 1, 2), pi, 15, None, A.bitwise_and)
-    ts(v("PJ", 2, 3), pi, 1, None, A.bitwise_and)
-    ts(v("PJ", 3, 4), pi, 4, 1, A.logical_shift_right, A.bitwise_and)
-    cp(v("PF", 0, 4), v("PJ"))
-    cp(v("PF", 4, 5), pi)
+    pj = lambda j: v("PJ", j, j + 1)
     pf = lambda j: v("PF", j, j + 1)
-    g16, acol, pcol = pf(0), pf(1), pf(4)
+    ts(pj(0), pi, 112, None, A.bitwise_and)
+    ts(pj(1), pi, 15, None, A.bitwise_and)
+    ts(pj(2), pi, 4, 1, A.logical_shift_right, A.bitwise_and)
+    ts(pj(3), pi, 3, None, A.logical_shift_right)
+    ts(pj(4), pi, 7, None, A.bitwise_and)
+    ts(pj(5), pi, 3, 1, A.logical_shift_right, A.bitwise_and)
+    ts(pj(6), pi, 1, None, A.bitwise_and)
+    cp(v("PF", 0, 7), v("PJ", 0, 7))
+    cp(pf(7), pi)
+    g16, acol, pcol, kcol, jcol = pf(0), pf(1), pf(7), pf(8), pf(9)
+    ts(kcol, pf(3), 128.0, None, A.mult)
+    ts(jcol, pf(3), -1.0, 15.0, A.mult, A.add)
+    ts(pf(10), acol, float(W), None, A.add)
+    ts(v("SP"), v("CI", 0, 4), float(WP), pf(10), A.mult, A.add)
+    tt(pf(12), pf(2), pf(6), A.not_equal)
+    ts(pf(13), pf(4), 16.0, pf(5), A.mult, A.add)
+    ts(pf(14), pf(12), 144.0, pf(13), A.mult, A.add)
+    ts(v("TRK"), v("CI", 0, 8), 2.0, pf(14), A.mult, A.add)
+    ts(v("T1"), v("CI", 0, 8), pf(2), None, A.add)
+    ts(v("T1"), v("T1"), 1, None, A.bitwise_and)
+    ts(v("T3"), v("T1"), 144.0, acol, A.mult, A.add)
+    tt(v("T4"), v("T3"), v("C16"), A.add)
+    cp(v("TRB"), v("T4"))
+    ts(v("GS"), v("C16"), g16, None, A.is_equal)
+    ts(v("ID"), v("CIB"), pcol, None, A.is_equal)
+    for nm_, x in [("IDM", -1.0), ("ID32", 1.0), ("IM64", -64.0), ("I16K", 2 * BIG), ("IM8K", -BIG), ("I8K", BIG), ("IH", 2 / BIG),
+                   ("IHM", -2 / BIG), ("I1536", float(HALF)), ("I2", 2.0)]:
+        act(v(nm_), v("ID"), scale=x)
+    act(v("PMT"), v("PM32"), scale=2.0 ** 23)
+    act(v("P4K"), v("PM32", 0, 128), scale=4096.0)
+    act(v("P22"), v("PM32", 0, 128), scale=2.0 ** 22)
     ts(v("CJ"), v("CI"), 15, None, A.bitwise_and)
+    ts(v("RST"), v("CJ", 0, 256), 0.0, 2.0 ** 25, A.is_equal, A.mult)
+    ts(v("RS0"), v("CJ", 0, 128), 0.0, None, A.not_equal)
     ts(v("DG"), v("CJ"), acol, None, A.is_equal)
-    cp(v("EXO"), v("CI", 0, 16))
-    tt(pf(5), pf(2), pf(3), A.not_equal)
-    ts(pf(6), acol, 16.0, None, A.mult)
-    ts(pf(7), pf(5), 272.0, pf(6), A.mult, A.add)
-    ts(v("TRO"), v("CI", 0, 16), pf(7), None, A.add)
-    act(v("NDG"), v("DG"), AF.Identity, -1.0, bias[1.0])
-    act(v("DGB"), v("DG", 0, 256), AF.Identity)
-    ts(pf(8), acol, float(W), None, A.add)
-    ts(v("HZ"), v("CJ", 0, 256), 0.0, 2.0, A.not_equal, A.mult)
-    scan(v("HS"), v("HZ", 0, 16), v("DG", 0, 16))
-    ts(pf(9), v("HS", 15, 16), 2.0, None, A.mult)
-    ts(v("ZT"), v("CI", 0, 144), g16, 15.0, A.subtract, A.is_equal)
-    act(v("ZS"), v("ZT"), AF.Identity, 2048.0)
-    ts(v("ID32"), v("CI", 0, 128), pcol, None, A.is_equal)
-    for nm_, x in [("ID", 1.0), ("IDM", -1.0), ("ID22", 2.0 ** 22), ("ID23", 2.0 ** 23), ("IM64", -64.0)]:
-        act(v(nm_), v("ID32"), AF.Identity, x)
-    ts(v("CK"), v("CI", 0, 256), 240, None, A.bitwise_and)
-    ts(v("KC"), v("CK"), 8.0, None, A.mult)
-    act(v("KC2"), v("KC"), AF.Identity, -32.0, bias[61440.0])
-    ts(v("G32"), v("CK", 0, 128), g16, None, A.is_equal)
-    for nm_, x in [("G2", 2.0), ("GM2", -2.0), ("G3K", 3072.0), ("GM1", -1.0), ("G23", 2.0 ** 23)]:
-        act(v(nm_), v("G32"), AF.Identity, x)
-    ms(v("ONES"), 1.0)
-    ts(v("PK"), v("CI", 0, 4), pcol, None, A.add)
-    ts(v("PK"), v("PK"), 15, None, A.bitwise_and)
-    ts(v("PL"), v("PK"), g16, None, A.add)
-    for t in range(RO):
-        ts(v("PRM", 128 * t, 128 * t + 128), v("CI", 0, 128), v("PL", t, t + 1), None, A.is_equal)
-    for nm_ in ("EP", "NP"):
-        ms(v(nm_, 0, 16), 0.0)
-        ms(v(nm_, 272, 288), 0.0)
-    ms(v("RS"), 0.0)
-    for nm_ in ("NT", "MT", "XT"):
+    act(v("CP"), v("DG"), scale=-BIG, bias=bias[4096])
+    act(v("CQ"), v("DG"), scale=BIG, bias=bias[HALF - BIG])
+    sv = v("CI", 1, 9)
+    ts(v("T2"), sv, acol, None, A.add)
+    ts(v("T2"), v("T2"), 15, None, A.bitwise_and)
+    ts(v("SHT"), v("T2"), g16, None, A.add)
+    ts(v("T3"), sv, acol, None, A.is_gt)
+    ts(v("T5"), sv, -1.0, 16.0, A.mult, A.add)
+    tt(v("T4"), v("T3"), v("T5"), A.mult)
+    ts(v("RTT"), v("T4"), pcol, None, A.add)
+    for s in range(8):
+        ts(v("CIR", 128 * s, 128 * s + 128), v("CIB"), v("SHT", s, s + 1), -1.0, A.is_equal, A.mult)
+        ts(v("RT", 128 * s, 128 * s + 128), v("CIB"), v("RTT", s, s + 1), BIG, A.is_equal, A.mult)
+    select(v("CIR"), v("CIR"), [[0, 8], [-1, 128]], A.not_equal, 1.0)
+    ts(v("KN", 0, 16), v("CI", 0, 16), 0.0, -4096.0, A.mult, A.add)
+    ts(v("KN", 16, 32), v("CI", 0, 16), 0.0, float(HALF - NONE), A.mult, A.add)
+    ms(v("NE"), 0.0)
+    for nm_ in TABLES[:3]:
         ms(v(nm_, W, WP), 0.0)
+    ms(v("M0", W, WP), 0.0)
     for c in range(NCH):
         a, b = c * cw, (c + 1) * cw
-        ts(v("F1", a, b), v("NMI", a, b), 4097.0, None, A.add)
-        act(v("MT", a, b), v("F1", a, b), AF.Identity, 2.0 ** -12, bias[2.0 ** 23 - 0.5])
-        ts(v("NMI", a, b), v("NMI", a, b), 4095, None, A.bitwise_and)
-        cp(v("NT", a, b), v("NMI", a, b))
+        pd = v("PD%d" % (c % 2), 0, cw)
+        ts(v("F1", a, b), v("NMI", a, b), -float(HALF), CM, A.add, A.add)
+        act(v("M0", a, b), v("F1", a, b), scale=2.0 ** -12, bias=bias[-CM / 4096])
+        act(pd, v("M0", a, b), scale=4096.0, bias=bias[NONE])
+        tt(v("NT", a, b), pd, v("NMI", a, b), A.subtract)
+        act(v("M1", a, b), v("F1", a, b), scale=2.0 ** -12, bias=bias[-CM / 4096])
+    for nm_ in ("M0", "M1"):
+        ms(v(nm_, NONE, W), -1.0)
     cp(v("WU0"), v("WIN"))
     cp(v("THF"), v("THI", 0, 1))
     ts(v("THR"), v("THF"), 2048.0, None, A.mult)
+    dma("g", v("XT", 0, W), v("XB"), 512 * W)
 
-    Nw, Mw, Xw = v("NT", 0, W), v("MT", 0, W), v("XT", 0, W)
-    kb = 16 // NBK
-    m = 16 * kb
+    Nw = v("NT", 0, W)
+    NP, EP = 16, 272
 
-    def turn(src, dst):
-        tr(v(dst, 0, 256), v(src, 16, 272))
-        tr(v(dst, 256, 544), v(src))
+    def turn(at, dst):
+        tr(v(dst, 0, 128), v("NE", at, at + 128))
+        tr(v(dst, 128, 288), v("NE", at - 16, at + 144))
 
-    def spread(src, tmp, dst, bi):
-        tt(v(tmp), ind(v(src), v("EXO")), v("DG", 0, 256), A.mult)
-        mm(v("PM", 0, 256), v("G32"), v(tmp), True, True)
-        for d in range(DUP):
-            act(v(dst, 256 * d, 256 * d + 256), v("PM", 0, 256), AF.Identity, None if bi is None else 1.0, bi)
-
-    def first_of(vl, vb, pl, s, out):
-        tt(v("DE" + s), ind(v(vl), v("EXO")), v(vb, 0, 256), A.is_equal)
-        scan(v("DS" + s), v("HZ"), v("DE" + s))
-        ts(v("DD" + s), v("DS" + s, 15, 256, 16), pf(9), pf(8), A.is_ge, A.mult)
-        tt(v("DM" + s), v("DD" + s), v(pl), A.max)
-        cp(v(out, 0, 32, 2), v("DM" + s))
-
-    def reduce16(out, src, c, st, sp):
+    def spread(ps, at, src, st=True, sp=True):
         for a in range(16):
-            mm(out, v("ZS", 15 - a, 143 - a), v(src, c * kb * 256 + a, (c + 1) * kb * 256, 16), st and a == 0, sp and a == 15)
+            mm(v(ps, at + a, at + 16 * src["n"], 16), v("SEL", 128 * a, 128 * a + 128), src, st, sp if not st and a == 15 else st)
         merge(16)
 
-    def lx(name, c):
-        return v(name, 16 * kb * c, 16 * kb * (c + 1))
+    def reduce16(ps, at, src, h):
+        for a in range(16):
+            mm(v(ps, at + a, at + 128, 16), v(src, 2048 * h + a, 2048 * h + 2048, 16), v("GS"))
+        merge(16)
 
-    for t in range(RO):
-        last = t == RO - 1
-        rnd[0] = t
-        wu, z, wb, rw, xo = v("WU%d" % t), v("Z%d" % t), "WB%d" % (t % 2), "RW%d" % (t % 2), v("XO%d" % t)
-        if last:
-            dma("y", v("M4"), v("MT"), 512 * WP)
-        phase[0] = "l"
-        act(v("EP", 16, 272), ind(Mw, wu), AF.Identity)
-        cp(v("WL"), wu)
-        spread("WL", rw, wb, None)
-        turn("EP", "TR")
-        ts(v("OFF"), ind(v("TR"), v("TRO")), float(MOFF), None, A.subtract)
-        first_of("WL", wb, "WL", "w", "SW")
-        for k in range(0, 16, DUP):
-            tt(v("EQ", 256 * k, 256 * (k + DUP)), ind(Nw, v("OFF", 16 * k, 16 * (k + DUP))), v(wb), A.is_equal)
-        for i in range(8):
-            xg, ab, pd = v("XG", 512 * i, 512 * i + 512), v("AB", 512 * i, 512 * i + 512), "PD%d" % (i % 3)
-            if i >= 8 - NV:
-                for k in (2 * i, 2 * i + 1):
-                    tt(v("XG", 256 * k, 256 * k + 256), ind(Xw, v("OFF", 16 * k, 16 * k + 16)), z, A.subtract)
+    def hv(name, h, k=128):
+        return v(name, k * h, k * h + k)
+
+    def listen(t, h):
+        z, vw, pk = hv("Z%d" % t, h), "VW%d" % (t % 2), "PK%d" % h
+        wu, trn = hv("WU%d" % t, h, 8), "TR%d" % h
+        Xw, Mw = v("XB") if t == 0 else v("XT", 0, W), v("M%d" % (t % 2), 0, W)
+        act(v("NE", EP + 128 * h, EP + 128 * h + 128), ind(Mw, wu))
+        ts(hv(vw, h, 8), wu, -1.0, float(NONE - HALF), A.mult, A.add)
+        spread("PS", 128 * h, hv(vw, h, 8))
+        for d in range(2):
+            act(hv("WB", 2 * h + d), hv("PS", h), scale=1.0, bias=bias[HALF])
+        turn(EP + 128 * h, trn)
+        cp(hv("OFF", h), ind(v(trn), v("TRK")))
+        for j in range(8 * h, 8 * h + 8):
+            tt(hv("EQ", j, 256), ind(Nw, hv("OFF", j, 16)), hv("WB", h, 256), A.is_equal)
+        ns = 4 - NV[h]
+        for i in range(4 * h, 4 * h + 4):
+            xg, ab, pd = hv("XG", i, 512), hv("AB", i, 512), "PD%d" % (i % 2)
+            if i - 4 * h >= ns:
+                for k in range(4 * i, 4 * i + 4):
+                    tt(hv("XG", k), ind(Xw, hv("OFF", k, 8)), z, A.subtract)
                 act(ab, xg, AF.Abs)
                 continue
-            act(xg, ind(Xw, v("OFF", 32 * i, 32 * i + 32)), AF.Identity)
-            for h in range(2):
-                o = v(pd, 256 * h, 256 * h + 256)
-                mm(o, v("ID"), v("XG", 512 * i + 256 * h, 512 * i + 256 * h + 256), True, False)
-                mm(o, v("IDM"), z, False, True)
-            merge(4)
+            if (i - 4 * h) % GW == 0:
+                e = min(i + GW, 4 * h + ns)
+                act(v("XG", 512 * i, 512 * e), ind(Xw, v("OFF", 32 * i, 32 * e)))
+            group((v(pd), v("ID"), xg), *[(hv(pd, k), v("IDM"), z) for k in range(4)])
+            merge(5)
             act(ab, v(pd), AF.Abs)
-        act(v("EF"), ind(v("TR"), v("TRO")), AF.Identity, 1.0, bias[-float(MOFF)])
-        act(v("HI"), v("EF"), AF.Identity, 2.0 ** -6, bias[128.0])
-        mm(v("PM", 256, 512), v("ID32"), v("EF"), True, False)
-        mm(v("PM", 256, 512), v("IM64"), v("HI"), False, True)
-        act(v("LO"), v("PM", 256, 512), AF.Identity, 1.0, bias[8224.0])
-        for c in range(NBK):
-            pa, pb = v("PA%d" % (c % 2), 0, m), v("PB%d" % (c % 2), 0, m)
-            mm(pa, v("ID"), lx("KC", c), True, False)
-            reduce16(pa, "AB", c, False, False)
-            reduce16(pb, "EQ", c, True, True)
-            act(lx("TT", c), pb, AF.Relu, -1.0, bias[1.0])
-            mm(pa, v("ID23"), lx("TT", c), False, True)
-            dst = "RUN" if c == 0 else "CH%d" % (c % 2)
-            tt(v(dst, 0, 2 * m, 2), pa, lx("HI", c), A.add)
-            tt(v(dst, 1, 2 * m, 2), pa, lx("LO", c), A.add)
-            if c > 0:
-                tt(v("RUN"), v("RUN"), v(dst), A.min)
-        tt(v("FO1"), v("RUN", 0, 64), v("RUN", 64, 128), A.min)
-        tt(v("ENDI"), v("FO1", 0, 32), v("FO1", 32, 64), A.min)
-        ts(v("ANDI"), v("ENDI"), 127, None, A.bitwise_and)
-        ts(v("OH"), v("ANDI", 0, 32, 2), 64.0, -32.0, A.mult, A.add)
-        tt(v("OL"), v("OH"), v("ANDI", 1, 32, 2), A.add)
-        cp(v("OU"), v("OL"))
-        phase[0] = "s"
-        act(v("NP", 16, 272), ind(Nw, v("OU")), AF.Identity)
-        spread("OL", "RR", "OB", bias[float(MOFF)])
-        act(xo, ind(Xw, v("OU")), AF.Identity)
-        move(t, v("Z%d" % (t + 1)), xo, "az%d" % t)
-        turn("NP", "TR2")
-        cp(v("OF2"), ind(v("TR2"), v("TRO")))
-        act(v("UL"), ind(v("TR2"), v("TRO")), AF.Identity)
-        ts(v("AL"), v("OL"), float(NONE), 2.0 ** 23, A.is_equal, A.mult)
-        act(v("AL2"), v("WL"), AF.Identity, 1.0, bias[2.0 ** 21])
-        tt(v("RS", 0, 16), v("AL"), v("AL2"), A.add)
-        for c in range(NBK):
-            for k in range(c * kb, (c + 1) * kb, DUP):
-                tt(v("EQ2", 256 * k, 256 * (k + DUP)), ind(Mw, v("OF2", 16 * k, 16 * (k + DUP))), v("OB"), A.is_equal)
-            for k in range(c * kb, (c + 1) * kb, 2):
-                act(v("CN", 256 * k, 256 * (k + 2)), ind(Mw, v("OF2", 16 * k, 16 * (k + 2))), AF.Relu, 32.0,
-                    bias[-32.0 * (MOFF + NONE - 1)])
-            pa, pb = v("PA%d" % (c % 2), 0, m), v("PB%d" % (c % 2), 0, m)
-            mm(pa, v("ID32"), lx("UL", c), True, False)
-            mm(pa, v("ID"), lx("KC2", c), False, False)
-            reduce16(pa, "CN", c, False, False)
-            reduce16(pb, "EQ2", c, True, True)
-            act(lx("TT2", c), pb, AF.Sign)
-            mm(pa, v("ID22"), lx("TT2", c), False, True)
-            tt(v("RS2"), pa, v("RS" if c == 0 else "RS2"), A.max)
-        tt(v("SF1"), v("RS2", 0, 32), v("RS2", 32, 64), A.max)
-        tt(v("WI"), v("SF1", 0, 16), v("SF1", 16, 32), A.max)
-        ts(v("WA"), v("WI"), 4095, None, A.bitwise_and)
-        if last:
-            cp(v("WFS"), v("WA"))
-            move(t, v("WF"), v("WFS"), "aw%d" % t)
+        act(hv("EF", h), ind(v(trn), v("TRB")), scale=1.0, bias=bias[8224])
+        act(hv("HI", h), hv("EF", h), scale=2.0 ** -6, bias=bias[-0.5])
+        reduce16("PE", 128 * h, "EQ", h)
+        act(hv("TT", h), hv("PE", h), AF.Relu, -1.0, bias[1])
+        reduce16("PR", 128 * h, "AB", h)
+        act(hv("DC", h), hv("PR", h), scale=2048.0, bias=kcol)
+        group((v(pk, 0, 256), hv("TT", h), v("PMT")), (v(pk, 0, 128), v("ID"), hv("HI", h)),
+              (v(pk, 128, 256), v("ID32"), hv("EF", h)), (v(pk, 128, 256), v("IM64"), hv("HI", h)),
+              (v(pk, 0, 256), hv("DC", h), v("PM32")))
+        scan(hv("SC", h, 256), v("RST"), v(pk, 0, 256), A.add, A.min)
+        ts(hv("AN", h, 16), v("SC", 256 * h + 15, 256 * h + 256, 16), 127, None, A.bitwise_and)
+        ts(hv("OH", h, 8), hv("AN", 2 * h, 8), 64.0, -32.0 - HALF, A.mult, A.add)
+        tt(hv(vw, 2 + h, 8), hv("OH", h, 8), hv("AN", 2 * h + 1, 8), A.add)
+        ts(hv("OU", h, 8), hv(vw, 2 + h, 8), float(HALF), None, A.add)
+        ts(hv(vw, 4 + h, 8), v("SC", 256 * h + 143, 256 * h + 256, 16), v("THR"), BIG, A.is_lt, A.mult)
+
+    def speak(t, h):
+        vw, pk, trn, ou = "VW%d" % (t % 2), "PK%d" % h, "TS%d" % h, hv("OU", h, 8)
+        Xw, Mw = v("XB") if t == 0 else v("XT", 0, W), v("M%d" % (t % 2), 0, W)
+        act(v("NE", NP + 128 * h, NP + 128 * h + 128), ind(Nw, ou))
+        if h == 0:
+            spread("PS", 256, v(vw, 16, 24))
+            for d in range(2):
+                act(hv("OB", d), hv("PS", 2), scale=1.0, bias=bias[HALF])
         else:
-            cp(v("WS%d" % t), v("WA"))
-            move(t, v("WU%d" % (t + 1)), v("WS%d" % t), "aw%d" % t)
-        phase[0] = "z" if last else "w"
-        ts(v("HL"), v("ENDI", 1, 32, 2), v("THR"), None, A.is_lt)
-        tt(v("RH"), ind(v("HL"), v("EXO")), v("DG", 0, 256), A.mult)
-        mm(v("PD0", 0, 256), v("G23"), v("RH"), True, False)
-        mm(v("PD0", 0, 256), v("G3K"), v("RH"), False, True)
-        mm(v("PD2", 0, 256), v("G3K"), v("RH"), True, False)
-        mm(v("PD2", 0, 256), v("GM1"), v("RH"), False, True)
-        ts(v("OLM"), v("OL"), float(MOFF), None, A.add)
-        first_of("OLM", "OB", "OL", "o", "SO")
-        tt(v("NE2"), ind(Mw, wu), v("OB", 0, 256), A.not_equal)
-        tt(v("C2"), v("NE2"), v("PD0", 0, 256), A.mult)
-        mm(v("PD0", 256, 512), v("G32"), v(rw), True, True)
-        mm(v("PD2", 256, 512), v("PRM", 128 * t, 128 * t + 128), v(rw), True, True)
-        tt(v("NE"), v("NP", 16, 272), v("PD0", 256, 512), A.not_equal)
-        tt(v("B1"), ind(Nw, v("OU")), v("NDG", t, t + 256), A.mult)
-        tt(v("C1"), v("NE"), v("PD2", 0, 256), A.mult)
-        tt(v("Q1"), v("C1"), v("PD2", 256, 512), A.max)
+            mm(v("PD0"), v("I1536"), v("ONE"), True, False)
+            spread("PD0", 0, v(vw, 16, 48), False, True)
+            act(v("HB"), v("PD0", 256, 512), scale=1.0, bias=bias[-HALF])
+            for d in range(2):
+                act(hv("OB", 2 + d), hv("PD0", 1))
+        act(hv("XO%d" % t, h), ind(Xw, ou))
+        if h == 1:
+            move(t, v("Z%d" % (t + 1)), v("XO%d" % t), "az%d" % t)
+        turn(NP + 128 * h, trn)
+        ts(hv("OF2", h), ind(v(trn), v("TRK")), -1.0, float(NONE), A.mult, A.add)
+        act(hv("UL", h), ind(v(trn), v("TRB")), scale=-1.0, bias=bias[NONE])
+        ts(hv("RS", h, 8), hv("WU%d" % t, h, 8), 2.0 ** 21, None, A.add)
+        for j in range(8 * h, 8 * h + 8):
+            tt(hv("EQ2", j, 256), ind(Mw, hv("OF2", j, 16)), hv("OB", h, 256), A.is_equal)
+        for i in range(4 * h, 4 * h + 4, GW):
+            act(v("CN", 512 * i, 512 * (i + GW)), ind(Mw, v("OF2", 32 * i, 32 * (i + GW))), AF.Relu, 1.0, bias[1 - NONE])
+
+    def choose(t, h):
+        reduce16("PR", 256 + 128 * h, "CN", h)
+        act(hv("CB", h), hv("PR", 2 + h), scale=16.0, bias=jcol)
+        reduce16("PE", 256 + 128 * h, "EQ2", h)
+        act(hv("SG", h), hv("PE", 2 + h), AF.Sign)
+        o = v("PK%d" % h, 384, 512)
+        group((o, v("ID32"), hv("UL", h)), (o, hv("CB", h), v("P4K")), (o, hv("SG", h), v("P22")))
+        scan(hv("SC2", h), v("RS0"), o, A.mult, A.max)
+        tt(hv("WI", h, 8), v("SC2", 128 * h + 15, 128 * h + 128, 16), hv("RS", h, 8), A.max)
+        ts(hv("WA", h, 8), hv("WI", h, 8), 4095, None, A.bitwise_and)
+        src, dst = ("WFS", "WF") if t == RO - 1 else ("WS%d" % t, "WU%d" % (t + 1))
+        cp(hv(src, h, 8), hv("WA", h, 8))
+        move(t, hv(dst, h, 8), hv(src, h, 8), "aw%d_%d" % (t, h))
+
+    def prepare(t):
+        last = t == RO - 1
+        vw, z, xo = "VW%d" % (t % 2), v("Z%d" % t), v("XO%d" % t)
+        tabs = ["NT", "M%d" % (1 - t % 2)] + ([] if last else ["XT"])
+        low = min(TABLES.index(x) for x in tabs)
+        one = v("ONE", 0, 256)
+        wo = v(vw, 0, 32)
+        for s in range(8):
+            mm(hv("PK0", s, 32), hv("CIR", s), wo)
+        group((hv("PK0", 8, 32), v("ID"), wo), (hv("PK0", 8, 32), v("ID"), v("KN")))
+        merge(10)
+        ts(v("EE"), v("PK0", 0, 288), 0.0, None, A.is_equal)
+        acc, aw, ao = hv("PK0", 9, 32), hv("PK0", 18, 16), hv("PK0", 19, 16)
+        group(*[(acc, hv("RT", s), hv("EE", s, 32)) for s in range(8)], (acc, v("I8K"), hv("EE", 8, 32)),
+              (aw, v("IDM"), v(vw, 0, 16)), (ao, v("ID"), v(vw, 16, 32)))
+        merge(11)
+        for j, x in enumerate(tabs):
+            at = TABLES.index(x) - low
+            ts(v("SO", j, 64, 4), aw if j == 1 else ao, float((NONE - HALF if j == 1 else HALF) + at * WP),
+               v("SP", at, at + 1), A.add, A.min)
         if not last:
-            for h, (ga, gb) in enumerate((("G2", "GM2"), ("GM2", "G2"))):
-                o = v("PD1", 256 * h, 256 * h + 256)
-                mm(o, v("ID"), xo, True, False)
-                mm(o, v(ga), v("RH"), False, False)
-                mm(o, v(gb), v("DGB"), False, True)
-            tt(v("X1"), z, v("PD1", 0, 256), A.max)
-            tt(v("X2"), v("X1"), v("PD1", 256, 512), A.min)
-            act(v("HLB"), v("HL"), AF.Identity)
-            mm(v("PM", 16, 32), v("ONES"), v("HLB"), True, True)
-            o, a = v("SC1"), v("PM", 16, 32)
+            o, a = v("S1"), v("PK1", 256, 272)
+            mm(a, v("ONE", 0, 128), v(vw, 32, 48))
             add("v", lambda o=o, a=a: V.tensor_reduce(ap(o), ap(a), AxisListType.X, A.add), o, [a], 70)
-            cp(v("SC2"), v("SC1"))
-            ts(v("SC3"), v("SC2"), 31, None, A.bitwise_and)
-            ts(v("THR"), v("SC3"), v("THF"), 2048.0, A.add, A.mult)
-        for b in range(15, -1, -1):
-            so, sw = v("SO", 2 * b, 2 * b + 1), v("SW", 2 * b, 2 * b + 1)
-            l0, l1 = 16 * b, 16 * b + 16
-            tt(ind(v("M4" if last else "MT"), sw), v("EP", 16 + l0, 16 + l1), v("C2", l0, l1), A.max)
-            if not last:
-                cp(ind(v("XT"), so), v("X2", l0, l1))
-            tt(ind(v("NT"), so), v("B1", l0, l1), v("Q1", l0, l1), A.max)
-        ms(v("NT", NONE, W), float(NONE))
+            ts(v("S2"), v("S1"), 1 / BIG, None, A.mult)
+            ts(v("S3"), v("S2"), 31, None, A.bitwise_and)
+            ts(v("THR"), v("S3"), v("THF"), 2048.0, A.add, A.mult)
+        q, qw = v("PQ", 0, 256), v("PQ", 256, 512)
+        mm(qw, v("I1536"), one, True, False)
+        spread("PQ", 256, v(vw, 0, 16), False, True)
+        mm(q, v("ID"), v("CQ", t, t + 256), True, False)
+        spread("PQ", 0, v(vw, 0, 16), False, False)
+        tt(v("EW", 0, 256), v("NE", NP, NP + 256), qw, A.is_equal)
+        mm(q, v("IDM"), v("HB"), False, True)
+        p, hi, c = v("PD1", 0, 256), v("PD1", 256, 512), v("PD0", 0, 256)
         if not last:
-            ms(v("XT", NONE, W), 255.0)
+            group((qw, v("ID"), xo), (qw, v("IH"), v("HB")))
+            group((hi, v("ID"), xo), (hi, v("I2"), one), (hi, v("IHM"), v("HB")))
+        act(part("VB", 0), q, AF.Relu)
+        group((p, v("ID"), v("CP", t, t + 256)), (p, v("IDM"), v("HB")), (p, v("I16K"), v("EW", 0, 256)))
+        tt(part("VA", 0), v("NE", NP, NP + 256), p, A.min)
+        tt(v("EW", 256, 512), v("NE", EP, EP + 256), c, A.is_equal)
+        group((c, v("ID"), v("HB")), (c, v("IM8K"), v("EW", 256, 512)))
+        act(part("VB", 1), c, scale=NONE / BIG)
+        act(part("VA", 1), v("NE", EP, EP + 256))
+        if not last:
+            act(part("VB", 2), qw, scale=1.0, bias=bias[-2])
+            tt(part("VA", 2), z, hi, A.min)
+        k = len(tabs)
+        for b in range(15, -1, -1):
+            tt(ind(v("TB", low * WP, (low + k) * WP), v("SO", 4 * b, 4 * b + k)), col("VA", b, k), col("VB", b, k), A.max)
+
+    for t in range(RO):
+        rnd[0] = t
+        phase[0] = "c"
+        if t:
+            dma("y", v("M%d" % (1 - t % 2), 0, W), v("M%d" % (t % 2), 0, W), 512 * W, ext(None, "law%d_1" % (t - 1)))
+        if t == RO - 1:
+            ms(v("M0", NONE, W), float(NONE))
+        for name, f in (("l", listen), ("s", speak), ("w", None), ("e", choose)):
+            for h in range(2 if f else 0):
+                phase[0] = name + "AB"[h]
+                f(t, h)
+            if not f:
+                phase[0] = name
+                prepare(t)
+    phase[0] = "z"
     ow = W // OCH
     for c in range(OCH):
         a, b = c * ow, (c + 1) * ow
-        pd = v("PD%d" % (c % 3), 0, ow)
-        act(pd, v("M4", a, b), AF.Identity, 4096.0, bias[-4096.0 * MOFF])
-        tt(v("F1", a, b), v("NT", a, b), pd, A.add)
+        pd = v("PD%d" % (c % 2), 0, ow)
+        act(pd, v("M0", a, b), scale=4096.0, bias=bias[NONE])
+        tt(v("F1", a, b), pd, v("NT", a, b), A.subtract)
         dma("y", ext(T.ynm[:, a:b], "ynm", a, b), v("F1", a, b), 512 * ow)
     dma("y", ext(T.yz[:], "yz"), v("Z%d" % RO), 65536)
     dma("y", ext(T.yw[:], "yw"), v("WF"), 8192)
-    return ops, sent[0]
+    return ops
 
 
 def hazards(ops):
@@ -430,46 +509,160 @@ def hazards(ops):
                 l[:] = [e for e in l if not (a <= e[1] and e[2] <= b)]
             l.append((i, a, b, wr))
         if o["kind"] == "ext":
-            pre = {i - 1: False}
+            pre = {o["from"]: False}
         if o["kind"] == "dma" and o["q"] == "y" and not pre:
             pre = {j: False for j in range(i) if ops[j]["q"] == "y"}
         o["pre"] = {j: w for j, w in pre.items() if ops[j]["kind"] != "rem" or o["kind"] == "ext"}
 
 
-def one_pass(res, dur, nxt, npre, prio, ready0):
+def one_pass(res, dur, nxt, npre, key, ready0):
     n = len(res)
     left, ready, start = list(npre), list(ready0), [0.0] * n
-    free = {q: 0.0 for q in ("v", "s", "p", "g", "D", None)}
-    cand = {q: [] for q in free}
-    for i in range(n):
-        if left[i] == 0:
-            cand[res[i]].append(i)
-    order = []
-    while len(order) < n:
+    lines = {q: ([], []) for q in set(res)}
+    done = [False] * n
+    late = []
+    for i in sorted(range(n), key=lambda i: key[i]):
+        done[i] = True
+        if left[i]:
+            continue
+        late.append(i)
+        while late:
+            j = late.pop()
+            t, d = ready[j], dur[j]
+            if d:
+                bs, es = lines[res[j]]
+                k = len(bs)
+                while k and es[k - 1] > t:
+                    k -= 1
+                while k < len(bs) and bs[k] < t + d:
+                    t = max(t, es[k])
+                    k += 1
+                bs.insert(k, t)
+                es.insert(k, t + d)
+            start[j] = t
+            for s, la in nxt[j]:
+                if ready[s] < t + d + la:
+                    ready[s] = t + d + la
+                left[s] -= 1
+                if left[s] == 0 and done[s]:
+                    late.append(s)
+    return start
+
+
+def improve(res, dur, succ, pred, r0, start, rng):
+    n = len(res)
+    line = {}
+    for i in sorted(range(n), key=lambda i: (start[i], i)):
+        if res[i] is not None:
+            line.setdefault(res[i], []).append(i)
+    npre = [len(p) for p in pred]
+
+    def times():
+        nx, pv = [-1] * n, [-1] * n
+        left = list(npre)
+        for l in line.values():
+            for a, b in zip(l, l[1:]):
+                nx[a], pv[b] = b, a
+                left[b] += 1
+        head = list(r0)
+        order = [i for i in range(n) if not left[i]]
+        for i in order:
+            e = head[i] + dur[i]
+            for s, la in succ[i]:
+                if head[s] < e + la:
+                    head[s] = e + la
+                left[s] -= 1
+                if not left[s]:
+                    order.append(s)
+            s = nx[i]
+            if s >= 0:
+                if head[s] < e:
+                    head[s] = e
+                left[s] -= 1
+                if not left[s]:
+                    order.append(s)
+        tail = [0.0] * n
+        for i in reversed(order):
+            t = tail[nx[i]] if nx[i] >= 0 else 0.0
+            for s, la in succ[i]:
+                if t < tail[s] + la:
+                    t = tail[s] + la
+            tail[i] = t + dur[i]
+        return head, tail, nx, pv
+
+    def guess(seq, first, last, head, tail):
+        e = head[first] + dur[first] if first >= 0 else 0.0
+        hs = []
+        for x in seq:
+            h = max([e, r0[x]] + [head[p] + dur[p] + la for p, la in pred[x]])
+            hs.append(h)
+            e = h + dur[x]
+        t, m = tail[last] if last >= 0 else 0.0, 0.0
+        for x, h in zip(reversed(seq), reversed(hs)):
+            t = max([t] + [tail[s] + la for s, la in succ[x]]) + dur[x]
+            m = max(m, h + t)
+        return m
+
+    best, tabu, since = (1e18, None, None), {}, 0
+    for it in range(STEPS):
+        head, tail, nx, pv = times()
+        end = max(head[i] + tail[i] for i in range(n))
+        since += 1
+        if end < best[0] - 0.5:
+            best, since = (end, head, {q: list(l) for q, l in line.items()}), 0
+        elif since > 1500:
+            line.update({q: list(l) for q, l in best[2].items()})
+            tabu, since = {}, 0
+            continue
+        way = [i for i in range(n) if head[i] == r0[i] and head[i] + tail[i] >= end - 0.01]
+        i = way[int(rng.randint(len(way)))]
+        runs = [[i]]
+        while tail[i] > dur[i] + 0.01:
+            e = head[i] + dur[i]
+            nxt = [s for s, la in succ[i] if abs(tail[i] - dur[i] - la - tail[s]) < 0.01 and abs(head[s] - e - la) < 0.01]
+            s = nx[i]
+            if s >= 0 and abs(tail[i] - dur[i] - tail[s]) < 0.01 and abs(head[s] - e) < 0.01 and (not nxt or rng.rand() < 0.5):
+                runs[-1].append(s)
+            else:
+                s = nxt[int(rng.randint(len(nxt)))]
+                runs.append([s])
+            i = s
         pick = None
-        for q, l in cand.items():
-            if l:
-                t0 = max(free[q], min(ready[i] for i in l))
-                if pick is None or t0 < pick[0]:
-                    pick = (t0, q)
-        t0, q = pick
-        l = cand[q]
-        best = max((i for i in l if ready[i] <= t0 + C["look"]), key=lambda i: prio[i])
-        if ready[best] > t0:
-            fit = [i for i in l if ready[i] <= t0 and t0 + dur[i] <= ready[best] + 30]
-            if fit:
-                best = max(fit, key=lambda i: prio[i])
-        l.remove(best)
-        start[best] = max(t0, ready[best])
-        end = start[best] + dur[best]
-        free[q] = end
-        order.append(best)
-        for s, la in nxt[best]:
-            ready[s] = max(ready[s], end + la)
-            left[s] -= 1
-            if left[s] == 0:
-                cand[res[s]].append(s)
-    return order, start
+        for r in runs:
+            m = len(r)
+            pairs = {(a, m - 1) for a in range(max(0, m - 7), m - 1)} | {(0, b) for b in range(1, min(m, 7))}
+            if m > 3:
+                a = int(rng.randint(m - 1))
+                pairs.add((a, min(m - 1, a + 1 + int(rng.randint(4)))))
+            for a, b in sorted(pairs):
+                u, w = r[a], r[b]
+                for fwd in (True, False) if b > a + 1 else (True,):
+                    if fwd:
+                        if any(head[s] <= head[w] for s, _ in succ[u]):
+                            continue
+                        seq = r[a + 1:b + 1] + [u]
+                        bad = any(tabu.get((x, u), 0) > it for x in seq)
+                    else:
+                        if any(tail[p] <= tail[u] for p, _ in pred[w]):
+                            continue
+                        seq = [w] + r[a:b]
+                        bad = any(tabu.get((w, x), 0) > it for x in seq)
+                    val = guess(seq, pv[u], nx[w], head, tail)
+                    if bad and val >= best[0]:
+                        continue
+                    val += rng.rand() * 30
+                    if pick is None or val < pick[0]:
+                        pick = (val, u, w, seq, fwd)
+        if pick is None:
+            tabu = {}
+            continue
+        _, u, w, seq, fwd = pick
+        l = line[res[u]]
+        k = l.index(u)
+        l[k:k + len(seq)] = seq
+        for x in seq:
+            tabu[(u, x) if fwd else (x, w)] = it + 8 + int(rng.randint(12))
+    return best[0], best[1]
 
 
 def schedule(ops):
@@ -480,53 +673,57 @@ def schedule(ops):
     for i, o in enumerate(ops):
         for j, w in sorted(o["pre"].items()):
             p = ops[j]
-            la = 0 if (p["q"] == "p" and o["q"] == "p") or not w else C["lat"]
+            la = 1 if (p["q"] == "p" and o["q"] == "p") or not w else C["lat"]
             la += C["dma"] if o["kind"] == "dma" and w else 0
             la += p["dur"] - 500 if p["kind"] == "rem" else 0
             succ[j].append((i, la))
             pred[i].append((j, la))
-    prio = [0.0] * n
-    for i in range(n - 1, -1, -1):
-        prio[i] = dur[i] + max([la + prio[s] for s, la in succ[i]], default=0.0)
-    npre, nsucc = [len(p) for p in pred], [len(p) for p in succ]
+    npre = [len(p) for p in pred]
     r0 = [C["dma"] if res[i] == "D" else 0.0 for i in range(n)]
 
-    def forward(pr):
-        order, st = one_pass(res, dur, succ, npre, pr, r0)
-        return max(st[i] + dur[i] for i in range(n)), order, st
+    def forward(key):
+        st = one_pass(res, dur, succ, npre, key, r0)
+        end = max(st[i] + dur[i] for i in range(n))
+        return end + 0.5 * sum(st) / n, end, st
 
-    def justified(st):
-        _, sb = one_pass(res, dur, pred, nsucc, [st[i] + dur[i] for i in range(n)], [0.0] * n)
-        return [sb[i] + dur[i] for i in range(n)]
-
-    groups = {}
+    key0, groups, nth = [], {}, {}
     for i, o in enumerate(ops):
-        groups.setdefault(o["lab"], []).append(i)
-        groups.setdefault((o["lab"], o["rnd"]), []).append(i)
-    groups = list(groups.values())
-    rng = np.random.RandomState(SEED)
-    best = forward(prio)
-    for it in range(TRIES):
-        if it % 200 == 0:
-            pr = justified(best[2])
+        k = (o["lab"], o["rnd"])
+        j = nth.get(k, 0)
+        nth[k] = j + 1
+        groups.setdefault(o["lab"], {}).setdefault(j, []).append(i)
+        first, step = PLAN.get(o["lab"], (None, None))
+        if first is None or (step is None and j):
+            key0.append(max([key0[p] + dur[p] + la for p, la in pred[i]], default=r0[i]))
         else:
-            pr = list(prio)
-            for _ in range(int(rng.randint(1, 4))):
-                grp = groups[int(rng.randint(len(groups)))]
-                if rng.rand() < 0.3:
-                    grp = grp[int(rng.randint(len(grp))):]
-                d = float(rng.choice([-1, 1]) * rng.choice([200, 600, 2000, 6000]))
-                for i in grp:
-                    pr[i] += d
-        got = forward(pr)
-        if got[0] <= best[0]:
-            best, prio = got, pr
-    order = best[1]
+            key0.append(1000 * (START + PERIOD * o["rnd"] + first + j * (step or 0)))
+    groups = [list(x.values()) for x in groups.values()]
+    rng = np.random.RandomState(SEED)
+    best = cur = forward(key0)
+    for it in range(TRIES):
+        key = list(key0)
+        one = int(rng.randint(RO)) if rng.rand() < it / TRIES else -1
+        for _ in range(int(rng.randint(1, 3))):
+            grp = groups[int(rng.randint(len(groups)))]
+            a = int(rng.randint(len(grp))) if rng.rand() < 0.4 else 0
+            b = a + 1 + int(rng.randint(len(grp) - a)) if rng.rand() < 0.4 else len(grp)
+            d = float(rng.choice([-1, 1]) * rng.choice([150, 400, 1000, 2500]))
+            for l in grp[a:b]:
+                for i in l:
+                    if one < 0 or ops[i]["rnd"] == one:
+                        key[i] += d
+        got = forward(key)
+        if got[0] <= cur[0] + HEAT * rng.rand() * (1 - it / TRIES):
+            cur, key0 = got, key
+            if got[1] < best[1]:
+                best = got
+    end, start = improve(res, dur, succ, pred, r0, best[2], rng)
+    order = sorted(range(n), key=lambda i: (start[i], i))
     first = [i for i in order if ops[i]["kind"] == "dma" and not any(ops[i]["pre"].values())]
-    return first + [i for i in order if i not in set(first)]
+    return first + [i for i in order if i not in set(first)], (end, order, start)
 
 
-def emit(g, T, ops, order, sent):
+def emit(g, T, ops, order):
     Q = {"v": g.vector, "s": g.scalar, "p": g.tensor, "g": g, "y": g.sync}
     at = {i: k for k, i in enumerate(order)}
     known = {q: {} for q in Q}
@@ -573,10 +770,9 @@ def emit(g, T, ops, order, sent):
             ins.then_inc(T.sem[o["sem"]], 16)
         elif o["kind"] == "c" and o.get("mark"):
             ins.then_inc(T.sem["c" + o["q"]], 1)
-    g.wait_ge(T.sem.sent, sent)
     for o in ops:
-        if o["kind"] == "dma" and not o.get("mark"):
-            g.wait_ge(T.sem[o["sem"]], 16)
+        if o["kind"] in ("dma", "ext") and not o.get("mark"):
+            g.wait_ge(T.sem[o["sem"]], o["cnt"])
 
 
 ORDER = []
@@ -585,8 +781,8 @@ ORDER = []
 def rank_program(g, core, T, topo):
     if T.rank_of(core) is None:
         return
-    ops, sent = build(g, core, T, topo)
+    ops = build(g, core, T, topo)
     hazards(ops)
     if not ORDER:
-        ORDER.extend(schedule(ops))
-    emit(g, T, ops, ORDER, sent)
+        ORDER.extend(schedule(ops)[0])
+    emit(g, T, ops, ORDER)

@@ -7,25 +7,69 @@ WP = W + 16
 CM = 1.5 * 2 ** 35
 HALF = 1536
 BIG = 8192.0
-NCH = 6
-OCH = 6
-NV = (0, 1)
+LOADS = (512, 1024, 1024, 512)
+STORES = (256, 768, 1024, 1024)
+NV = ((1, 1), (1, 1), (1, 1), (1, 1))
+WIDE = ((4, 4, 4, 4), (1, 1, 2, 4, 4, 4))
+EES = True
+FAR = 63.0
 GW = 1
-TRIES = 12000
-STEPS = 8000
+STEPS = ((55000, 100, None), (25000, 60, (3,)), (25000, 80, (0,)), (20000, 30, (0, 1, 2, 3)))
 SEED = 0
-HEAT = 100
-C = {"cyc": 0.83, "g": 1.56, "s": 3.8, "tt": 2.0, "v": 50, "a": 65, "pe": 0.5, "pf": 10, "lat": 120,
-     "dma": 2000, "bw": 180.0, "rem": 2500}
-START, PERIOD = 12.5, 23.5
-PLAN = {"sNElA": (0.1, 0), "sWBlA": (-1.0, 0.2), "sXGlA": (1.1, 1.1), "sABlA": (2.6, 1.3), "sEFlA": (3.8, 0),
-        "sHIlA": (5.7, 0), "sNElB": (5.0, 0), "sWBlB": (5.9, 0.2), "sTTlA": (6.9, 0), "sXGlB": (7.1, 1.0),
-        "sDClA": (7.85, 0), "sABlB": (8.75, 1.0), "sNEsA": (9.8, 0), "sOBsA": (10.6, 0.2), "sEFlB": (12.0, 0),
-        "sHIlB": (12.2, 0), "sTTlB": (12.4, 0), "sXOsA": (12.6, 0), "sDClB": (12.9, 0), "sULsA": (16.0, 0),
-        "sCNsA": (13.1, 1.1), "sNEsB": (14.6, 0), "sXOsB": (15.8, 0), "sHBsB": (15.5, 0), "sOBsB": (15.75, 0.15),
-        "sVAw": (14.0, 0), "sULsB": (18.5, 0), "sCNsB": (18.2, 0.8), "vEQlA": (1.2, 0.4), "vEQlB": (6.4, 0.4),
-        "vXGlA": (4.3, 0.2), "vXGlB": (5.8, 0.2), "vEQ2sA": (11.0, 0.4), "vEQ2sB": (17.0, 0.6), "vTBw": (17.4, 0.4),
-        "pPQw": (9.0, None), "pPD0sB": (13.0, None)}
+C = {"cyc": 0.87, "in": 1.56, "out": 3.8, "tt": 2.0, "v": 53, "s": 68, "fix": 25, "act": 1.04, "pe": 0.5, "pf": 10, "lat": 110,
+     "dma": 2500, "bw": 340.0, "rem": 2600, "hold": 700, "once": 3000}
+ROUND = {
+    "v": "OFFlA -NTw:14-15 XGlA:2-3 XGlA:1 EQlA:2-3 XGlA:0 WUlB EQlA:0 TR1lB:1 EQlA:1 TR1lB:0 OFFlB EQlB:0 EQlB:5 DClA EQlB:2 SClA ANlA VWlA:1 OHlA VWlA:0 OUlA EQlB:1 EQlB:3-4 TS0sA:0-1 OF2sA EQ2sA:1 EQ2sA:0 EQ2sA:2-4 DClB EQ2sA:5 SClB ANlB OHlB VWlB:1 VWlB:0 OUlB TS1sB:1 TS1sB:0 EWw:0 OF2sB EWw:1 EQ2sB:1 EQ2sB:0 EQ2sB:2 VAw:0 EQ2sB:4 SOw:0 EQ2sB:3 SOw:1 VAw:1 SOw:2 EQ2sB:5 TBw:0 SC2eA TBw:1 WIeA NTw:0 WAeA TBw:2 WSeA TBw:3 NTw:1 TBw:4 NTw:2 TBw:5 NTw:3 TBw:6 NTw:4 TBw:7-8 NTw:5 TBw:9 SC2eB TBw:10 WIeB NTw:6 TBw:11 NTw:7 TBw:12 WAeB NTw:8 WSeB TBw:13 NTw:9 TBw:14 NTw:10 TBw:15 NTw:11 +WUlA NTw:12-13 +TR0lA:1 +TR0lA:0",
+    "s": "EFlA HIlA XGlA:0 XGlA:2 XGlA:1 ABlA:0 WBlB NElB ABlA:3 ABlA:1-2 EFlB XGlB:0 TTlA HIlB XGlB:1-3 ABlB:0 NEsA OBsA ABlB:1 XOsA ULsA ABlB:2-3 CNsA:3 TTlB CNsA:2 CNsA:0-1 NEsB XOsB S1w HBsB OBsB AEw EEw SGeA ULsB CNsB:0 VBw:0 CNsB:2 S2w VBw:2 CBeA S3w VBw:1 CNsB:3 CNsB:1 CBeB SGeB S4w THRw +NElA +WBlA",
+    "p": "PK0lA:1 PK1lB:0 PK0lA:2-3 PD0lA:0 PSlB PD1lA PD0lA:1 PQw:1 PElA PRlA PK0lA:4-5 PD0lB:0 PQw:2 PK1lB:1 PD1lB:0 PSsA PQw:3 PK1lB:2 PD0lB:1 PD1lB:1 PElB PD1w:0 PRlB PK1lB:3 PD0sB:0 PK1lB:4 PSeA:0 PK1lB:5 PEeA PK1w PD0sB:1 PK0w:0 PD1w:1 PQw:4-6 PD1w:2-3 PD0w:0 PD1w:4 PQw:7 PK0w:1 PReA PD0w:1 PK1eB:0 PSeA:1 +PK0lA:0 PSeA:2 PEeB +PQw:0 PReB PK1eB:1-2 +PSlA",
+    "g": "WBlA:0-1 WBlB:0-1 OBsA:0-1 VAw sendsB OBsB:0-1 sendeA sendeB",
+}
+LAST = {
+    "v": "OFFlA -NTw:14-15 XGlA:0-3 EQlA:2 EQlA:0 WUlB EQlA:3 TR1lB:0-1 EQlA:1 OFFlB XGlB:0-3 EQlB:3 DClA EQlB:5 SClA EQlB:0 ANlA EQlB:2 OHlA VWlA:1 VWlA:0 EQlB:1 OUlA EQlB:4 TS0sA:1 TS0sA:0 OF2sA XTlB EQ2sA:2 EQ2sA:0 EQ2sA:4 DClB EQ2sA:3 SClB EQ2sA:1 ANlB OHlB VWlB:1 VWlB:0 OUlB EQ2sA:5 EWw:0 EEw TS1sB:0-1 EWw:1 OF2sB VAw SOw:0-1 EQ2sB:0-2 NTw:0 TBw:0 NTw:1 TBw:1 NTw:2 TBw:2 NTw:3 TBw:3 NTw:4 TBw:4 NTw:5 TBw:5 NTw:6 TBw:6 NTw:7 TBw:7 NTw:8 TBw:8 NTw:9 TBw:9 NTw:10 TBw:10 NTw:11 TBw:11 NTw:12 TBw:12 NTw:13 TBw:13 NTw:14 TBw:14 NTw:15 TBw:15 SC2eA F1z:0 WIeA F1z:1 EQ2sB:3 F1z:2 WAeA EQ2sB:4 WSeA F1z:3 EQ2sB:5 WFeA F1z:4-7 SC2eB WIeB WAeB WSeB WFeB",
+    "s": "EFlA HIlA XGlA:1 XGlA:0 ABlA:3 NElB XGlA:2 ABlA:0 WBlB EFlB ABlA:1-2 XGlB:1 TTlA HIlB XGlB:0 XGlB:2 ABlB:1 ABlB:0 NEsA OBsA ABlB:3 ABlB:2 CNsA:0 TTlB CNsA:1 CNsA:3 XOsA NEsB ULsA HBsB OBsB XOsB VBw:0-1 CNsA:2 ULsB CNsB:0-1 CBeA SGeA CNsB:2-3 PD0z:0 PD1z:0 PD0z:1 CBeB PD1z:1 PD0z:2 PD1z:2 PD0z:3 SGeB",
+    "p": "PK0lA:1-3 PSlB PD0lA:0 PD1lA PQw:1 PD0lA:1 PElA PRlA PQw:2 PK0lA:4-5 PD1lB PK1lB:1 PD0lB:0 PK1lB:2 PSsA PD0lB:1 PElB PK1lB:3 PRlB PD0sB:0 PK1lB:4-5 PQw:3 PD0sB:1 PK0w:0 PQw:4-7 PK0w:1 PD0w:0-1 PEeA PReA PSeA:0-2 PK1eB:0 PReB PEeB PK1eB:1-2",
+    "g": "WBlA:0-1 WBlB:0-1 OBsA:0-1 OBsB:0-1 sendsB VAw sendeA sendeB",
+}
+
+ROUND = {
+    "v": "OFFlA -NTw:14 XGlA:1 XGlA:0 XGlA:2 -NTw:15 XGlA:3 EQlA:0 WUlB EQlA:1 EQlA:3 EQlA:2 TR1lB:0-1 OFFlB XGlB:3 EQlB:2 EQlB:5 DClA XGlB:1-2 SClA EQlB:1 ANlA VWlA:1 OHlA XGlB:0 VWlA:0 EQlB:3 OUlA EQlB:0 EQlB:4 TS0sA:1 TS0sA:0 OF2sA EQ2sA:0-3 DClB EQ2sA:4 SClB ANlB OHlB VWlB:1 VWlB:0 OUlB EQ2sA:5 EWw:0 TS1sB:0-1 OF2sB EQ2sB:0-1 EWw:1 EQ2sB:2-4 SOw:0 VAw:0 SOw:1 EQ2sB:5 SOw:2 VAw:1 SC2eA WIeA TBw:0 WAeA TBw:1 WSeA TBw:2 NTw:0 TBw:3 NTw:1 TBw:4 NTw:2 TBw:5 NTw:3 TBw:6 NTw:4 TBw:7 NTw:5 TBw:8 NTw:6 TBw:9 SC2eB NTw:7 TBw:10 NTw:8 WIeB TBw:11 WAeB NTw:9 TBw:12 WSeB TBw:13 NTw:10 TBw:14 NTw:11 +WUlA TBw:15 NTw:12-13 +TR0lA:1 +TR0lA:0",
+    "s": "EFlA HIlA XGlA:0 XGlA:2 XGlA:1 NElB ABlA:0 ABlA:3 WBlB ABlA:1-2 EFlB HIlB TTlA XGlB:0-2 ABlB:0-1 NEsA XOsA OBsA ABlB:3 ABlB:2 ULsA TTlB CNsA:1 CNsA:0 CNsA:3 CNsA:2 NEsB XOsB HBsB S1w OBsB ULsB AEw CNsB:2 EEw S2w CNsB:1 S3w CNsB:0 S4w VBw:0 CBeA SGeA VBw:2 VBw:1 CNsB:3 SGeB CBeB THRw +NElA +WBlA",
+    "p": "PK0lA:1-3 PD0lA:0 PSlB PD1lA PD0lA:1 PElA PRlA PK0lA:4 PK1lB:1-2 PK0lA:5 PD0lB:0 PD1lB PSsA PK1lB:3 PD0lB:1 PElB PRlB PD0sB:0 PK1lB:4-5 PQw:1 PSeA:0 PQw:2 PD0sB:1 PD1w:0-1 PK1w PK0w:0 PD1w:2-3 PQw:3 PD1w:4 PEeA PD0w:0 PQw:4 PK0w:1 PReA PQw:5-6 PD0w:1 PSeA:1-2 PEeB PK1eB:0 +PK0lA:0 PReB +PQw:0 PK1eB:1-2 +PK1lB:0 +PSlA",
+    "g": "WBlA:0-1 Mc:0-1 WBlB:0 Q2w:0 WBlB:1 Q2w:1 Mc:2-4 OBsA:0-1 Mc:5 VAw OBsB:0-1 sendsB sendeA sendeB",
+}
+LAST = {
+    "v": "OFFlA -NTw:14-15 XGlA:0 XGlA:3 XGlA:2 XGlA:1 EQlA:2 EQlA:1 WUlB EQlA:0 EQlA:3 TR1lB:1 TR1lB:0 OFFlB XGlB:2 EQlB:1 XGlB:3 EQlB:5 DClA EQlB:4 SClA XGlB:0 ANlA EQlB:0 OHlA XGlB:1 VWlA:0 EQlB:2 OUlA EQlB:3 TS0sA:1 TS0sA:0 VWlA:1 OF2sA XTlB EQ2sA:0-3 DClB EQ2sA:4 SClB ANlB VWlB:1 OHlB VWlB:0 OUlB EQ2sA:5 EWw:0 TS1sB:1 TS1sB:0 OF2sB EEw EWw:1 VAw EQ2sB:2 SOw:0 EQ2sB:1 SOw:1 EQ2sB:0 NTw:0 TBw:0 NTw:1 TBw:1 NTw:2 TBw:2 NTw:3 TBw:3 NTw:4 TBw:4 NTw:5 TBw:5 NTw:6 TBw:6 NTw:7 TBw:7 NTw:8 TBw:8 NTw:9 TBw:9 NTw:10 TBw:10 NTw:11 TBw:11 NTw:12 TBw:12 NTw:13 TBw:13 NTw:14 TBw:14 NTw:15 TBw:15 EQ2sB:5 F1z:0 SC2eA F1z:1 WIeA WAeA F1z:2 EQ2sB:3 F1z:3-4 EQ2sB:4 F1z:5 WSeA F1z:6 WFeA F1z:7 SC2eB WIeB WAeB WSeB WFeB",
+    "s": "EFlA HIlA XGlA:1 XGlA:0 XGlA:2 ABlA:1 ABlA:0 NElB WBlB ABlA:3 ABlA:2 EFlB HIlB XGlB:1 TTlA XGlB:0 XGlB:2 ABlB:1 ABlB:0 NEsA OBsA ABlB:3 ABlB:2 CNsA:2 ULsA TTlB CNsA:3 CNsA:0-1 NEsB XOsB HBsB OBsB CNsB:3 XOsA VBw:0-1 CNsB:0 CBeA CNsB:1 SGeA ULsB CNsB:2 PD0z:0 PD1z:0 PD0z:1 PD1z:1 PD0z:2 CBeB PD1z:2 PD0z:3 SGeB",
+    "p": "PK0lA:1-3 PD1lA PD0lA:0 PSlB PD0lA:1 PElA PRlA PK1lB:1-2 PK0lA:4-5 PD1lB PK1lB:3 PD0lB:0 PSsA PD0lB:1 PElB PRlB PK1lB:4-5 PQw:1 PD0sB:0 PQw:2 PD0sB:1 PK0w:0 PQw:3-6 PK0w:1 PD0w:0-1 PSeA:0 PReA PEeA PSeA:1 PReB PK1eB:0 PSeA:2 PK1eB:1 PEeB PK1eB:2",
+    "g": "WBlA:0-1 Mc:0-1 WBlB:0-1 Q2w:0-1 Mc:2-4 OBsA:0-1 Mc:5 VAw OBsB:0-1 sendsB sendeA sendeB",
+}
+
+ROUND = {
+    "v": "OFFlA -NTw:13 XGlA:3 XGlA:2 -NTw:14 XGlA:0 -NTw:15 EQlA:1 WUlB XGlA:1 EQlA:3 EQlA:2 TR1lB:1 TR1lB:0 EQlA:0 OFFlB EQlB:5 EQlB:4 EQlB:2 EQlB:1 DClA EQlB:0 SClA ANlA OHlA VWlA:0-1 OUlA EQlB:3 TS0sA:1 TS0sA:0 OF2sA EQ2sA:2 EQ2sA:0 EQ2sA:4 DClB EQ2sA:3 SClB ANlB VWlB:1 OHlB VWlB:0 EQ2sA:1 OUlB EQ2sA:5 TS1sB:1 TS1sB:0 EWw:1 OF2sB EWw:0 EQ2sB:2 EQ2sB:1 EQ2sB:4 EQ2sB:3 VAw:0 SOw:0 EQ2sB:0 SOw:1 SC2eA EQ2sB:5 SOw:2 VAw:1 WIeA TBw:0 WAeA TBw:1 WSeA TBw:2 NTw:0 TBw:3 NTw:1 TBw:4 NTw:2 TBw:5 NTw:3 TBw:6 NTw:4 TBw:7 NTw:5 TBw:8 NTw:6 TBw:9 NTw:7 TBw:10 SC2eB TBw:11 NTw:8 TBw:12 WIeB +WUlA TBw:13 NTw:9 TBw:14 WAeB TBw:15 WSeB NTw:10-11 +TR0lA:0-1 NTw:12",
+    "s": "EFlA HIlA XGlA:0-2 NElB WBlB ABlA:0 ABlA:3 ABlA:1 EFlB ABlA:2 HIlB XGlB:0-1 TTlA XGlB:2 ABlB:0 XGlB:3 ABlB:1 NEsA OBsA ABlB:2-3 CNsA:3 TTlB ULsA CNsA:1 CNsA:0 CNsA:2 NEsB HBsB OBsB XOsA ULsB XOsB CNsB:2 AEw EEw SGeA CBeA S1w CNsB:0 S2w S3w VBw:0 S4w THRw VBw:2 CNsB:1 VBw:1 CNsB:3 SGeB CBeB +NElA +WBlA",
+    "p": "PK0lA:1 PD0lA:0 PSlB PK0lA:2 PD1lA PK0lA:3 PD0lA:1 PQw:1-2 PElA PRlA PD0lB:0 PD1lB:0 PK0lA:4-5 PK1lB:1-2 PD0lB:1 PSsA PD1lB:1 PElB PRlB PK1lB:3 PD0sB:0 PD1w:0 PK1lB:4 PSeA:0 PK1lB:5 PD0sB:1 PK0w:0 PQw:3 PK1w PEeA PD1w:1 PD0w:0 PQw:4 PReA PD1w:2 PD0w:1 PD1w:3-4 PK0w:1 PQw:5-6 PSeA:1-2 +PK0lA:0 PK1eB:0 +PQw:0 PEeB PReB PK1eB:1-2 +PSlA +PK1lB:0",
+    "g": "WBlA:1 Q2w:0-1 WBlB:0-1 Mc:5 Mc:1 Mc:0 OBsA:0-1 VAw Mc:4 Mc:3 Mc:2 OBsB:0-1 sendsB sendeA sendeB +WBlA:0",
+}
+ROUND = {
+    "v": "OFFlA -NTw:15 XGlA:1 XGlA:3 XGlA:0 WUlB EQlA:3 EQlA:2 XGlA:2 TR1lB:0-1 EQlA:0 OFFlB EQlA:1 EQlB:4 EQlB:1 XGlB:3 EQlB:2 DClA EQlB:5 XGlB:2 XGlB:1 SClA XGlB:0 ANlA VWlA:1 OHlA VWlA:0 EQlB:0 OUlA EQlB:3 TS0sA:0-1 OF2sA EQ2sA:2 EQ2sA:1 EQ2sA:3 DClB EQ2sA:4 SClB EQ2sA:0 ANlB VWlB:1 OHlB VWlB:0 OUlB EQ2sA:5 TS1sB:0-1 OF2sB EWw:0 EQ2sB:0-2 EWw:1 EQ2sB:4 SOw:0 VAw:0 SOw:1 EQ2sB:5 SOw:2 VAw:1 EQ2sB:3 TBw:0 SC2eA TBw:1 NTw:0 WIeA TBw:2 WAeA TBw:3 WSeA NTw:1 TBw:4 NTw:2 TBw:5 NTw:3 TBw:6 NTw:4 TBw:7 NTw:5 SC2eB TBw:8 WIeB NTw:6 TBw:9 NTw:7 WAeB TBw:10 NTw:8 WSeB TBw:11 NTw:9 TBw:12 NTw:10 TBw:13 NTw:11 TBw:14 +WUlA TBw:15 NTw:12-13 +TR0lA:0-1 NTw:14",
+    "s": "EFlA HIlA XGlA:0 NElB XGlA:2 WBlB ABlA:0 XGlA:1 EFlB ABlA:3 ABlA:2 ABlA:1 HIlB XGlB:0 TTlA XGlB:2 XGlB:1 ABlB:0 ABlB:3 ABlB:1 NEsA OBsA XOsA ULsA ABlB:2 CNsA:0 TTlB CNsA:2 CNsA:1 CNsA:3 NEsB S1w XOsB HBsB S2w OBsB AEw CNsB:0 EEw S3w CNsB:1 CBeA S4w ULsB SGeA VBw:0 CNsB:2 THRw VBw:2 VBw:1 CNsB:3 SGeB CBeB +NElA +WBlA",
+    "p": "PK0lA:1 PQw:0 PSlB PD0lA:0 PK0lA:2 PD0lA:1 PK0lA:3 PD1lA PElA PRlA PK1lB:1 PK0lA:4 PK1lB:2 PK0lA:5 PK1lB:3 PD0lB:0 PD1lB PSsA PD0lB:1 PElB PRlB PD1w:0 PK1lB:4 PSeA:0 PK1lB:5 PQw:1 PD0sB:0 PQw:2 PK1w PD0sB:1 PK0w:0 PQw:3 PD1w:1-2 PQw:4 PReA PD1w:3-4 PK0w:1 PEeA PD0w:0-1 PQw:5-6 PSeA:1 PK1eB:0 +PK0lA:0 PSeA:2 PEeB PReB PK1eB:1-2 +PSlA +PK1lB:0",
+    "g": "WBlA:1 Q2w:1 Mc:4 WBlB:0-1 Q2w:0 Mc:3 VAw Mc:1 Mc:5 OBsA:0-1 Mc:2 Mc:0 OBsB:0-1 sendsB sendeA sendeB +WBlA:0",
+}
+ROUND["v"] = "OFFlA XGlA EQlA:2 WUlB EQlA:3 TR1lB:1 EQlA:0 TR1lB:0 EQlA:1 OFFlB XGlB EQlB:1 EQlB:4 DClA EQlB:2 SClA ANlA VWlA:1 OHlA VWlA:0 OUlA EQlB:5 TS0sA:1 TS0sA:0 EQlB:0 OF2sA EQlB:3 EQ2sA:1-2 EQ2sA:0 EQ2sA:4 DClB EQ2sA:3 SClB ANlB OHlB VWlB:1 VWlB:0 OUlB EQ2sA:5 TS1sB:0-1 OF2sB EWw:1 EQ2sB:1 EQ2sB:0 EWw:0 EQ2sB:2 VAw:0 S2w SOw:0 EQ2sB:5 SOw:1 VAw:1 EQ2sB:4 SOw:2 S3w EQ2sB:3 Mw:0 TBw:0 SC2eA TBw:1 Mw:1 WIeA TBw:2 WAeA Mw:2 TBw:3 Mw:3 WSeA TBw:4 Mw:4 TBw:5 Mw:5 TBw:6 Mw:6 TBw:7 Mw:7 TBw:8 Mw:8 TBw:9 Mw:9 TBw:10 Mw:10 SC2eB Mw:11 TBw:11 WIeB Mw:12 WAeB Mw:13 TBw:12 Mw:14 +WUlA WSeB Mw:15 TBw:13 THRw TBw:14 +TR0lA:0-1 TBw:15"
+ROUND["v"] = "OFFlA XGlA WUlB TR1lB:1 TR1lB:0 EQlA:0 OFFlB EQlA:2-3 EQlA:1 XGlB EQlB:4 EQlB:1 DClA EQlB:2 SClA ANlA OHlA VWlA:1 VWlA:0 OUlA EQlB:0 EQlB:5 TS0sA:0-1 EQlB:3 OF2sA EQ2sA:1 EQ2sA:0 EQ2sA:3-4 DClB EQ2sA:2 SClB ANlB VWlB:1 OHlB VWlB:0 OUlB EQ2sA:5 S2w TS1sB:0 S3w TS1sB:1 EWw:1 OF2sB EWw:0 EQ2sB:1-3 EQ2sB:0 VAw:0 EQ2sB:5 SOw:0 SC2eA SOw:1 VAw:1 SOw:2 EQ2sB:4 WIeA TBw:0 WAeA Mw:0 TBw:1 Mw:1 WSeA TBw:2 Mw:2 TBw:3 Mw:3 TBw:4 Mw:4 TBw:5 Mw:5 TBw:6 Mw:6 TBw:7 Mw:7 SC2eB Mw:8 TBw:8 WIeB Mw:9 WAeB Mw:10 TBw:9 Mw:11 WSeB TBw:10 Mw:12 TBw:11 Mw:13 +WUlA Mw:14 TBw:12 Mw:15 TBw:13 THRw TBw:14 +TR0lA:1 +TR0lA:0 TBw:15"
+ROUND["s"] = "HIlA XGlA:0 NElB ABlA:3 WBlB XGlA:1-2 ABlA:0 EFlB ABlA:1 HIlB ABlA:2 XGlB:0 TTlA XGlB:1-2 ABlB:0 NEsA XOsA ABlB:1 OBsA ULsA ABlB:3 ABlB:2 CNsA:2 TTlB CNsA:1 CNsA:3 CNsA:0 S1w XOsB NEsB HBsB OBsB ULsB AEw CNsB:2 EEw CBeA CNsB:0 SGeA VBw:0 CNsB:1 VBw:2 VBw:1 CNsB:3 CBeB SGeB +WBlA +NElA +EFlA"
+ROUND["p"] = "PSlB PK1lB:0 PK0lA:1-2 PD0lA:0 PQw:1 PK0lA:3 PD1lA PQw:2 PD0lA:1 PElA PK1lB:1 PRlA PK1lB:2 PK0lA:4-5 PD0lB:0 PD1lB PSsA PD0lB:1 PSeA:0 PD1w:0 PElB PRlB PD0sB:0 PK1lB:3-5 PK1w PD0sB:1 PK0w:0 PD1w:1 PQw:3 PD1w:2 PReA PQw:4 PD1w:3 PEeA PD1w:4 PK0w:1 PSeA:1 PD0w:0-1 PK1eB:0 PSeA:2 PQw:5-6 +PQw:0 PEeB PReB +PK0lA:0 PK1eB:1-2 +PSlA"
+ROUND["g"] = "WBlA:1 ZRlB:0-2 WBlB:0-1 Q2w:0-1 VAw OBsA:0-1 OBsB:0-1 sendsB sendeA +ZRlA:0-2 sendeB +WBlA:0"
+LAST["v"] = LAST["v"].replace("-NTw:14-15 ", "").replace("TBw", "Mw").replace("NTw", "TBw")
+LAST["v"] = LAST["v"][:LAST["v"].index("EQ2sA:5 EWw:0")] + (
+    "EQ2sA:5 TS1sB:0-1 EWw:1 OF2sB EEw EQ2sB:0-2 EWw:0 EQ2sB:3 VAw SOw:0-1 EQ2sB:4 SC2eA EQ2sB:5 WIeA "
+    + " ".join("TBw:%d Mw:%d" % (j, j) + {0: " WAeA", 1: " WSeA", 2: " WFeA", 8: " SC2eB", 9: " WIeB", 10: " WAeB", 11: " WSeB",
+                                          12: " WFeB"}.get(j, "") for j in range(16)) + " F1z:0-7")
+LAST["s"] = LAST["s"][:LAST["s"].index("NEsB XOsB")] + (
+    "NEsB HBsB OBsB XOsA XOsB ULsB CNsB:0-1 CBeA SGeA VBw:0-1 CNsB:2-3 CBeB SGeB PD0z:0 PD1z:0 PD0z:1 PD1z:1 PD0z:2 PD1z:2 PD0z:3")
+LAST["p"] = ""
+LAST["g"] = "WBlA:1 ZRlB:0-2 WBlB:0-1 Q2w:0-1 OBsA:0-1 VAw OBsB:0-1 sendsB sendeA sendeB"
 
 F, B, H, I32, U16 = "float32", "bfloat16", "float16", "int32", "uint16"
 SIZE = {F: 4, B: 2, H: 2, I32: 4, U16: 2}
@@ -59,14 +103,15 @@ for _t in range(RO + 1):
 for _t in range(RO):
     _own("WU%d" % _t, 16, U16)
     _own("XO%d" % _t, 256, B)
-    _own("WS%d" % _t, 16, U16)
+    _own("WS%d" % _t, 16, H)
+    _own("VW%d" % _t, 48, H)
 for _d, _l in [
-    (F, "NE 544 TR0 288 TR1 288 TS0 288 TS1 288 WB 512 OB 512 EF 256 UL 256 DC 256 SC2 256 RS 16 SP 4 OH 16 RST 256 "
-        "RS0 128 DG 272 PM32 256 ID32 128 THF 1 THR 1 S1 1 PF 16 BI 16 T3 8 T4 8 T5 8 SHT 8 RTT 8"),
+    (F, "NE 544 TR0 288 TR1 288 TS0 288 TS1 288 WB 1024 OB 1024 EF 256 UL 256 SC2 256 WI 16 WA 16 JK 16 SP 4 OH 16 RST 256 "
+        "RS0 128 DG 272 ID32 128 TH2 1 THR 1 S1 1 PF 16 BI 16 T3 8 T4 8 T5 8 SHT 8 RTT 8"),
     (B, "HI 256 TT 256 CB 256 SG 256 EW 512 EE 288 HB 256 SEL 2048 ONE 512 CIB 128 ID 128 IDM 128 IM64 128 I16K 128 "
-        "IM8K 128 I8K 128 IH 128 IHM 128 I1536 128 I2 128 PMT 256 P4K 128 P22 128 GS 8 CP 272 CQ 272 CIR 1024 RT 1024"),
-    (H, "VW0 48 VW1 48 KN 32"),
-    (I32, "SC 512 AN 32 WI 16 WA 16 S2 1 S3 1 PI 1 PJ 8 CI 272 CJ 272 C16 8 T1 8 T2 8"),
+        "IM8K 128 I8K 128 IH 128 IHM 128 I1536 128 I2 128 ZR 1024 AE 288 KC 256 PM 256 PMD 256 PMT 256 P4K 128 P21 128 GS 8 CP 272 CQ 272 CIR 1024 RT 1024"),
+    (H, "KN 32 Q2 32 DC 256"),
+    (I32, "SC 512 AN 32 S2 1 S3 1 PI 1 PJ 8 CI 272 CJ 272 C16 8 T1 8 T2 8"),
     (U16, "OFF 256 OF2 256 OU 16 SO 64 TRK 8 TRB 8"),
 ]:
     for _n, _c in zip(_l.split()[0::2], _l.split()[1::2]):
@@ -77,9 +122,9 @@ for _n in PSUM:
     PLACE[_n] = (_n, 0, 512, F)
 
 MOVES = ["az%d" % t for t in range(RO)] + ["aw%d_%d" % (t, h) for t in range(RO) for h in range(2)]
-SEMAPHORES = (["cv", "cs", "cp", "cg"] + ["d%d" % i for i in range(NCH + OCH + 10)] + MOVES + ["l" + m for m in MOVES])
+SEMAPHORES = (["cv", "cs", "cp", "cg"] + ["d%d" % i for i in range(len(LOADS + STORES) + 11)] + MOVES + ["l" + m for m in MOVES])
 
-SAME = {x: x for x in ("XO", "WS", "WU", "VW", "WF")}
+SAME = dict({x: x for x in ("XO", "WS", "WU", "VW", "WF")}, M0="M", M1="M")
 
 A = AluOpType
 AF = ActivationFunctionType
@@ -104,9 +149,9 @@ def build(g, core, T, topo):
     def part(name, j):
         return view(T[name][:, :, 16 * j:16 * j + 16], 256, (name + str(j), 0, 16), False, False, name)
 
-    def col(name, b, k):
-        r = view(T[name][:, b, 0:16 * k], 16 * k, None, False, False, name)
-        r["rg"] = [(name + str(j), b, b + 1) for j in range(k)]
+    def col(name, b, j0, j1):
+        r = view(T[name][:, b, 16 * j0:16 * j1], 16 * (j1 - j0), None, False, False, name)
+        r["rg"] = [(name + str(j), b, b + 1) for j in range(j0, j1)]
         return r
 
     def ind(win, off):
@@ -129,9 +174,9 @@ def build(g, core, T, topo):
                     "lab": (q or "x") + SAME.get(lab[:2], lab) + phase[0], "rnd": rnd[0]})
 
     def cost(q, out, a, base):
-        fx = C["v"] if q == "v" else C["a"]
-        rate = C["s"] if out["ind"] else C["g"] if a["ind"] else base
-        return fx + max(20, a["n"] * rate) * C["cyc"]
+        if out["ind"] or a["ind"]:
+            return C[q] + a["n"] * C["out" if out["ind"] else "in"] * C["cyc"]
+        return C["fix"] + max(64, a["n"] * base) * C["cyc"]
 
     def ap(x):
         return x["ap"] if isinstance(x, dict) else x
@@ -160,7 +205,7 @@ def build(g, core, T, topo):
         add("v", lambda: V.transpose(ap(out), ap(a)), out, [a], cost("v", out, a, 1))
 
     def act(out, a, f=AF.Identity, scale=None, bias=None):
-        d = cost("s", out, a, 1)
+        d = cost("s", out, a, 1) * C["act"]
         if bias is not None:
             add("s", lambda: S.activation(ap(out), ap(a), f, bias=ap(bias), scale=scale), out, [a, bias], d)
         elif scale is not None:
@@ -193,7 +238,7 @@ def build(g, core, T, topo):
             add("g", lambda: g.iota(ap(out), pat, 0, cm), out, [], 130 + 1.7 * out["n"])
 
     def select(out, a, pat, op, fill):
-        add("g", lambda: g.affine_select(ap(out), ap(a), pat, op, fill, 0, 1), out, [a], 170 + 1.7 * out["n"])
+        add("g", lambda: g.affine_select(ap(out), ap(a), pat, op, fill, 0, 1), out, [a], 190 + 2 * C["cyc"] * out["n"])
 
     nd = [0]
 
@@ -210,16 +255,18 @@ def build(g, core, T, topo):
         m = sum(1 << e for e in eng)
         rid, pid, _ = topo.addr(dst)
         add("g", lambda: g.remote_dma(ap(out), ap(src), T.sem[sem], T.sem["l" + sem], pid, rid, m), None, [src],
-            C["rem"] + src["n"] * 5, "rem")
+            C["rem"] + src["n"] * 10, "rem")
         k = len(ops) - 1
         add(None, None, out, [], 0, "ext", sem, len(topo.engines(frm, core)[:8]))
         add(None, None, ext(None, "l" + sem), [], 0, "ext", "l" + sem, len(eng))
         ops[-1]["from"] = ops[-2]["from"] = k
 
-    cw = W // NCH
+    def blocks(sizes):
+        return [(sum(sizes[:c]), sum(sizes[:c + 1])) for c in range(len(sizes))]
+
     dma("s", v("WIN"), ext(T.w[:], "w"), 8192)
-    for c in range(NCH):
-        dma("y", v("NMI", c * cw, (c + 1) * cw), ext(T.nm[:, c * cw:(c + 1) * cw], "nm"), 512 * cw)
+    for a, b in blocks(LOADS):
+        dma("y", v("NMI", a, b), ext(T.nm[:, a:b], "nm"), 512 * (b - a))
     dma("s", v("Z0"), ext(T.z[:], "z"), 65536)
     dma("s", v("THI", 0, 1), ext(T.th[:], "th"), 4096)
     iota(v("PI"), [[1, 1]])
@@ -228,13 +275,13 @@ def build(g, core, T, topo):
     iota(v("C16"), [[16, 8]])
     dma("y", v("XB"), ext(T.x[:], "x"), 256 * W)
     bias = {}
-    for j, x in enumerate([-CM / 4096, NONE, HALF, 1, -0.5, 8224, 1 - NONE, 4096, HALF - BIG, -2, -HALF]):
+    for j, x in enumerate([-CM / 4096, NONE, HALF, 1, -0.5, 8224, 1 - NONE, 4096, -BIG, -2, -HALF]):
         ms(v("BI", j, j + 1), float(x))
         bias[x] = v("BI", j, j + 1)
     ms(v("SEL"), 1.0)
     ms(v("ONE"), 1.0)
     select(v("SEL"), v("SEL"), [[-1, 16], [-16, 8], [0, 16]], A.is_equal, 0.0)
-    select(v("PM32"), v("ONE", 0, 256), [[0, 2], [-1, 8], [-8, 16]], A.is_equal, 0.0)
+    select(v("PM"), v("ONE", 0, 256), [[0, 2], [-1, 8], [-8, 16]], A.is_equal, 0.0)
     pi = v("PI")
     pj = lambda j: v("PJ", j, j + 1)
     pf = lambda j: v("PF", j, j + 1)
@@ -247,8 +294,7 @@ def build(g, core, T, topo):
     ts(pj(6), pi, 1, None, A.bitwise_and)
     cp(v("PF", 0, 7), v("PJ", 0, 7))
     cp(pf(7), pi)
-    g16, acol, pcol, kcol, jcol = pf(0), pf(1), pf(7), pf(8), pf(9)
-    ts(kcol, pf(3), 128.0, None, A.mult)
+    g16, acol, pcol, jcol = pf(0), pf(1), pf(7), pf(9)
     ts(jcol, pf(3), -1.0, 15.0, A.mult, A.add)
     ts(pf(10), acol, float(W), None, A.add)
     ts(v("SP"), v("CI", 0, 4), float(WP), pf(10), A.mult, A.add)
@@ -266,15 +312,18 @@ def build(g, core, T, topo):
     for nm_, x in [("IDM", -1.0), ("ID32", 1.0), ("IM64", -64.0), ("I16K", 2 * BIG), ("IM8K", -BIG), ("I8K", BIG), ("IH", 2 / BIG),
                    ("IHM", -2 / BIG), ("I1536", float(HALF)), ("I2", 2.0)]:
         act(v(nm_), v("ID"), scale=x)
-    act(v("PMT"), v("PM32"), scale=2.0 ** 23)
-    act(v("P4K"), v("PM32", 0, 128), scale=4096.0)
-    act(v("P22"), v("PM32", 0, 128), scale=2.0 ** 22)
+    act(v("PMT"), v("PM"), scale=2.0 ** 23)
+    act(v("PMD"), v("PM"), scale=2048.0)
+    act(v("P4K"), v("PM", 0, 128), scale=4096.0)
+    act(v("P21"), v("PM", 0, 128), scale=2.0 ** 21)
     ts(v("CJ"), v("CI"), 15, None, A.bitwise_and)
+    ts(v("KC"), v("CJ", 0, 256), 128.0, None, A.mult)
+    ms(v("XB", NONE, W), FAR)
     ts(v("RST"), v("CJ", 0, 256), 0.0, 2.0 ** 25, A.is_equal, A.mult)
-    ts(v("RS0"), v("CJ", 0, 128), 0.0, None, A.not_equal)
+    act(v("RS0"), v("RST", 0, 128), scale=-1.0)
     ts(v("DG"), v("CJ"), acol, None, A.is_equal)
     act(v("CP"), v("DG"), scale=-BIG, bias=bias[4096])
-    act(v("CQ"), v("DG"), scale=BIG, bias=bias[HALF - BIG])
+    act(v("CQ"), v("DG"), scale=BIG, bias=bias[-BIG])
     sv = v("CI", 1, 9)
     ts(v("T2"), sv, acol, None, A.add)
     ts(v("T2"), v("T2"), 15, None, A.bitwise_and)
@@ -290,23 +339,21 @@ def build(g, core, T, topo):
     ts(v("KN", 0, 16), v("CI", 0, 16), 0.0, -4096.0, A.mult, A.add)
     ts(v("KN", 16, 32), v("CI", 0, 16), 0.0, float(HALF - NONE), A.mult, A.add)
     ms(v("NE"), 0.0)
-    for nm_ in TABLES[:3]:
+    for nm_ in TABLES:
         ms(v(nm_, W, WP), 0.0)
-    ms(v("M0", W, WP), 0.0)
-    for c in range(NCH):
-        a, b = c * cw, (c + 1) * cw
-        pd = v("PD%d" % (c % 2), 0, cw)
+    for c, (a, b) in enumerate(blocks((512,) * (W // 512))):
+        pd = v("PD%d" % (c % 2))
         ts(v("F1", a, b), v("NMI", a, b), -float(HALF), CM, A.add, A.add)
         act(v("M0", a, b), v("F1", a, b), scale=2.0 ** -12, bias=bias[-CM / 4096])
         act(pd, v("M0", a, b), scale=4096.0, bias=bias[NONE])
         tt(v("NT", a, b), pd, v("NMI", a, b), A.subtract)
-        act(v("M1", a, b), v("F1", a, b), scale=2.0 ** -12, bias=bias[-CM / 4096])
-    for nm_ in ("M0", "M1"):
-        ms(v(nm_, NONE, W), -1.0)
+    ms(v("M0", NONE, W), -1.0)
     cp(v("WU0"), v("WIN"))
-    cp(v("THF"), v("THI", 0, 1))
-    ts(v("THR"), v("THF"), 2048.0, None, A.mult)
-    dma("g", v("XT", 0, W), v("XB"), 512 * W)
+    ts(v("VW0", 0, 16), v("WIN"), -1.0, float(NONE - HALF), A.mult, A.add)
+    ts(v("THR"), v("THI", 0, 1), 2048.0, None, A.mult)
+    ts(v("TH2"), v("THI", 0, 1), 2048.0, None, A.mult)
+    for a, b in blocks((W // 6,) * 6):
+        select(v("XT", a, b), v("XB", a, b), [[0, b - a]], A.is_ge, 0.0)
 
     Nw = v("NT", 0, W)
     NP, EP = 16, 272
@@ -328,25 +375,39 @@ def build(g, core, T, topo):
     def hv(name, h, k=128):
         return v(name, k * h, k * h + k)
 
+    def copy(out, a):
+        select(out, a, [[0, a["n"]]], A.is_ge, 0.0)
+
+    def repeat(name, h):
+        for k in (128, 256):
+            copy(v(name, 512 * h + k, 512 * h + 2 * k), v(name, 512 * h, 512 * h + k))
+
+    def compare(out, win, off, name, h, wide):
+        for a, b in blocks(wide):
+            tt(v(out, 2048 * h + 128 * a, 2048 * h + 128 * b), ind(win, v(off, 128 * h + 8 * a, 128 * h + 8 * b)),
+               v(name, 512 * h, 512 * h + 128 * (b - a)), A.is_equal)
+
     def listen(t, h):
-        z, vw, pk = hv("Z%d" % t, h), "VW%d" % (t % 2), "PK%d" % h
+        z, vw, pk = hv("Z%d" % t, h), "VW%d" % t, "PK%d" % h
         wu, trn = hv("WU%d" % t, h, 8), "TR%d" % h
         Xw, Mw = v("XB") if t == 0 else v("XT", 0, W), v("M%d" % (t % 2), 0, W)
+        if t:
+            ts(wu, hv(vw, h, 8), -1.0, float(NONE - HALF), A.mult, A.add)
         act(v("NE", EP + 128 * h, EP + 128 * h + 128), ind(Mw, wu))
-        ts(hv(vw, h, 8), wu, -1.0, float(NONE - HALF), A.mult, A.add)
         spread("PS", 128 * h, hv(vw, h, 8))
-        for d in range(2):
-            act(hv("WB", 2 * h + d), hv("PS", h), scale=1.0, bias=bias[HALF])
+        act(hv("WB", 4 * h), hv("PS", h), scale=1.0, bias=bias[HALF])
+        repeat("WB", h)
         turn(EP + 128 * h, trn)
         cp(hv("OFF", h), ind(v(trn), v("TRK")))
-        for j in range(8 * h, 8 * h + 8):
-            tt(hv("EQ", j, 256), ind(Nw, hv("OFF", j, 16)), hv("WB", h, 256), A.is_equal)
-        ns = 4 - NV[h]
+        compare("EQ", Nw, "OFF", "WB", h, WIDE[h if t else 0])
+        ns = 4 - NV[t][h]
         for i in range(4 * h, 4 * h + 4):
             xg, ab, pd = hv("XG", i, 512), hv("AB", i, 512), "PD%d" % (i % 2)
             if i - 4 * h >= ns:
-                for k in range(4 * i, 4 * i + 4):
-                    tt(hv("XG", k), ind(Xw, hv("OFF", k, 8)), z, A.subtract)
+                if i - 4 * h == ns:
+                    copy(hv("ZR", 4 * h), z)
+                    repeat("ZR", h)
+                tt(xg, ind(Xw, hv("OFF", i, 32)), hv("ZR", h, 512), A.subtract)
                 act(ab, xg, AF.Abs)
                 continue
             if (i - 4 * h) % GW == 0:
@@ -360,10 +421,10 @@ def build(g, core, T, topo):
         reduce16("PE", 128 * h, "EQ", h)
         act(hv("TT", h), hv("PE", h), AF.Relu, -1.0, bias[1])
         reduce16("PR", 128 * h, "AB", h)
-        act(hv("DC", h), hv("PR", h), scale=2048.0, bias=kcol)
-        group((v(pk, 0, 256), hv("TT", h), v("PMT")), (v(pk, 0, 128), v("ID"), hv("HI", h)),
+        cp(hv("DC", h), hv("PR", h))
+        group((v(pk, 0, 256), v("ID"), v("KC")), (v(pk, 0, 128), v("ID"), hv("HI", h)),
               (v(pk, 128, 256), v("ID32"), hv("EF", h)), (v(pk, 128, 256), v("IM64"), hv("HI", h)),
-              (v(pk, 0, 256), hv("DC", h), v("PM32")))
+              (v(pk, 0, 256), hv("TT", h), v("PMT")), (v(pk, 0, 256), hv("DC", h), v("PMD")))
         scan(hv("SC", h, 256), v("RST"), v(pk, 0, 256), A.add, A.min)
         ts(hv("AN", h, 16), v("SC", 256 * h + 15, 256 * h + 256, 16), 127, None, A.bitwise_and)
         ts(hv("OH", h, 8), hv("AN", 2 * h, 8), 64.0, -32.0 - HALF, A.mult, A.add)
@@ -372,28 +433,25 @@ def build(g, core, T, topo):
         ts(hv(vw, 4 + h, 8), v("SC", 256 * h + 143, 256 * h + 256, 16), v("THR"), BIG, A.is_lt, A.mult)
 
     def speak(t, h):
-        vw, pk, trn, ou = "VW%d" % (t % 2), "PK%d" % h, "TS%d" % h, hv("OU", h, 8)
+        vw, trn, ou = "VW%d" % t, "TS%d" % h, hv("OU", h, 8)
         Xw, Mw = v("XB") if t == 0 else v("XT", 0, W), v("M%d" % (t % 2), 0, W)
         act(v("NE", NP + 128 * h, NP + 128 * h + 128), ind(Nw, ou))
         if h == 0:
             spread("PS", 256, v(vw, 16, 24))
-            for d in range(2):
-                act(hv("OB", d), hv("PS", 2), scale=1.0, bias=bias[HALF])
+            act(hv("OB", 0), hv("PS", 2), scale=1.0, bias=bias[HALF])
         else:
             mm(v("PD0"), v("I1536"), v("ONE"), True, False)
             spread("PD0", 0, v(vw, 16, 48), False, True)
             act(v("HB"), v("PD0", 256, 512), scale=1.0, bias=bias[-HALF])
-            for d in range(2):
-                act(hv("OB", 2 + d), hv("PD0", 1))
+            act(hv("OB", 4), hv("PD0", 1))
+        repeat("OB", h)
         act(hv("XO%d" % t, h), ind(Xw, ou))
         if h == 1:
             move(t, v("Z%d" % (t + 1)), v("XO%d" % t), "az%d" % t)
         turn(NP + 128 * h, trn)
         ts(hv("OF2", h), ind(v(trn), v("TRK")), -1.0, float(NONE), A.mult, A.add)
-        act(hv("UL", h), ind(v(trn), v("TRB")), scale=-1.0, bias=bias[NONE])
-        ts(hv("RS", h, 8), hv("WU%d" % t, h, 8), 2.0 ** 21, None, A.add)
-        for j in range(8 * h, 8 * h + 8):
-            tt(hv("EQ2", j, 256), ind(Mw, hv("OF2", j, 16)), hv("OB", h, 256), A.is_equal)
+        act(hv("UL", h), ind(v(trn), v("TRB")), scale=1.0, bias=bias[-HALF])
+        compare("EQ2", Mw, "OF2", "OB", h, WIDE[1])
         for i in range(4 * h, 4 * h + 4, GW):
             act(v("CN", 512 * i, 512 * (i + GW)), ind(Mw, v("OF2", 32 * i, 32 * (i + GW))), AF.Relu, 1.0, bias[1 - NONE])
 
@@ -401,92 +459,103 @@ def build(g, core, T, topo):
         reduce16("PR", 256 + 128 * h, "CN", h)
         act(hv("CB", h), hv("PR", 2 + h), scale=16.0, bias=jcol)
         reduce16("PE", 256 + 128 * h, "EQ2", h)
-        act(hv("SG", h), hv("PE", 2 + h), AF.Sign)
-        o = v("PK%d" % h, 384, 512)
-        group((o, v("ID32"), hv("UL", h)), (o, hv("CB", h), v("P4K")), (o, hv("SG", h), v("P22")))
-        scan(hv("SC2", h), v("RS0"), o, A.mult, A.max)
-        tt(hv("WI", h, 8), v("SC2", 128 * h + 15, 128 * h + 128, 16), hv("RS", h, 8), A.max)
-        ts(hv("WA", h, 8), hv("WI", h, 8), 4095, None, A.bitwise_and)
-        src, dst = ("WFS", "WF") if t == RO - 1 else ("WS%d" % t, "WU%d" % (t + 1))
-        cp(hv(src, h, 8), hv("WA", h, 8))
+        act(hv("SG", h), hv("PE", 2 + h), AF.Sign, 1.0, bias[-0.5])
+        o = v("PK1" if h else "PS", 384, 512)
+        group((o, v("ID32"), hv("UL", h)), (o, hv("CB", h), v("P4K")), (o, hv("SG", h), v("P21")))
+        scan(hv("SC2", h), v("RS0"), o, A.add, A.max)
+        tt(hv("WI", h, 8), v("SC2", 128 * h + 15, 128 * h + 128, 16), hv("VW%d" % t, h, 8), A.max)
+        ts(hv("WA", h, 8), hv("WI", h, 8), CM, CM, A.add, A.subtract)
+        src, dst = "WS%d" % t, "VW%d" % (t + 1)
+        tt(hv(src, h, 8), hv("WI", h, 8), hv("WA", h, 8), A.subtract)
+        if t == RO - 1:
+            ts(hv("WFS", h, 8), hv(src, h, 8), -1.0, float(NONE - HALF), A.mult, A.add)
+            src, dst = "WFS", "WF"
         move(t, hv(dst, h, 8), hv(src, h, 8), "aw%d_%d" % (t, h))
 
     def prepare(t):
         last = t == RO - 1
-        vw, z, xo = "VW%d" % (t % 2), v("Z%d" % t), v("XO%d" % t)
-        tabs = ["NT", "M%d" % (1 - t % 2)] + ([] if last else ["XT"])
-        low = min(TABLES.index(x) for x in tabs)
+        vw, z, xo = "VW%d" % t, v("Z%d" % t), v("XO%d" % t)
+        tabs = ["M%d" % (1 - t % 2)] + ([] if last else ["XT"]) + ["NT"]
         one = v("ONE", 0, 256)
         wo = v(vw, 0, 32)
         for s in range(8):
             mm(hv("PK0", s, 32), hv("CIR", s), wo)
         group((hv("PK0", 8, 32), v("ID"), wo), (hv("PK0", 8, 32), v("ID"), v("KN")))
         merge(10)
-        ts(v("EE"), v("PK0", 0, 288), 0.0, None, A.is_equal)
+        if EES and not last:
+            act(v("AE"), v("PK0", 0, 288), AF.Abs)
+            act(v("EE"), v("AE"), AF.Relu, -1.0, bias[1])
+        else:
+            ts(v("EE"), v("PK0", 0, 288), 0.0, None, A.is_equal)
         acc, aw, ao = hv("PK0", 9, 32), hv("PK0", 18, 16), hv("PK0", 19, 16)
         group(*[(acc, hv("RT", s), hv("EE", s, 32)) for s in range(8)], (acc, v("I8K"), hv("EE", 8, 32)),
               (aw, v("IDM"), v(vw, 0, 16)), (ao, v("ID"), v(vw, 16, 32)))
         merge(11)
         for j, x in enumerate(tabs):
-            at = TABLES.index(x) - low
-            ts(v("SO", j, 64, 4), aw if j == 1 else ao, float((NONE - HALF if j == 1 else HALF) + at * WP),
+            at = j // 2
+            ts(v("SO", j + min(j, 1), 64, 4), ao if j else aw, float((HALF if j else NONE - HALF) + at * WP),
                v("SP", at, at + 1), A.add, A.min)
         if not last:
             o, a = v("S1"), v("PK1", 256, 272)
             mm(a, v("ONE", 0, 128), v(vw, 32, 48))
-            add("v", lambda o=o, a=a: V.tensor_reduce(ap(o), ap(a), AxisListType.X, A.add), o, [a], 70)
-            ts(v("S2"), v("S1"), 1 / BIG, None, A.mult)
+            add("s", lambda o=o, a=a: S.activation(ap(v("JK")), ap(a), AF.Identity, scale=1 / BIG, accum_out=ap(o)), o, [a], 105)
+            ops[-1]["w"] += v("JK")["rg"]
+            cp(v("S2"), o)
             ts(v("S3"), v("S2"), 31, None, A.bitwise_and)
-            ts(v("THR"), v("S3"), v("THF"), 2048.0, A.add, A.mult)
+            ts(v("THR"), v("S3"), 2048.0, v("TH2"), A.mult, A.add)
         q, qw = v("PQ", 0, 256), v("PQ", 256, 512)
-        mm(qw, v("I1536"), one, True, False)
-        spread("PQ", 256, v(vw, 0, 16), False, True)
-        mm(q, v("ID"), v("CQ", t, t + 256), True, False)
-        spread("PQ", 0, v(vw, 0, 16), False, False)
-        tt(v("EW", 0, 256), v("NE", NP, NP + 256), qw, A.is_equal)
+        for j in range(2):
+            copy(hv("Q2", j, 16), v(vw, 0, 16))
+        mm(v("PQ"), v("I1536"), v("ONE"), True, False)
+        spread("PQ", 0, v("Q2"), False, False)
+        mm(q, v("ID"), v("CQ", t, t + 256), False, False)
         mm(q, v("IDM"), v("HB"), False, True)
-        p, hi, c = v("PD1", 0, 256), v("PD1", 256, 512), v("PD0", 0, 256)
+        tt(v("EW", 0, 256), v("NE", NP, NP + 256), qw, A.is_equal)
+        p, c = v("PQ", 256, 512), v("PD0", 0, 256)
         if not last:
-            group((qw, v("ID"), xo), (qw, v("IH"), v("HB")))
-            group((hi, v("ID"), xo), (hi, v("I2"), one), (hi, v("IHM"), v("HB")))
-        act(part("VB", 0), q, AF.Relu)
+            lo, hi = hv("PD1", 0, 256), hv("PD1", 1, 256)
+            group((hi, v("I2"), one), (hi, v("ID"), xo), (hi, v("IHM"), v("HB")))
+            group((lo, v("ID"), xo), (lo, v("IH"), v("HB")))
+            tt(part("VA", 1), z, hi, A.min)
+            act(part("VB", 1), lo, scale=1.0, bias=bias[-2])
         group((p, v("ID"), v("CP", t, t + 256)), (p, v("IDM"), v("HB")), (p, v("I16K"), v("EW", 0, 256)))
-        tt(part("VA", 0), v("NE", NP, NP + 256), p, A.min)
+        tt(part("VA", len(tabs) - 1), v("NE", NP, NP + 256), p, A.min)
+        act(part("VB", len(tabs) - 1), q, AF.Relu)
         tt(v("EW", 256, 512), v("NE", EP, EP + 256), c, A.is_equal)
         group((c, v("ID"), v("HB")), (c, v("IM8K"), v("EW", 256, 512)))
-        act(part("VB", 1), c, scale=NONE / BIG)
-        act(part("VA", 1), v("NE", EP, EP + 256))
-        if not last:
-            act(part("VB", 2), qw, scale=1.0, bias=bias[-2])
-            tt(part("VA", 2), z, hi, A.min)
-        k = len(tabs)
+        act(part("VB", 0), c, scale=NONE / BIG)
+        copy(part("VA", 0), v("NE", EP, EP + 256))
         for b in range(15, -1, -1):
-            tt(ind(v("TB", low * WP, (low + k) * WP), v("SO", 4 * b, 4 * b + k)), col("VA", b, k), col("VB", b, k), A.max)
+            k = len(tabs)
+            tt(ind(v(tabs[0]), v("SO", 4 * b, 4 * b + 1)), col("VA", b, 0, 1), col("VB", b, 0, 1), A.max)
+            tt(ind(v("TB", (4 - k) * WP, 3 * WP), v("SO", 4 * b + 2, 4 * b + 1 + k)), col("VA", b, 1, k), col("VB", b, 1, k), A.max)
 
     for t in range(RO):
         rnd[0] = t
         phase[0] = "c"
-        if t:
-            dma("y", v("M%d" % (1 - t % 2), 0, W), v("M%d" % (t % 2), 0, W), 512 * W, ext(None, "law%d_1" % (t - 1)))
-        if t == RO - 1:
-            ms(v("M0", NONE, W), float(NONE))
-        for name, f in (("l", listen), ("s", speak), ("w", None), ("e", choose)):
-            for h in range(2 if f else 0):
+        dma("y", v("M%d" % (1 - t % 2), 0, W), v("M%d" % (t % 2), 0, W), 512 * W,
+            ext(None, "law%d_1" % (t - 1)) if t else v("XB"))
+        for name, f in (("l", listen), ("s", speak)):
+            if t == RO - 1 and f is speak:
+                ms(v("XT", NONE, W), 255.0)
+            for h in range(2):
                 phase[0] = name + "AB"[h]
                 f(t, h)
-            if not f:
-                phase[0] = name
-                prepare(t)
+        phase[0] = "w"
+        prepare(t)
+        for h in range(2):
+            phase[0] = "e" + "AB"[h]
+            choose(t, h)
     phase[0] = "z"
-    ow = W // OCH
-    for c in range(OCH):
-        a, b = c * ow, (c + 1) * ow
-        pd = v("PD%d" % (c % 2), 0, ow)
+    for c, (a, b) in enumerate(blocks((256, 256) + (512,) * (W // 512 - 1))):
+        pd = v("PD%d" % (c % 2), 0, b - a)
         act(pd, v("M0", a, b), scale=4096.0, bias=bias[NONE])
         tt(v("F1", a, b), pd, v("NT", a, b), A.subtract)
-        dma("y", ext(T.ynm[:, a:b], "ynm", a, b), v("F1", a, b), 512 * ow)
-    dma("y", ext(T.yz[:], "yz"), v("Z%d" % RO), 65536)
-    dma("y", ext(T.yw[:], "yw"), v("WF"), 8192)
+    ms(v("F1", NONE, W), float(NONE + 4096 * NONE))
+    for a, b in blocks(STORES):
+        dma("y", ext(T.ynm[:, a:b], "ynm", a, b), v("F1", a, b), 512 * (b - a))
+    for name, src, size in (("yz", "Z%d" % RO, 65536), ("yw", "WF", 8192)):
+        dma("y", ext(T[name][:], name), v(src), size, v("F1", NONE, W))
     return ops
 
 
@@ -549,175 +618,149 @@ def one_pass(res, dur, nxt, npre, key, ready0):
     return start
 
 
-def improve(res, dur, succ, pred, r0, start, rng):
+def improve(res, dur, succ, npre, r0, key, mates, steps, heat, rng):
     n = len(res)
     line = {}
-    for i in sorted(range(n), key=lambda i: (start[i], i)):
+    for i in range(n):
         if res[i] is not None:
             line.setdefault(res[i], []).append(i)
-    npre = [len(p) for p in pred]
+
+    def place(i):
+        return key[i]
 
     def times():
-        nx, pv = [-1] * n, [-1] * n
-        left = list(npre)
+        nx, left = [-1] * n, list(npre)
         for l in line.values():
+            l.sort(key=place)
             for a, b in zip(l, l[1:]):
-                nx[a], pv[b] = b, a
+                nx[a] = b
                 left[b] += 1
-        head = list(r0)
+        head, by = list(r0), [-1] * n
         order = [i for i in range(n) if not left[i]]
+        end, last = 0.0, 0
         for i in order:
             e = head[i] + dur[i]
+            if e > end:
+                end, last = e, i
             for s, la in succ[i]:
                 if head[s] < e + la:
-                    head[s] = e + la
+                    head[s], by[s] = e + la, i
                 left[s] -= 1
                 if not left[s]:
                     order.append(s)
             s = nx[i]
             if s >= 0:
                 if head[s] < e:
-                    head[s] = e
+                    head[s], by[s] = e, i
                 left[s] -= 1
                 if not left[s]:
                     order.append(s)
-        tail = [0.0] * n
-        for i in reversed(order):
-            t = tail[nx[i]] if nx[i] >= 0 else 0.0
-            for s, la in succ[i]:
-                if t < tail[s] + la:
-                    t = tail[s] + la
-            tail[i] = t + dur[i]
-        return head, tail, nx, pv
+        if len(order) < n:
+            return None
+        pairs = []
+        while by[last] >= 0:
+            if nx[by[last]] == last and mates[last]:
+                pairs.append((by[last], last))
+            last = by[last]
+        return end, head, pairs, nx
 
-    def guess(seq, first, last, head, tail):
-        e = head[first] + dur[first] if first >= 0 else 0.0
-        hs = []
-        for x in seq:
-            h = max([e, r0[x]] + [head[p] + dur[p] + la for p, la in pred[x]])
-            hs.append(h)
-            e = h + dur[x]
-        t, m = tail[last] if last >= 0 else 0.0, 0.0
-        for x, h in zip(reversed(seq), reversed(hs)):
-            t = max([t] + [tail[s] + la for s, la in succ[x]]) + dur[x]
-            m = max(m, h + t)
-        return m
-
-    best, tabu, since = (1e18, None, None), {}, 0
-    for it in range(STEPS):
-        head, tail, nx, pv = times()
-        end = max(head[i] + tail[i] for i in range(n))
-        since += 1
-        if end < best[0] - 0.5:
-            best, since = (end, head, {q: list(l) for q, l in line.items()}), 0
-        elif since > 1500:
-            line.update({q: list(l) for q, l in best[2].items()})
-            tabu, since = {}, 0
-            continue
-        way = [i for i in range(n) if head[i] == r0[i] and head[i] + tail[i] >= end - 0.01]
-        i = way[int(rng.randint(len(way)))]
-        runs = [[i]]
-        while tail[i] > dur[i] + 0.01:
-            e = head[i] + dur[i]
-            nxt = [s for s, la in succ[i] if abs(tail[i] - dur[i] - la - tail[s]) < 0.01 and abs(head[s] - e - la) < 0.01]
-            s = nx[i]
-            if s >= 0 and abs(tail[i] - dur[i] - tail[s]) < 0.01 and abs(head[s] - e) < 0.01 and (not nxt or rng.rand() < 0.5):
-                runs[-1].append(s)
-            else:
-                s = nxt[int(rng.randint(len(nxt)))]
-                runs.append([s])
-            i = s
-        pick = None
-        for r in runs:
-            m = len(r)
-            pairs = {(a, m - 1) for a in range(max(0, m - 7), m - 1)} | {(0, b) for b in range(1, min(m, 7))}
-            if m > 3:
-                a = int(rng.randint(m - 1))
-                pairs.add((a, min(m - 1, a + 1 + int(rng.randint(4)))))
-            for a, b in sorted(pairs):
-                u, w = r[a], r[b]
-                for fwd in (True, False) if b > a + 1 else (True,):
-                    if fwd:
-                        if any(head[s] <= head[w] for s, _ in succ[u]):
-                            continue
-                        seq = r[a + 1:b + 1] + [u]
-                        bad = any(tabu.get((x, u), 0) > it for x in seq)
-                    else:
-                        if any(tail[p] <= tail[u] for p, _ in pred[w]):
-                            continue
-                        seq = [w] + r[a:b]
-                        bad = any(tabu.get((w, x), 0) > it for x in seq)
-                    val = guess(seq, pv[u], nx[w], head, tail)
-                    if bad and val >= best[0]:
-                        continue
-                    val += rng.rand() * 30
-                    if pick is None or val < pick[0]:
-                        pick = (val, u, w, seq, fwd)
-        if pick is None:
-            tabu = {}
-            continue
-        _, u, w, seq, fwd = pick
-        l = line[res[u]]
-        k = l.index(u)
-        l[k:k + len(seq)] = seq
-        for x in seq:
-            tabu[(u, x) if fwd else (x, w)] = it + 8 + int(rng.randint(12))
+    best = cur = times()
+    free = [i for i in range(n) if mates[i]]
+    for it in range(steps):
+        r = rng.rand(4)
+        if r[0] < 0.8 and cur[2]:
+            u, w = cur[2][int(r[1] * len(cur[2]))]
+        else:
+            u = free[int(r[1] * len(free))]
+            w = cur[3][u]
+            if w < 0:
+                continue
+        l = sorted(line[res[u]], key=place)
+        k, far = l.index(u), int(rng.geometric(0.45)) - 1
+        gaps = [a for a in range(max(1, k - 24), k + 1) if cur[1][l[a]] - cur[1][l[a - 1]] - dur[l[a - 1]] > 60]
+        if r[2] > 0.7 and gaps:
+            a = gaps[-1 - far % len(gaps)]
+            x, new = w, (key[l[a - 1]] + key[l[a]]) / 2
+        elif r[2] < 0.35:
+            a = min(len(l) - 1, k + 1 + far)
+            x, new = u, (key[l[a]] + (key[l[a + 1]] if a + 1 < len(l) else key[l[a]] + 100)) / 2
+        else:
+            a = max(0, k - far)
+            x, new = w, (key[l[a]] + (key[l[a - 1]] if a else key[l[a]] - 100)) / 2
+        d, old = new - key[x], [key[i] for i in mates[x]]
+        for i in mates[x]:
+            key[i] += d
+        got = times()
+        if got is not None and got[0] <= cur[0] - heat * (1 - it / steps) * np.log(r[3]):
+            cur = got
+            if got[0] < best[0]:
+                best = got
+        else:
+            for i, y in zip(mates[x], old):
+                key[i] = y
     return best[0], best[1]
 
 
 def schedule(ops):
     n = len(ops)
     res = ["D" if o["kind"] == "dma" else o["q"] for o in ops]
-    dur = [500 if o["kind"] == "rem" else o["dur"] for o in ops]
-    succ, pred = [[] for _ in ops], [[] for _ in ops]
+    dur = [C["hold"] if o["kind"] == "rem" else o["dur"] for o in ops]
+    dur[[o["kind"] for o in ops].index("rem")] += C["once"]
+    succ, pred, older = [[] for _ in ops], [[] for _ in ops], []
     for i, o in enumerate(ops):
+        las = {}
         for j, w in sorted(o["pre"].items()):
             p = ops[j]
             la = 1 if (p["q"] == "p" and o["q"] == "p") or not w else C["lat"]
             la += C["dma"] if o["kind"] == "dma" and w else 0
-            la += p["dur"] - 500 if p["kind"] == "rem" else 0
-            succ[j].append((i, la))
-            pred[i].append((j, la))
+            las[j] = la + (p["dur"] - C["hold"] if p["kind"] == "rem" else 0)
+        older.append({j for j in las if j < i}.union(*[older[j] for j in las if j < i]))
+        for j, la in las.items():
+            if not any(k < i and j in older[k] and la <= dur[k] + l2 for k, l2 in las.items()):
+                succ[j].append((i, la))
+                pred[i].append((j, la))
+    GRAPH[:] = [res, dur, succ, pred]
     npre = [len(p) for p in pred]
     r0 = [C["dma"] if res[i] == "D" else 0.0 for i in range(n)]
-
-    def forward(key):
-        st = one_pass(res, dur, succ, npre, key, r0)
-        end = max(st[i] + dur[i] for i in range(n))
-        return end + 0.5 * sum(st) / n, end, st
-
-    key0, groups, nth = [], {}, {}
+    where, nth, alike = {}, {}, {}
     for i, o in enumerate(ops):
         k = (o["lab"], o["rnd"])
-        j = nth.get(k, 0)
-        nth[k] = j + 1
-        groups.setdefault(o["lab"], {}).setdefault(j, []).append(i)
-        first, step = PLAN.get(o["lab"], (None, None))
-        if first is None or (step is None and j):
-            key0.append(max([key0[p] + dur[p] + la for p, la in pred[i]], default=r0[i]))
-        else:
-            key0.append(1000 * (START + PERIOD * o["rnd"] + first + j * (step or 0)))
-    groups = [list(x.values()) for x in groups.values()]
+        nth[k] = nth.get(k, -1) + 1
+        where[o["lab"], nth[k], o["rnd"]] = i
+    behind, left = [list(x) for x in succ], list(npre)
+    for q in ROUND:
+        row = []
+        for t in range(-1, RO):
+            for word in (LAST if t == RO - 1 else ROUND)[q].split():
+                lab, _, js = word.strip("+-").partition(":")
+                js = [int(j) for j in (js or "0").split("-")]
+                for j in range(js[0], js[-1] + 1):
+                    i = where.pop((q + lab, j, t + {"+": 1, "-": -1}.get(word[0], 0)), None)
+                    if i is not None:
+                        row.append(i)
+                        alike.setdefault((q + lab, j, t == RO - 1), []).append(i)
+        for a, b in zip(row, row[1:]):
+            behind[a].append((b, 0))
+            left[b] += 1
+    count, tail = list(left), [0.0] * n
+    order = [i for i in range(n) if not count[i]]
+    for i in order:
+        for s, _ in behind[i]:
+            count[s] -= 1
+            if not count[s]:
+                order.append(s)
+    assert len(order) == n, [ops[i]["lab"] for i in range(n) if count[i]][:12]
+    for i in reversed(order):
+        tail[i] = dur[i] + max([la + tail[s] for s, la in behind[i]], default=0.0)
+    start = one_pass(res, dur, behind, left, [-x for x in tail], r0)
     rng = np.random.RandomState(SEED)
-    best = cur = forward(key0)
-    for it in range(TRIES):
-        key = list(key0)
-        one = int(rng.randint(RO)) if rng.rand() < it / TRIES else -1
-        for _ in range(int(rng.randint(1, 3))):
-            grp = groups[int(rng.randint(len(groups)))]
-            a = int(rng.randint(len(grp))) if rng.rand() < 0.4 else 0
-            b = a + 1 + int(rng.randint(len(grp) - a)) if rng.rand() < 0.4 else len(grp)
-            d = float(rng.choice([-1, 1]) * rng.choice([150, 400, 1000, 2500]))
-            for l in grp[a:b]:
+    for steps, heat, rounds in STEPS:
+        mates = [[i] if rounds is None or ops[i]["rnd"] in rounds else [] for i in range(n)]
+        if rounds is None:
+            for l in alike.values():
                 for i in l:
-                    if one < 0 or ops[i]["rnd"] == one:
-                        key[i] += d
-        got = forward(key)
-        if got[0] <= cur[0] + HEAT * rng.rand() * (1 - it / TRIES):
-            cur, key0 = got, key
-            if got[1] < best[1]:
-                best = got
-    end, start = improve(res, dur, succ, pred, r0, best[2], rng)
+                    mates[i] = l
+        end, start = improve(res, dur, succ, npre, r0, list(start), mates, steps, heat, rng)
     order = sorted(range(n), key=lambda i: (start[i], i))
     first = [i for i in order if ops[i]["kind"] == "dma" and not any(ops[i]["pre"].values())]
     return first + [i for i in order if i not in set(first)], (end, order, start)
@@ -776,6 +819,7 @@ def emit(g, T, ops, order):
 
 
 ORDER = []
+GRAPH = []
 
 
 def rank_program(g, core, T, topo):

import numpy as np
from concourse.mybir import AluOpType, ActivationFunctionType, AxisListType

W, L, RO = 3072, 256, 4
NONE = W - 1
WP = W + 16
CM = 1.5 * 2 ** 35
HALF = 1536
BIG = 8192.0
LOADS = (512, 1024, 1024, 512)
STORES = (256, 768, 1024, 1024)
NV = ((1, 1), (1, 1), (1, 1), (1, 1))
WIDE = ((4, 4, 4, 4), (1, 1, 2, 4, 4, 4))
EES = True
FAR = 63.0
GW = 1
STEPS = ((55000, 100, None), (25000, 60, (3,)), (25000, 80, (0,)), (20000, 30, (0, 1, 2, 3)))
SEED = 0
C = {"cyc": 0.87, "in": 1.56, "out": 3.8, "tt": 2.0, "v": 53, "s": 68, "fix": 25, "act": 1.04, "pe": 0.5, "pf": 10, "lat": 110,
     "dma": 2500, "bw": 340.0, "rem": 2600, "hold": 700, "once": 3000}
ROUND = {
    "v": "OFFlA -NTw:14-15 XGlA:2-3 XGlA:1 EQlA:2-3 XGlA:0 WUlB EQlA:0 TR1lB:1 EQlA:1 TR1lB:0 OFFlB EQlB:0 EQlB:5 DClA EQlB:2 SClA ANlA VWlA:1 OHlA VWlA:0 OUlA EQlB:1 EQlB:3-4 TS0sA:0-1 OF2sA EQ2sA:1 EQ2sA:0 EQ2sA:2-4 DClB EQ2sA:5 SClB ANlB OHlB VWlB:1 VWlB:0 OUlB TS1sB:1 TS1sB:0 EWw:0 OF2sB EWw:1 EQ2sB:1 EQ2sB:0 EQ2sB:2 VAw:0 EQ2sB:4 SOw:0 EQ2sB:3 SOw:1 VAw:1 SOw:2 EQ2sB:5 TBw:0 SC2eA TBw:1 WIeA NTw:0 WAeA TBw:2 WSeA TBw:3 NTw:1 TBw:4 NTw:2 TBw:5 NTw:3 TBw:6 NTw:4 TBw:7-8 NTw:5 TBw:9 SC2eB TBw:10 WIeB NTw:6 TBw:11 NTw:7 TBw:12 WAeB NTw:8 WSeB TBw:13 NTw:9 TBw:14 NTw:10 TBw:15 NTw:11 +WUlA NTw:12-13 +TR0lA:1 +TR0lA:0",
    "s": "EFlA HIlA XGlA:0 XGlA:2 XGlA:1 ABlA:0 WBlB NElB ABlA:3 ABlA:1-2 EFlB XGlB:0 TTlA HIlB XGlB:1-3 ABlB:0 NEsA OBsA ABlB:1 XOsA ULsA ABlB:2-3 CNsA:3 TTlB CNsA:2 CNsA:0-1 NEsB XOsB S1w HBsB OBsB AEw EEw SGeA ULsB CNsB:0 VBw:0 CNsB:2 S2w VBw:2 CBeA S3w VBw:1 CNsB:3 CNsB:1 CBeB SGeB S4w THRw +NElA +WBlA",
    "p": "PK0lA:1 PK1lB:0 PK0lA:2-3 PD0lA:0 PSlB PD1lA PD0lA:1 PQw:1 PElA PRlA PK0lA:4-5 PD0lB:0 PQw:2 PK1lB:1 PD1lB:0 PSsA PQw:3 PK1lB:2 PD0lB:1 PD1lB:1 PElB PD1w:0 PRlB PK1lB:3 PD0sB:0 PK1lB:4 PSeA:0 PK1lB:5 PEeA PK1w PD0sB:1 PK0w:0 PD1w:1 PQw:4-6 PD1w:2-3 PD0w:0 PD1w:4 PQw:7 PK0w:1 PReA PD0w:1 PK1eB:0 PSeA:1 +PK0lA:0 PSeA:2 PEeB +PQw:0 PReB PK1eB:1-2 +PSlA",
    "g": "WBlA:0-1 WBlB:0-1 OBsA:0-1 VAw sendsB OBsB:0-1 sendeA sendeB",
}
LAST = {
    "v": "OFFlA -NTw:14-15 XGlA:0-3 EQlA:2 EQlA:0 WUlB EQlA:3 TR1lB:0-1 EQlA:1 OFFlB XGlB:0-3 EQlB:3 DClA EQlB:5 SClA EQlB:0 ANlA EQlB:2 OHlA VWlA:1 VWlA:0 EQlB:1 OUlA EQlB:4 TS0sA:1 TS0sA:0 OF2sA XTlB EQ2sA:2 EQ2sA:0 EQ2sA:4 DClB EQ2sA:3 SClB EQ2sA:1 ANlB OHlB VWlB:1 VWlB:0 OUlB EQ2sA:5 EWw:0 EEw TS1sB:0-1 EWw:1 OF2sB VAw SOw:0-1 EQ2sB:0-2 NTw:0 TBw:0 NTw:1 TBw:1 NTw:2 TBw:2 NTw:3 TBw:3 NTw:4 TBw:4 NTw:5 TBw:5 NTw:6 TBw:6 NTw:7 TBw:7 NTw:8 TBw:8 NTw:9 TBw:9 NTw:10 TBw:10 NTw:11 TBw:11 NTw:12 TBw:12 NTw:13 TBw:13 NTw:14 TBw:14 NTw:15 TBw:15 SC2eA F1z:0 WIeA F1z:1 EQ2sB:3 F1z:2 WAeA EQ2sB:4 WSeA F1z:3 EQ2sB:5 WFeA F1z:4-7 SC2eB WIeB WAeB WSeB WFeB",
    "s": "EFlA HIlA XGlA:1 XGlA:0 ABlA:3 NElB XGlA:2 ABlA:0 WBlB EFlB ABlA:1-2 XGlB:1 TTlA HIlB XGlB:0 XGlB:2 ABlB:1 ABlB:0 NEsA OBsA ABlB:3 ABlB:2 CNsA:0 TTlB CNsA:1 CNsA:3 XOsA NEsB ULsA HBsB OBsB XOsB VBw:0-1 CNsA:2 ULsB CNsB:0-1 CBeA SGeA CNsB:2-3 PD0z:0 PD1z:0 PD0z:1 CBeB PD1z:1 PD0z:2 PD1z:2 PD0z:3 SGeB",
    "p": "PK0lA:1-3 PSlB PD0lA:0 PD1lA PQw:1 PD0lA:1 PElA PRlA PQw:2 PK0lA:4-5 PD1lB PK1lB:1 PD0lB:0 PK1lB:2 PSsA PD0lB:1 PElB PK1lB:3 PRlB PD0sB:0 PK1lB:4-5 PQw:3 PD0sB:1 PK0w:0 PQw:4-7 PK0w:1 PD0w:0-1 PEeA PReA PSeA:0-2 PK1eB:0 PReB PEeB PK1eB:1-2",
    "g": "WBlA:0-1 WBlB:0-1 OBsA:0-1 OBsB:0-1 sendsB VAw sendeA sendeB",
}

ROUND = {
    "v": "OFFlA -NTw:14 XGlA:1 XGlA:0 XGlA:2 -NTw:15 XGlA:3 EQlA:0 WUlB EQlA:1 EQlA:3 EQlA:2 TR1lB:0-1 OFFlB XGlB:3 EQlB:2 EQlB:5 DClA XGlB:1-2 SClA EQlB:1 ANlA VWlA:1 OHlA XGlB:0 VWlA:0 EQlB:3 OUlA EQlB:0 EQlB:4 TS0sA:1 TS0sA:0 OF2sA EQ2sA:0-3 DClB EQ2sA:4 SClB ANlB OHlB VWlB:1 VWlB:0 OUlB EQ2sA:5 EWw:0 TS1sB:0-1 OF2sB EQ2sB:0-1 EWw:1 EQ2sB:2-4 SOw:0 VAw:0 SOw:1 EQ2sB:5 SOw:2 VAw:1 SC2eA WIeA TBw:0 WAeA TBw:1 WSeA TBw:2 NTw:0 TBw:3 NTw:1 TBw:4 NTw:2 TBw:5 NTw:3 TBw:6 NTw:4 TBw:7 NTw:5 TBw:8 NTw:6 TBw:9 SC2eB NTw:7 TBw:10 NTw:8 WIeB TBw:11 WAeB NTw:9 TBw:12 WSeB TBw:13 NTw:10 TBw:14 NTw:11 +WUlA TBw:15 NTw:12-13 +TR0lA:1 +TR0lA:0",
    "s": "EFlA HIlA XGlA:0 XGlA:2 XGlA:1 NElB ABlA:0 ABlA:3 WBlB ABlA:1-2 EFlB HIlB TTlA XGlB:0-2 ABlB:0-1 NEsA XOsA OBsA ABlB:3 ABlB:2 ULsA TTlB CNsA:1 CNsA:0 CNsA:3 CNsA:2 NEsB XOsB HBsB S1w OBsB ULsB AEw CNsB:2 EEw S2w CNsB:1 S3w CNsB:0 S4w VBw:0 CBeA SGeA VBw:2 VBw:1 CNsB:3 SGeB CBeB THRw +NElA +WBlA",
    "p": "PK0lA:1-3 PD0lA:0 PSlB PD1lA PD0lA:1 PElA PRlA PK0lA:4 PK1lB:1-2 PK0lA:5 PD0lB:0 PD1lB PSsA PK1lB:3 PD0lB:1 PElB PRlB PD0sB:0 PK1lB:4-5 PQw:1 PSeA:0 PQw:2 PD0sB:1 PD1w:0-1 PK1w PK0w:0 PD1w:2-3 PQw:3 PD1w:4 PEeA PD0w:0 PQw:4 PK0w:1 PReA PQw:5-6 PD0w:1 PSeA:1-2 PEeB PK1eB:0 +PK0lA:0 PReB +PQw:0 PK1eB:1-2 +PK1lB:0 +PSlA",
    "g": "WBlA:0-1 Mc:0-1 WBlB:0 Q2w:0 WBlB:1 Q2w:1 Mc:2-4 OBsA:0-1 Mc:5 VAw OBsB:0-1 sendsB sendeA sendeB",
}
LAST = {
    "v": "OFFlA -NTw:14-15 XGlA:0 XGlA:3 XGlA:2 XGlA:1 EQlA:2 EQlA:1 WUlB EQlA:0 EQlA:3 TR1lB:1 TR1lB:0 OFFlB XGlB:2 EQlB:1 XGlB:3 EQlB:5 DClA EQlB:4 SClA XGlB:0 ANlA EQlB:0 OHlA XGlB:1 VWlA:0 EQlB:2 OUlA EQlB:3 TS0sA:1 TS0sA:0 VWlA:1 OF2sA XTlB EQ2sA:0-3 DClB EQ2sA:4 SClB ANlB VWlB:1 OHlB VWlB:0 OUlB EQ2sA:5 EWw:0 TS1sB:1 TS1sB:0 OF2sB EEw EWw:1 VAw EQ2sB:2 SOw:0 EQ2sB:1 SOw:1 EQ2sB:0 NTw:0 TBw:0 NTw:1 TBw:1 NTw:2 TBw:2 NTw:3 TBw:3 NTw:4 TBw:4 NTw:5 TBw:5 NTw:6 TBw:6 NTw:7 TBw:7 NTw:8 TBw:8 NTw:9 TBw:9 NTw:10 TBw:10 NTw:11 TBw:11 NTw:12 TBw:12 NTw:13 TBw:13 NTw:14 TBw:14 NTw:15 TBw:15 EQ2sB:5 F1z:0 SC2eA F1z:1 WIeA WAeA F1z:2 EQ2sB:3 F1z:3-4 EQ2sB:4 F1z:5 WSeA F1z:6 WFeA F1z:7 SC2eB WIeB WAeB WSeB WFeB",
    "s": "EFlA HIlA XGlA:1 XGlA:0 XGlA:2 ABlA:1 ABlA:0 NElB WBlB ABlA:3 ABlA:2 EFlB HIlB XGlB:1 TTlA XGlB:0 XGlB:2 ABlB:1 ABlB:0 NEsA OBsA ABlB:3 ABlB:2 CNsA:2 ULsA TTlB CNsA:3 CNsA:0-1 NEsB XOsB HBsB OBsB CNsB:3 XOsA VBw:0-1 CNsB:0 CBeA CNsB:1 SGeA ULsB CNsB:2 PD0z:0 PD1z:0 PD0z:1 PD1z:1 PD0z:2 CBeB PD1z:2 PD0z:3 SGeB",
    "p": "PK0lA:1-3 PD1lA PD0lA:0 PSlB PD0lA:1 PElA PRlA PK1lB:1-2 PK0lA:4-5 PD1lB PK1lB:3 PD0lB:0 PSsA PD0lB:1 PElB PRlB PK1lB:4-5 PQw:1 PD0sB:0 PQw:2 PD0sB:1 PK0w:0 PQw:3-6 PK0w:1 PD0w:0-1 PSeA:0 PReA PEeA PSeA:1 PReB PK1eB:0 PSeA:2 PK1eB:1 PEeB PK1eB:2",
    "g": "WBlA:0-1 Mc:0-1 WBlB:0-1 Q2w:0-1 Mc:2-4 OBsA:0-1 Mc:5 VAw OBsB:0-1 sendsB sendeA sendeB",
}

ROUND = {
    "v": "OFFlA -NTw:13 XGlA:3 XGlA:2 -NTw:14 XGlA:0 -NTw:15 EQlA:1 WUlB XGlA:1 EQlA:3 EQlA:2 TR1lB:1 TR1lB:0 EQlA:0 OFFlB EQlB:5 EQlB:4 EQlB:2 EQlB:1 DClA EQlB:0 SClA ANlA OHlA VWlA:0-1 OUlA EQlB:3 TS0sA:1 TS0sA:0 OF2sA EQ2sA:2 EQ2sA:0 EQ2sA:4 DClB EQ2sA:3 SClB ANlB VWlB:1 OHlB VWlB:0 EQ2sA:1 OUlB EQ2sA:5 TS1sB:1 TS1sB:0 EWw:1 OF2sB EWw:0 EQ2sB:2 EQ2sB:1 EQ2sB:4 EQ2sB:3 VAw:0 SOw:0 EQ2sB:0 SOw:1 SC2eA EQ2sB:5 SOw:2 VAw:1 WIeA TBw:0 WAeA TBw:1 WSeA TBw:2 NTw:0 TBw:3 NTw:1 TBw:4 NTw:2 TBw:5 NTw:3 TBw:6 NTw:4 TBw:7 NTw:5 TBw:8 NTw:6 TBw:9 NTw:7 TBw:10 SC2eB TBw:11 NTw:8 TBw:12 WIeB +WUlA TBw:13 NTw:9 TBw:14 WAeB TBw:15 WSeB NTw:10-11 +TR0lA:0-1 NTw:12",
    "s": "EFlA HIlA XGlA:0-2 NElB WBlB ABlA:0 ABlA:3 ABlA:1 EFlB ABlA:2 HIlB XGlB:0-1 TTlA XGlB:2 ABlB:0 XGlB:3 ABlB:1 NEsA OBsA ABlB:2-3 CNsA:3 TTlB ULsA CNsA:1 CNsA:0 CNsA:2 NEsB HBsB OBsB XOsA ULsB XOsB CNsB:2 AEw EEw SGeA CBeA S1w CNsB:0 S2w S3w VBw:0 S4w THRw VBw:2 CNsB:1 VBw:1 CNsB:3 SGeB CBeB +NElA +WBlA",
    "p": "PK0lA:1 PD0lA:0 PSlB PK0lA:2 PD1lA PK0lA:3 PD0lA:1 PQw:1-2 PElA PRlA PD0lB:0 PD1lB:0 PK0lA:4-5 PK1lB:1-2 PD0lB:1 PSsA PD1lB:1 PElB PRlB PK1lB:3 PD0sB:0 PD1w:0 PK1lB:4 PSeA:0 PK1lB:5 PD0sB:1 PK0w:0 PQw:3 PK1w PEeA PD1w:1 PD0w:0 PQw:4 PReA PD1w:2 PD0w:1 PD1w:3-4 PK0w:1 PQw:5-6 PSeA:1-2 +PK0lA:0 PK1eB:0 +PQw:0 PEeB PReB PK1eB:1-2 +PSlA +PK1lB:0",
    "g": "WBlA:1 Q2w:0-1 WBlB:0-1 Mc:5 Mc:1 Mc:0 OBsA:0-1 VAw Mc:4 Mc:3 Mc:2 OBsB:0-1 sendsB sendeA sendeB +WBlA:0",
}
ROUND = {
    "v": "OFFlA -NTw:15 XGlA:1 XGlA:3 XGlA:0 WUlB EQlA:3 EQlA:2 XGlA:2 TR1lB:0-1 EQlA:0 OFFlB EQlA:1 EQlB:4 EQlB:1 XGlB:3 EQlB:2 DClA EQlB:5 XGlB:2 XGlB:1 SClA XGlB:0 ANlA VWlA:1 OHlA VWlA:0 EQlB:0 OUlA EQlB:3 TS0sA:0-1 OF2sA EQ2sA:2 EQ2sA:1 EQ2sA:3 DClB EQ2sA:4 SClB EQ2sA:0 ANlB VWlB:1 OHlB VWlB:0 OUlB EQ2sA:5 TS1sB:0-1 OF2sB EWw:0 EQ2sB:0-2 EWw:1 EQ2sB:4 SOw:0 VAw:0 SOw:1 EQ2sB:5 SOw:2 VAw:1 EQ2sB:3 TBw:0 SC2eA TBw:1 NTw:0 WIeA TBw:2 WAeA TBw:3 WSeA NTw:1 TBw:4 NTw:2 TBw:5 NTw:3 TBw:6 NTw:4 TBw:7 NTw:5 SC2eB TBw:8 WIeB NTw:6 TBw:9 NTw:7 WAeB TBw:10 NTw:8 WSeB TBw:11 NTw:9 TBw:12 NTw:10 TBw:13 NTw:11 TBw:14 +WUlA TBw:15 NTw:12-13 +TR0lA:0-1 NTw:14",
    "s": "EFlA HIlA XGlA:0 NElB XGlA:2 WBlB ABlA:0 XGlA:1 EFlB ABlA:3 ABlA:2 ABlA:1 HIlB XGlB:0 TTlA XGlB:2 XGlB:1 ABlB:0 ABlB:3 ABlB:1 NEsA OBsA XOsA ULsA ABlB:2 CNsA:0 TTlB CNsA:2 CNsA:1 CNsA:3 NEsB S1w XOsB HBsB S2w OBsB AEw CNsB:0 EEw S3w CNsB:1 CBeA S4w ULsB SGeA VBw:0 CNsB:2 THRw VBw:2 VBw:1 CNsB:3 SGeB CBeB +NElA +WBlA",
    "p": "PK0lA:1 PQw:0 PSlB PD0lA:0 PK0lA:2 PD0lA:1 PK0lA:3 PD1lA PElA PRlA PK1lB:1 PK0lA:4 PK1lB:2 PK0lA:5 PK1lB:3 PD0lB:0 PD1lB PSsA PD0lB:1 PElB PRlB PD1w:0 PK1lB:4 PSeA:0 PK1lB:5 PQw:1 PD0sB:0 PQw:2 PK1w PD0sB:1 PK0w:0 PQw:3 PD1w:1-2 PQw:4 PReA PD1w:3-4 PK0w:1 PEeA PD0w:0-1 PQw:5-6 PSeA:1 PK1eB:0 +PK0lA:0 PSeA:2 PEeB PReB PK1eB:1-2 +PSlA +PK1lB:0",
    "g": "WBlA:1 Q2w:1 Mc:4 WBlB:0-1 Q2w:0 Mc:3 VAw Mc:1 Mc:5 OBsA:0-1 Mc:2 Mc:0 OBsB:0-1 sendsB sendeA sendeB +WBlA:0",
}
ROUND["v"] = "OFFlA XGlA EQlA:2 WUlB EQlA:3 TR1lB:1 EQlA:0 TR1lB:0 EQlA:1 OFFlB XGlB EQlB:1 EQlB:4 DClA EQlB:2 SClA ANlA VWlA:1 OHlA VWlA:0 OUlA EQlB:5 TS0sA:1 TS0sA:0 EQlB:0 OF2sA EQlB:3 EQ2sA:1-2 EQ2sA:0 EQ2sA:4 DClB EQ2sA:3 SClB ANlB OHlB VWlB:1 VWlB:0 OUlB EQ2sA:5 TS1sB:0-1 OF2sB EWw:1 EQ2sB:1 EQ2sB:0 EWw:0 EQ2sB:2 VAw:0 S2w SOw:0 EQ2sB:5 SOw:1 VAw:1 EQ2sB:4 SOw:2 S3w EQ2sB:3 Mw:0 TBw:0 SC2eA TBw:1 Mw:1 WIeA TBw:2 WAeA Mw:2 TBw:3 Mw:3 WSeA TBw:4 Mw:4 TBw:5 Mw:5 TBw:6 Mw:6 TBw:7 Mw:7 TBw:8 Mw:8 TBw:9 Mw:9 TBw:10 Mw:10 SC2eB Mw:11 TBw:11 WIeB Mw:12 WAeB Mw:13 TBw:12 Mw:14 +WUlA WSeB Mw:15 TBw:13 THRw TBw:14 +TR0lA:0-1 TBw:15"
ROUND["v"] = "OFFlA XGlA WUlB TR1lB:1 TR1lB:0 EQlA:0 OFFlB EQlA:2-3 EQlA:1 XGlB EQlB:4 EQlB:1 DClA EQlB:2 SClA ANlA OHlA VWlA:1 VWlA:0 OUlA EQlB:0 EQlB:5 TS0sA:0-1 EQlB:3 OF2sA EQ2sA:1 EQ2sA:0 EQ2sA:3-4 DClB EQ2sA:2 SClB ANlB VWlB:1 OHlB VWlB:0 OUlB EQ2sA:5 S2w TS1sB:0 S3w TS1sB:1 EWw:1 OF2sB EWw:0 EQ2sB:1-3 EQ2sB:0 VAw:0 EQ2sB:5 SOw:0 SC2eA SOw:1 VAw:1 SOw:2 EQ2sB:4 WIeA TBw:0 WAeA Mw:0 TBw:1 Mw:1 WSeA TBw:2 Mw:2 TBw:3 Mw:3 TBw:4 Mw:4 TBw:5 Mw:5 TBw:6 Mw:6 TBw:7 Mw:7 SC2eB Mw:8 TBw:8 WIeB Mw:9 WAeB Mw:10 TBw:9 Mw:11 WSeB TBw:10 Mw:12 TBw:11 Mw:13 +WUlA Mw:14 TBw:12 Mw:15 TBw:13 THRw TBw:14 +TR0lA:1 +TR0lA:0 TBw:15"
ROUND["s"] = "HIlA XGlA:0 NElB ABlA:3 WBlB XGlA:1-2 ABlA:0 EFlB ABlA:1 HIlB ABlA:2 XGlB:0 TTlA XGlB:1-2 ABlB:0 NEsA XOsA ABlB:1 OBsA ULsA ABlB:3 ABlB:2 CNsA:2 TTlB CNsA:1 CNsA:3 CNsA:0 S1w XOsB NEsB HBsB OBsB ULsB AEw CNsB:2 EEw CBeA CNsB:0 SGeA VBw:0 CNsB:1 VBw:2 VBw:1 CNsB:3 CBeB SGeB +WBlA +NElA +EFlA"
ROUND["p"] = "PSlB PK1lB:0 PK0lA:1-2 PD0lA:0 PQw:1 PK0lA:3 PD1lA PQw:2 PD0lA:1 PElA PK1lB:1 PRlA PK1lB:2 PK0lA:4-5 PD0lB:0 PD1lB PSsA PD0lB:1 PSeA:0 PD1w:0 PElB PRlB PD0sB:0 PK1lB:3-5 PK1w PD0sB:1 PK0w:0 PD1w:1 PQw:3 PD1w:2 PReA PQw:4 PD1w:3 PEeA PD1w:4 PK0w:1 PSeA:1 PD0w:0-1 PK1eB:0 PSeA:2 PQw:5-6 +PQw:0 PEeB PReB +PK0lA:0 PK1eB:1-2 +PSlA"
ROUND["g"] = "WBlA:1 ZRlB:0-2 WBlB:0-1 Q2w:0-1 VAw OBsA:0-1 OBsB:0-1 sendsB sendeA +ZRlA:0-2 sendeB +WBlA:0"
LAST["v"] = LAST["v"].replace("-NTw:14-15 ", "").replace("TBw", "Mw").replace("NTw", "TBw")
LAST["v"] = LAST["v"][:LAST["v"].index("EQ2sA:5 EWw:0")] + (
    "EQ2sA:5 TS1sB:0-1 EWw:1 OF2sB EEw EQ2sB:0-2 EWw:0 EQ2sB:3 VAw SOw:0-1 EQ2sB:4 SC2eA EQ2sB:5 WIeA "
    + " ".join("TBw:%d Mw:%d" % (j, j) + {0: " WAeA", 1: " WSeA", 2: " WFeA", 8: " SC2eB", 9: " WIeB", 10: " WAeB", 11: " WSeB",
                                          12: " WFeB"}.get(j, "") for j in range(16)) + " F1z:0-7")
LAST["s"] = LAST["s"][:LAST["s"].index("NEsB XOsB")] + (
    "NEsB HBsB OBsB XOsA XOsB ULsB CNsB:0-1 CBeA SGeA VBw:0-1 CNsB:2-3 CBeB SGeB PD0z:0 PD1z:0 PD0z:1 PD1z:1 PD0z:2 PD1z:2 PD0z:3")
LAST["p"] = ""
LAST["g"] = "WBlA:1 ZRlB:0-2 WBlB:0-1 Q2w:0-1 OBsA:0-1 VAw OBsB:0-1 sendsB sendeA sendeB"

F, B, H, I32, U16 = "float32", "bfloat16", "float16", "int32", "uint16"
SIZE = {F: 4, B: 2, H: 2, I32: 4, U16: 2}
SCRATCH = {}
PLACE = {}


def _own(name, cols, d):
    SCRATCH[name] = ("sbuf", [128, cols], d)
    PLACE[name] = (name, 0, cols, d)


def _pool(name, cols, d):
    p = "pool_" + d
    at = SCRATCH[p][1][1] if p in SCRATCH else 0
    SCRATCH[p] = ("sbuf", [128, at + (cols + 15) // 16 * 16], d)
    PLACE[name] = (p, at, cols, d)


for _n, _c, _d in [("NMI", W, I32), ("F1", W, F), ("TB", 4 * WP, F), ("XB", W, B),
                   ("XG", 4096, B), ("AB", 4096, B), ("EQ", 4096, B), ("EQ2", 4096, B), ("CN", 4096, B),
                   ("WIN", 16, I32), ("THI", 16, I32), ("WF", 16, F), ("WFS", 16, F)]:
    _own(_n, _c, _d)
TABLES = ("M1", "XT", "NT", "M0")
for _j, _n in enumerate(TABLES):
    PLACE[_n] = ("TB", _j * WP, WP, F)
for _n in ("VA", "VB"):
    SCRATCH[_n] = ("sbuf", [128, 16, 48], F)
for _t in range(RO + 1):
    _own("Z%d" % _t, 256, B)
for _t in range(RO):
    _own("WU%d" % _t, 16, U16)
    _own("XO%d" % _t, 256, B)
    _own("WS%d" % _t, 16, H)
    _own("VW%d" % _t, 48, H)
for _d, _l in [
    (F, "NE 544 TR0 288 TR1 288 TS0 288 TS1 288 WB 1024 OB 1024 EF 256 UL 256 SC2 256 WI 16 WA 16 JK 16 SP 4 OH 16 RST 256 "
        "RS0 128 DG 272 ID32 128 TH2 1 THR 1 S1 1 PF 16 BI 16 T3 8 T4 8 T5 8 SHT 8 RTT 8"),
    (B, "HI 256 TT 256 CB 256 SG 256 EW 512 EE 288 HB 256 SEL 2048 ONE 512 CIB 128 ID 128 IDM 128 IM64 128 I16K 128 "
        "IM8K 128 I8K 128 IH 128 IHM 128 I1536 128 I2 128 ZR 1024 AE 288 KC 256 PM 256 PMD 256 PMT 256 P4K 128 P21 128 GS 8 CP 272 CQ 272 CIR 1024 RT 1024"),
    (H, "KN 32 Q2 32 DC 256"),
    (I32, "SC 512 AN 32 S2 1 S3 1 PI 1 PJ 8 CI 272 CJ 272 C16 8 T1 8 T2 8"),
    (U16, "OFF 256 OF2 256 OU 16 SO 64 TRK 8 TRB 8"),
]:
    for _n, _c in zip(_l.split()[0::2], _l.split()[1::2]):
        _pool(_n, int(_c), _d)
PSUM = ("PD0", "PD1", "PR", "PE", "PK0", "PK1", "PS", "PQ")
for _n in PSUM:
    SCRATCH[_n] = ("psum", [128, 512], F)
    PLACE[_n] = (_n, 0, 512, F)

MOVES = ["az%d" % t for t in range(RO)] + ["aw%d_%d" % (t, h) for t in range(RO) for h in range(2)]
SEMAPHORES = (["cv", "cs", "cp", "cg"] + ["d%d" % i for i in range(len(LOADS + STORES) + 11)] + MOVES + ["l" + m for m in MOVES])

SAME = dict({x: x for x in ("XO", "WS", "WU", "VW", "WF")}, M0="M", M1="M")

A = AluOpType
AF = ActivationFunctionType


def build(g, core, T, topo):
    ops = []
    rank = T.rank_of(core)
    n = len(T.cores)
    V, S, P = g.vector, g.scalar, g.tensor
    phase, rnd = ["0"], [0]

    def view(ap_, cols, rg, two, ps, lab):
        return {"ap": ap_, "n": cols, "rg": [rg], "two": two, "ps": ps, "ind": False, "off": [], "lab": lab}

    def v(name, a=0, b=None, s=1):
        buf, at, cols, d = PLACE[name]
        b = cols if b is None else b
        ap_ = T[buf][:, at + a:at + b] if s == 1 else T[buf][:, at + a:at + b:s]
        return view(ap_, len(range(a, b, s)), (buf, at + a, at + b), SIZE[d] == 2, buf in PSUM, name)

    def part(name, j):
        return view(T[name][:, :, 16 * j:16 * j + 16], 256, (name + str(j), 0, 16), False, False, name)

    def col(name, b, j0, j1):
        r = view(T[name][:, b, 16 * j0:16 * j1], 16 * (j1 - j0), None, False, False, name)
        r["rg"] = [(name + str(j), b, b + 1) for j in range(j0, j1)]
        return r

    def ind(win, off):
        return {"ap": win["ap"].indirect(off["ap"]), "n": 16 * off["n"], "rg": win["rg"], "off": off["rg"], "two": False,
                "ps": False, "ind": True, "lab": win["lab"]}

    def ext(ap_, key, a=0, b=1):
        return {"ap": ap_, "n": b - a, "rg": [(key, a, b)], "off": [], "ind": False, "lab": key}

    def add(q, fn, out, ins, dur, kind="c", sem=None, cnt=0):
        r, w = [], []
        for x in ins:
            if isinstance(x, dict):
                r += x["rg"] + x["off"]
        if out is not None:
            w += out["rg"]
            r += out["off"]
        lab = out["lab"] if out else "send"
        ops.append({"q": q, "fn": fn, "r": r, "w": w, "kind": kind, "sem": sem, "cnt": cnt, "dur": dur,
                    "lab": (q or "x") + SAME.get(lab[:2], lab) + phase[0], "rnd": rnd[0]})

    def cost(q, out, a, base):
        if out["ind"] or a["ind"]:
            return C[q] + a["n"] * C["out" if out["ind"] else "in"] * C["cyc"]
        return C["fix"] + max(64, a["n"] * base) * C["cyc"]

    def ap(x):
        return x["ap"] if isinstance(x, dict) else x

    def ts(out, a, s1, s2, o0, o1=None):
        d = cost("v", out, a, 0.5 if out["two"] and a["two"] else 1)
        if o1 is None:
            add("v", lambda: V.tensor_scalar(ap(out), ap(a), ap(s1), None, o0), out, [a, s1], d)
        else:
            add("v", lambda: V.tensor_scalar(ap(out), ap(a), ap(s1), ap(s2), o0, o1), out, [a, s1, s2], d)

    def tt(out, a, b, op):
        add("v", lambda: V.tensor_tensor(ap(out), ap(a), ap(b), op), out, [a, b],
            cost("v", out, a, 1 if a["ps"] or b["ps"] else C["tt"]))

    def cp(out, a):
        add("v", lambda: V.tensor_copy(ap(out), ap(a)), out, [a], cost("v", out, a, 0.5 if out["two"] and a["two"] else 1))

    def ms(out, c):
        add("v", lambda: V.memset(ap(out), c), out, [], cost("v", out, out, 0.5 if out["two"] else 1))

    def scan(out, a, b, o0, o1):
        add("v", lambda: V.tensor_tensor_scan(ap(out), ap(a), ap(b), 0.0, o0, o1), out, [a, b], cost("v", out, a, 1))

    def tr(out, a):
        add("v", lambda: V.transpose(ap(out), ap(a)), out, [a], cost("v", out, a, 1))

    def act(out, a, f=AF.Identity, scale=None, bias=None):
        d = cost("s", out, a, 1) * C["act"]
        if bias is not None:
            add("s", lambda: S.activation(ap(out), ap(a), f, bias=ap(bias), scale=scale), out, [a, bias], d)
        elif scale is not None:
            add("s", lambda: S.activation(ap(out), ap(a), f, scale=scale), out, [a], d)
        else:
            add("s", lambda: S.activation(ap(out), ap(a), f), out, [a], d)

    def mm(out, lt, rhs, st=True, sp=True):
        add("p", lambda: P.matmul(ap(out), ap(lt), ap(rhs), st, sp), out, [lt, rhs],
            C["pf"] + max(64, rhs["n"]) * C["pe"] * (1 if rhs["two"] else 4))

    def group(*terms):
        for j, (o, lt, rhs) in enumerate(terms):
            mm(o, lt, rhs, j == 0, j == len(terms) - 1)

    def merge(k):
        l = ops[-k:]
        del ops[-k:]
        fns = [o["fn"] for o in l]
        o = dict(l[0])
        o.update({"fn": lambda: [f() for f in fns][-1], "r": [x for y in l for x in y["r"]],
                  "w": [x for y in l for x in y["w"]], "dur": sum(y["dur"] for y in l)})
        ops.append(o)

    def iota(out, pat):
        cm = 1 if out["n"] == 1 else 0
        if out["two"]:
            add("g", lambda: g.iota(ap(out), pat, 0, cm, allow_small_or_imprecise_dtypes=True), out, [], 130 + 1.7 * out["n"])
        else:
            add("g", lambda: g.iota(ap(out), pat, 0, cm), out, [], 130 + 1.7 * out["n"])

    def select(out, a, pat, op, fill):
        add("g", lambda: g.affine_select(ap(out), ap(a), pat, op, fill, 0, 1), out, [a], 190 + 2 * C["cyc"] * out["n"])

    nd = [0]

    def dma(q, out, src, nbytes, after=None):
        s = "d%d" % nd[0]
        nd[0] += 1
        e = {"y": g.sync, "s": g.scalar, "g": g}[q]
        add(q, lambda: e.dma_start(ap(out), ap(src)), out, [src, after], nbytes / C["bw"], "dma", s, 16)

    def move(t, out, src, sem):
        dst = T.cores[(rank + 1 + t % (n - 1)) % n]
        frm = T.cores[(rank - 1 - t % (n - 1)) % n]
        eng = topo.engines(core, dst)[:8]
        m = sum(1 << e for e in eng)
        rid, pid, _ = topo.addr(dst)
        add("g", lambda: g.remote_dma(ap(out), ap(src), T.sem[sem], T.sem["l" + sem], pid, rid, m), None, [src],
            C["rem"] + src["n"] * 10, "rem")
        k = len(ops) - 1
        add(None, None, out, [], 0, "ext", sem, len(topo.engines(frm, core)[:8]))
        add(None, None, ext(None, "l" + sem), [], 0, "ext", "l" + sem, len(eng))
        ops[-1]["from"] = ops[-2]["from"] = k

    def blocks(sizes):
        return [(sum(sizes[:c]), sum(sizes[:c + 1])) for c in range(len(sizes))]

    dma("s", v("WIN"), ext(T.w[:], "w"), 8192)
    for a, b in blocks(LOADS):
        dma("y", v("NMI", a, b), ext(T.nm[:, a:b], "nm"), 512 * (b - a))
    dma("s", v("Z0"), ext(T.z[:], "z"), 65536)
    dma("s", v("THI", 0, 1), ext(T.th[:], "th"), 4096)
    iota(v("PI"), [[1, 1]])
    iota(v("CI"), [[1, 272]])
    iota(v("CIB"), [[1, 128]])
    iota(v("C16"), [[16, 8]])
    dma("y", v("XB"), ext(T.x[:], "x"), 256 * W)
    bias = {}
    for j, x in enumerate([-CM / 4096, NONE, HALF, 1, -0.5, 8224, 1 - NONE, 4096, -BIG, -2, -HALF]):
        ms(v("BI", j, j + 1), float(x))
        bias[x] = v("BI", j, j + 1)
    ms(v("SEL"), 1.0)
    ms(v("ONE"), 1.0)
    select(v("SEL"), v("SEL"), [[-1, 16], [-16, 8], [0, 16]], A.is_equal, 0.0)
    select(v("PM"), v("ONE", 0, 256), [[0, 2], [-1, 8], [-8, 16]], A.is_equal, 0.0)
    pi = v("PI")
    pj = lambda j: v("PJ", j, j + 1)
    pf = lambda j: v("PF", j, j + 1)
    ts(pj(0), pi, 112, None, A.bitwise_and)
    ts(pj(1), pi, 15, None, A.bitwise_and)
    ts(pj(2), pi, 4, 1, A.logical_shift_right, A.bitwise_and)
    ts(pj(3), pi, 3, None, A.logical_shift_right)
    ts(pj(4), pi, 7, None, A.bitwise_and)
    ts(pj(5), pi, 3, 1, A.logical_shift_right, A.bitwise_and)
    ts(pj(6), pi, 1, None, A.bitwise_and)
    cp(v("PF", 0, 7), v("PJ", 0, 7))
    cp(pf(7), pi)
    g16, acol, pcol, jcol = pf(0), pf(1), pf(7), pf(9)
    ts(jcol, pf(3), -1.0, 15.0, A.mult, A.add)
    ts(pf(10), acol, float(W), None, A.add)
    ts(v("SP"), v("CI", 0, 4), float(WP), pf(10), A.mult, A.add)
    tt(pf(12), pf(2), pf(6), A.not_equal)
    ts(pf(13), pf(4), 16.0, pf(5), A.mult, A.add)
    ts(pf(14), pf(12), 144.0, pf(13), A.mult, A.add)
    ts(v("TRK"), v("CI", 0, 8), 2.0, pf(14), A.mult, A.add)
    ts(v("T1"), v("CI", 0, 8), pf(2), None, A.add)
    ts(v("T1"), v("T1"), 1, None, A.bitwise_and)
    ts(v("T3"), v("T1"), 144.0, acol, A.mult, A.add)
    tt(v("T4"), v("T3"), v("C16"), A.add)
    cp(v("TRB"), v("T4"))
    ts(v("GS"), v("C16"), g16, None, A.is_equal)
    ts(v("ID"), v("CIB"), pcol, None, A.is_equal)
    for nm_, x in [("IDM", -1.0), ("ID32", 1.0), ("IM64", -64.0), ("I16K", 2 * BIG), ("IM8K", -BIG), ("I8K", BIG), ("IH", 2 / BIG),
                   ("IHM", -2 / BIG), ("I1536", float(HALF)), ("I2", 2.0)]:
        act(v(nm_), v("ID"), scale=x)
    act(v("PMT"), v("PM"), scale=2.0 ** 23)
    act(v("PMD"), v("PM"), scale=2048.0)
    act(v("P4K"), v("PM", 0, 128), scale=4096.0)
    act(v("P21"), v("PM", 0, 128), scale=2.0 ** 21)
    ts(v("CJ"), v("CI"), 15, None, A.bitwise_and)
    ts(v("KC"), v("CJ", 0, 256), 128.0, None, A.mult)
    ms(v("XB", NONE, W), FAR)
    ts(v("RST"), v("CJ", 0, 256), 0.0, 2.0 ** 25, A.is_equal, A.mult)
    act(v("RS0"), v("RST", 0, 128), scale=-1.0)
    ts(v("DG"), v("CJ"), acol, None, A.is_equal)
    act(v("CP"), v("DG"), scale=-BIG, bias=bias[4096])
    act(v("CQ"), v("DG"), scale=BIG, bias=bias[-BIG])
    sv = v("CI", 1, 9)
    ts(v("T2"), sv, acol, None, A.add)
    ts(v("T2"), v("T2"), 15, None, A.bitwise_and)
    ts(v("SHT"), v("T2"), g16, None, A.add)
    ts(v("T3"), sv, acol, None, A.is_gt)
    ts(v("T5"), sv, -1.0, 16.0, A.mult, A.add)
    tt(v("T4"), v("T3"), v("T5"), A.mult)
    ts(v("RTT"), v("T4"), pcol, None, A.add)
    for s in range(8):
        ts(v("CIR", 128 * s, 128 * s + 128), v("CIB"), v("SHT", s, s + 1), -1.0, A.is_equal, A.mult)
        ts(v("RT", 128 * s, 128 * s + 128), v("CIB"), v("RTT", s, s + 1), BIG, A.is_equal, A.mult)
    select(v("CIR"), v("CIR"), [[0, 8], [-1, 128]], A.not_equal, 1.0)
    ts(v("KN", 0, 16), v("CI", 0, 16), 0.0, -4096.0, A.mult, A.add)
    ts(v("KN", 16, 32), v("CI", 0, 16), 0.0, float(HALF - NONE), A.mult, A.add)
    ms(v("NE"), 0.0)
    for nm_ in TABLES:
        ms(v(nm_, W, WP), 0.0)
    for c, (a, b) in enumerate(blocks((512,) * (W // 512))):
        pd = v("PD%d" % (c % 2))
        ts(v("F1", a, b), v("NMI", a, b), -float(HALF), CM, A.add, A.add)
        act(v("M0", a, b), v("F1", a, b), scale=2.0 ** -12, bias=bias[-CM / 4096])
        act(pd, v("M0", a, b), scale=4096.0, bias=bias[NONE])
        tt(v("NT", a, b), pd, v("NMI", a, b), A.subtract)
    ms(v("M0", NONE, W), -1.0)
    cp(v("WU0"), v("WIN"))
    ts(v("VW0", 0, 16), v("WIN"), -1.0, float(NONE - HALF), A.mult, A.add)
    ts(v("THR"), v("THI", 0, 1), 2048.0, None, A.mult)
    ts(v("TH2"), v("THI", 0, 1), 2048.0, None, A.mult)
    for a, b in blocks((W // 6,) * 6):
        select(v("XT", a, b), v("XB", a, b), [[0, b - a]], A.is_ge, 0.0)

    Nw = v("NT", 0, W)
    NP, EP = 16, 272

    def turn(at, dst):
        tr(v(dst, 0, 128), v("NE", at, at + 128))
        tr(v(dst, 128, 288), v("NE", at - 16, at + 144))

    def spread(ps, at, src, st=True, sp=True):
        for a in range(16):
            mm(v(ps, at + a, at + 16 * src["n"], 16), v("SEL", 128 * a, 128 * a + 128), src, st, sp if not st and a == 15 else st)
        merge(16)

    def reduce16(ps, at, src, h):
        for a in range(16):
            mm(v(ps, at + a, at + 128, 16), v(src, 2048 * h + a, 2048 * h + 2048, 16), v("GS"))
        merge(16)

    def hv(name, h, k=128):
        return v(name, k * h, k * h + k)

    def copy(out, a):
        select(out, a, [[0, a["n"]]], A.is_ge, 0.0)

    def repeat(name, h):
        for k in (128, 256):
            copy(v(name, 512 * h + k, 512 * h + 2 * k), v(name, 512 * h, 512 * h + k))

    def compare(out, win, off, name, h, wide):
        for a, b in blocks(wide):
            tt(v(out, 2048 * h + 128 * a, 2048 * h + 128 * b), ind(win, v(off, 128 * h + 8 * a, 128 * h + 8 * b)),
               v(name, 512 * h, 512 * h + 128 * (b - a)), A.is_equal)

    def listen(t, h):
        z, vw, pk = hv("Z%d" % t, h), "VW%d" % t, "PK%d" % h
        wu, trn = hv("WU%d" % t, h, 8), "TR%d" % h
        Xw, Mw = v("XB") if t == 0 else v("XT", 0, W), v("M%d" % (t % 2), 0, W)
        if t:
            ts(wu, hv(vw, h, 8), -1.0, float(NONE - HALF), A.mult, A.add)
        act(v("NE", EP + 128 * h, EP + 128 * h + 128), ind(Mw, wu))
        spread("PS", 128 * h, hv(vw, h, 8))
        act(hv("WB", 4 * h), hv("PS", h), scale=1.0, bias=bias[HALF])
        repeat("WB", h)
        turn(EP + 128 * h, trn)
        cp(hv("OFF", h), ind(v(trn), v("TRK")))
        compare("EQ", Nw, "OFF", "WB", h, WIDE[h if t else 0])
        ns = 4 - NV[t][h]
        for i in range(4 * h, 4 * h + 4):
            xg, ab, pd = hv("XG", i, 512), hv("AB", i, 512), "PD%d" % (i % 2)
            if i - 4 * h >= ns:
                if i - 4 * h == ns:
                    copy(hv("ZR", 4 * h), z)
                    repeat("ZR", h)
                tt(xg, ind(Xw, hv("OFF", i, 32)), hv("ZR", h, 512), A.subtract)
                act(ab, xg, AF.Abs)
                continue
            if (i - 4 * h) % GW == 0:
                e = min(i + GW, 4 * h + ns)
                act(v("XG", 512 * i, 512 * e), ind(Xw, v("OFF", 32 * i, 32 * e)))
            group((v(pd), v("ID"), xg), *[(hv(pd, k), v("IDM"), z) for k in range(4)])
            merge(5)
            act(ab, v(pd), AF.Abs)
        act(hv("EF", h), ind(v(trn), v("TRB")), scale=1.0, bias=bias[8224])
        act(hv("HI", h), hv("EF", h), scale=2.0 ** -6, bias=bias[-0.5])
        reduce16("PE", 128 * h, "EQ", h)
        act(hv("TT", h), hv("PE", h), AF.Relu, -1.0, bias[1])
        reduce16("PR", 128 * h, "AB", h)
        cp(hv("DC", h), hv("PR", h))
        group((v(pk, 0, 256), v("ID"), v("KC")), (v(pk, 0, 128), v("ID"), hv("HI", h)),
              (v(pk, 128, 256), v("ID32"), hv("EF", h)), (v(pk, 128, 256), v("IM64"), hv("HI", h)),
              (v(pk, 0, 256), hv("TT", h), v("PMT")), (v(pk, 0, 256), hv("DC", h), v("PMD")))
        scan(hv("SC", h, 256), v("RST"), v(pk, 0, 256), A.add, A.min)
        ts(hv("AN", h, 16), v("SC", 256 * h + 15, 256 * h + 256, 16), 127, None, A.bitwise_and)
        ts(hv("OH", h, 8), hv("AN", 2 * h, 8), 64.0, -32.0 - HALF, A.mult, A.add)
        tt(hv(vw, 2 + h, 8), hv("OH", h, 8), hv("AN", 2 * h + 1, 8), A.add)
        ts(hv("OU", h, 8), hv(vw, 2 + h, 8), float(HALF), None, A.add)
        ts(hv(vw, 4 + h, 8), v("SC", 256 * h + 143, 256 * h + 256, 16), v("THR"), BIG, A.is_lt, A.mult)

    def speak(t, h):
        vw, trn, ou = "VW%d" % t, "TS%d" % h, hv("OU", h, 8)
        Xw, Mw = v("XB") if t == 0 else v("XT", 0, W), v("M%d" % (t % 2), 0, W)
        act(v("NE", NP + 128 * h, NP + 128 * h + 128), ind(Nw, ou))
        if h == 0:
            spread("PS", 256, v(vw, 16, 24))
            act(hv("OB", 0), hv("PS", 2), scale=1.0, bias=bias[HALF])
        else:
            mm(v("PD0"), v("I1536"), v("ONE"), True, False)
            spread("PD0", 0, v(vw, 16, 48), False, True)
            act(v("HB"), v("PD0", 256, 512), scale=1.0, bias=bias[-HALF])
            act(hv("OB", 4), hv("PD0", 1))
        repeat("OB", h)
        act(hv("XO%d" % t, h), ind(Xw, ou))
        if h == 1:
            move(t, v("Z%d" % (t + 1)), v("XO%d" % t), "az%d" % t)
        turn(NP + 128 * h, trn)
        ts(hv("OF2", h), ind(v(trn), v("TRK")), -1.0, float(NONE), A.mult, A.add)
        act(hv("UL", h), ind(v(trn), v("TRB")), scale=1.0, bias=bias[-HALF])
        compare("EQ2", Mw, "OF2", "OB", h, WIDE[1])
        for i in range(4 * h, 4 * h + 4, GW):
            act(v("CN", 512 * i, 512 * (i + GW)), ind(Mw, v("OF2", 32 * i, 32 * (i + GW))), AF.Relu, 1.0, bias[1 - NONE])

    def choose(t, h):
        reduce16("PR", 256 + 128 * h, "CN", h)
        act(hv("CB", h), hv("PR", 2 + h), scale=16.0, bias=jcol)
        reduce16("PE", 256 + 128 * h, "EQ2", h)
        act(hv("SG", h), hv("PE", 2 + h), AF.Sign, 1.0, bias[-0.5])
        o = v("PK1" if h else "PS", 384, 512)
        group((o, v("ID32"), hv("UL", h)), (o, hv("CB", h), v("P4K")), (o, hv("SG", h), v("P21")))
        scan(hv("SC2", h), v("RS0"), o, A.add, A.max)
        tt(hv("WI", h, 8), v("SC2", 128 * h + 15, 128 * h + 128, 16), hv("VW%d" % t, h, 8), A.max)
        ts(hv("WA", h, 8), hv("WI", h, 8), CM, CM, A.add, A.subtract)
        src, dst = "WS%d" % t, "VW%d" % (t + 1)
        tt(hv(src, h, 8), hv("WI", h, 8), hv("WA", h, 8), A.subtract)
        if t == RO - 1:
            ts(hv("WFS", h, 8), hv(src, h, 8), -1.0, float(NONE - HALF), A.mult, A.add)
            src, dst = "WFS", "WF"
        move(t, hv(dst, h, 8), hv(src, h, 8), "aw%d_%d" % (t, h))

    def prepare(t):
        last = t == RO - 1
        vw, z, xo = "VW%d" % t, v("Z%d" % t), v("XO%d" % t)
        tabs = ["M%d" % (1 - t % 2)] + ([] if last else ["XT"]) + ["NT"]
        one = v("ONE", 0, 256)
        wo = v(vw, 0, 32)
        for s in range(8):
            mm(hv("PK0", s, 32), hv("CIR", s), wo)
        group((hv("PK0", 8, 32), v("ID"), wo), (hv("PK0", 8, 32), v("ID"), v("KN")))
        merge(10)
        if EES and not last:
            act(v("AE"), v("PK0", 0, 288), AF.Abs)
            act(v("EE"), v("AE"), AF.Relu, -1.0, bias[1])
        else:
            ts(v("EE"), v("PK0", 0, 288), 0.0, None, A.is_equal)
        acc, aw, ao = hv("PK0", 9, 32), hv("PK0", 18, 16), hv("PK0", 19, 16)
        group(*[(acc, hv("RT", s), hv("EE", s, 32)) for s in range(8)], (acc, v("I8K"), hv("EE", 8, 32)),
              (aw, v("IDM"), v(vw, 0, 16)), (ao, v("ID"), v(vw, 16, 32)))
        merge(11)
        for j, x in enumerate(tabs):
            at = j // 2
            ts(v("SO", j + min(j, 1), 64, 4), ao if j else aw, float((HALF if j else NONE - HALF) + at * WP),
               v("SP", at, at + 1), A.add, A.min)
        if not last:
            o, a = v("S1"), v("PK1", 256, 272)
            mm(a, v("ONE", 0, 128), v(vw, 32, 48))
            add("s", lambda o=o, a=a: S.activation(ap(v("JK")), ap(a), AF.Identity, scale=1 / BIG, accum_out=ap(o)), o, [a], 105)
            ops[-1]["w"] += v("JK")["rg"]
            cp(v("S2"), o)
            ts(v("S3"), v("S2"), 31, None, A.bitwise_and)
            ts(v("THR"), v("S3"), 2048.0, v("TH2"), A.mult, A.add)
        q, qw = v("PQ", 0, 256), v("PQ", 256, 512)
        for j in range(2):
            copy(hv("Q2", j, 16), v(vw, 0, 16))
        mm(v("PQ"), v("I1536"), v("ONE"), True, False)
        spread("PQ", 0, v("Q2"), False, False)
        mm(q, v("ID"), v("CQ", t, t + 256), False, False)
        mm(q, v("IDM"), v("HB"), False, True)
        tt(v("EW", 0, 256), v("NE", NP, NP + 256), qw, A.is_equal)
        p, c = v("PQ", 256, 512), v("PD0", 0, 256)
        if not last:
            lo, hi = hv("PD1", 0, 256), hv("PD1", 1, 256)
            group((hi, v("I2"), one), (hi, v("ID"), xo), (hi, v("IHM"), v("HB")))
            group((lo, v("ID"), xo), (lo, v("IH"), v("HB")))
            tt(part("VA", 1), z, hi, A.min)
            act(part("VB", 1), lo, scale=1.0, bias=bias[-2])
        group((p, v("ID"), v("CP", t, t + 256)), (p, v("IDM"), v("HB")), (p, v("I16K"), v("EW", 0, 256)))
        tt(part("VA", len(tabs) - 1), v("NE", NP, NP + 256), p, A.min)
        act(part("VB", len(tabs) - 1), q, AF.Relu)
        tt(v("EW", 256, 512), v("NE", EP, EP + 256), c, A.is_equal)
        group((c, v("ID"), v("HB")), (c, v("IM8K"), v("EW", 256, 512)))
        act(part("VB", 0), c, scale=NONE / BIG)
        copy(part("VA", 0), v("NE", EP, EP + 256))
        for b in range(15, -1, -1):
            k = len(tabs)
            tt(ind(v(tabs[0]), v("SO", 4 * b, 4 * b + 1)), col("VA", b, 0, 1), col("VB", b, 0, 1), A.max)
            tt(ind(v("TB", (4 - k) * WP, 3 * WP), v("SO", 4 * b + 2, 4 * b + 1 + k)), col("VA", b, 1, k), col("VB", b, 1, k), A.max)

    for t in range(RO):
        rnd[0] = t
        phase[0] = "c"
        dma("y", v("M%d" % (1 - t % 2), 0, W), v("M%d" % (t % 2), 0, W), 512 * W,
            ext(None, "law%d_1" % (t - 1)) if t else v("XB"))
        for name, f in (("l", listen), ("s", speak)):
            if t == RO - 1 and f is speak:
                ms(v("XT", NONE, W), 255.0)
            for h in range(2):
                phase[0] = name + "AB"[h]
                f(t, h)
        phase[0] = "w"
        prepare(t)
        for h in range(2):
            phase[0] = "e" + "AB"[h]
            choose(t, h)
    phase[0] = "z"
    for c, (a, b) in enumerate(blocks((256, 256) + (512,) * (W // 512 - 1))):
        pd = v("PD%d" % (c % 2), 0, b - a)
        act(pd, v("M0", a, b), scale=4096.0, bias=bias[NONE])
        tt(v("F1", a, b), pd, v("NT", a, b), A.subtract)
    ms(v("F1", NONE, W), float(NONE + 4096 * NONE))
    for a, b in blocks(STORES):
        dma("y", ext(T.ynm[:, a:b], "ynm", a, b), v("F1", a, b), 512 * (b - a))
    for name, src, size in (("yz", "Z%d" % RO, 65536), ("yw", "WF", 8192)):
        dma("y", ext(T[name][:], name), v(src), size, v("F1", NONE, W))
    return ops


def hazards(ops):
    acc = {}
    for i, o in enumerate(ops):
        pre = {}
        both = [(x, False) for x in sorted(set(o["r"]))] + [(x, True) for x in sorted(set(o["w"]))]
        for (buf, a, b), wr in both:
            bank = buf in PSUM
            for (j, a2, b2, w2) in acc.get(buf, []):
                hit = a < b2 and a2 < b and (wr or w2)
                if hit or bank:
                    pre[j] = pre.get(j, False) or hit or ops[j]["q"] != o["q"]
        for (buf, a, b), wr in both:
            l = acc.setdefault(buf, [])
            if buf in PSUM:
                l[:] = [e for e in l if ops[e[0]]["q"] == o["q"]][-6:]
            elif wr:
                l[:] = [e for e in l if not (a <= e[1] and e[2] <= b)]
            l.append((i, a, b, wr))
        if o["kind"] == "ext":
            pre = {o["from"]: False}
        if o["kind"] == "dma" and o["q"] == "y" and not pre:
            pre = {j: False for j in range(i) if ops[j]["q"] == "y"}
        o["pre"] = {j: w for j, w in pre.items() if ops[j]["kind"] != "rem" or o["kind"] == "ext"}


def one_pass(res, dur, nxt, npre, key, ready0):
    n = len(res)
    left, ready, start = list(npre), list(ready0), [0.0] * n
    lines = {q: ([], []) for q in set(res)}
    done = [False] * n
    late = []
    for i in sorted(range(n), key=lambda i: key[i]):
        done[i] = True
        if left[i]:
            continue
        late.append(i)
        while late:
            j = late.pop()
            t, d = ready[j], dur[j]
            if d:
                bs, es = lines[res[j]]
                k = len(bs)
                while k and es[k - 1] > t:
                    k -= 1
                while k < len(bs) and bs[k] < t + d:
                    t = max(t, es[k])
                    k += 1
                bs.insert(k, t)
                es.insert(k, t + d)
            start[j] = t
            for s, la in nxt[j]:
                if ready[s] < t + d + la:
                    ready[s] = t + d + la
                left[s] -= 1
                if left[s] == 0 and done[s]:
                    late.append(s)
    return start


def improve(res, dur, succ, npre, r0, key, mates, steps, heat, rng):
    n = len(res)
    line = {}
    for i in range(n):
        if res[i] is not None:
            line.setdefault(res[i], []).append(i)

    def place(i):
        return key[i]

    def times():
        nx, left = [-1] * n, list(npre)
        for l in line.values():
            l.sort(key=place)
            for a, b in zip(l, l[1:]):
                nx[a] = b
                left[b] += 1
        head, by = list(r0), [-1] * n
        order = [i for i in range(n) if not left[i]]
        end, last = 0.0, 0
        for i in order:
            e = head[i] + dur[i]
            if e > end:
                end, last = e, i
            for s, la in succ[i]:
                if head[s] < e + la:
                    head[s], by[s] = e + la, i
                left[s] -= 1
                if not left[s]:
                    order.append(s)
            s = nx[i]
            if s >= 0:
                if head[s] < e:
                    head[s], by[s] = e, i
                left[s] -= 1
                if not left[s]:
                    order.append(s)
        if len(order) < n:
            return None
        pairs = []
        while by[last] >= 0:
            if nx[by[last]] == last and mates[last]:
                pairs.append((by[last], last))
            last = by[last]
        return end, head, pairs, nx

    best = cur = times()
    free = [i for i in range(n) if mates[i]]
    for it in range(steps):
        r = rng.rand(4)
        if r[0] < 0.8 and cur[2]:
            u, w = cur[2][int(r[1] * len(cur[2]))]
        else:
            u = free[int(r[1] * len(free))]
            w = cur[3][u]
            if w < 0:
                continue
        l = sorted(line[res[u]], key=place)
        k, far = l.index(u), int(rng.geometric(0.45)) - 1
        gaps = [a for a in range(max(1, k - 24), k + 1) if cur[1][l[a]] - cur[1][l[a - 1]] - dur[l[a - 1]] > 60]
        if r[2] > 0.7 and gaps:
            a = gaps[-1 - far % len(gaps)]
            x, new = w, (key[l[a - 1]] + key[l[a]]) / 2
        elif r[2] < 0.35:
            a = min(len(l) - 1, k + 1 + far)
            x, new = u, (key[l[a]] + (key[l[a + 1]] if a + 1 < len(l) else key[l[a]] + 100)) / 2
        else:
            a = max(0, k - far)
            x, new = w, (key[l[a]] + (key[l[a - 1]] if a else key[l[a]] - 100)) / 2
        d, old = new - key[x], [key[i] for i in mates[x]]
        for i in mates[x]:
            key[i] += d
        got = times()
        if got is not None and got[0] <= cur[0] - heat * (1 - it / steps) * np.log(r[3]):
            cur = got
            if got[0] < best[0]:
                best = got
        else:
            for i, y in zip(mates[x], old):
                key[i] = y
    return best[0], best[1]


def schedule(ops):
    n = len(ops)
    res = ["D" if o["kind"] == "dma" else o["q"] for o in ops]
    dur = [C["hold"] if o["kind"] == "rem" else o["dur"] for o in ops]
    dur[[o["kind"] for o in ops].index("rem")] += C["once"]
    succ, pred, older = [[] for _ in ops], [[] for _ in ops], []
    for i, o in enumerate(ops):
        las = {}
        for j, w in sorted(o["pre"].items()):
            p = ops[j]
            la = 1 if (p["q"] == "p" and o["q"] == "p") or not w else C["lat"]
            la += C["dma"] if o["kind"] == "dma" and w else 0
            las[j] = la + (p["dur"] - C["hold"] if p["kind"] == "rem" else 0)
        older.append({j for j in las if j < i}.union(*[older[j] for j in las if j < i]))
        for j, la in las.items():
            if not any(k < i and j in older[k] and la <= dur[k] + l2 for k, l2 in las.items()):
                succ[j].append((i, la))
                pred[i].append((j, la))
    GRAPH[:] = [res, dur, succ, pred]
    npre = [len(p) for p in pred]
    r0 = [C["dma"] if res[i] == "D" else 0.0 for i in range(n)]
    where, nth, alike = {}, {}, {}
    for i, o in enumerate(ops):
        k = (o["lab"], o["rnd"])
        nth[k] = nth.get(k, -1) + 1
        where[o["lab"], nth[k], o["rnd"]] = i
    behind, left = [list(x) for x in succ], list(npre)
    for q in ROUND:
        row = []
        for t in range(-1, RO):
            for word in (LAST if t == RO - 1 else ROUND)[q].split():
                lab, _, js = word.strip("+-").partition(":")
                js = [int(j) for j in (js or "0").split("-")]
                for j in range(js[0], js[-1] + 1):
                    i = where.pop((q + lab, j, t + {"+": 1, "-": -1}.get(word[0], 0)), None)
                    if i is not None:
                        row.append(i)
                        alike.setdefault((q + lab, j, t == RO - 1), []).append(i)
        for a, b in zip(row, row[1:]):
            behind[a].append((b, 0))
            left[b] += 1
    count, tail = list(left), [0.0] * n
    order = [i for i in range(n) if not count[i]]
    for i in order:
        for s, _ in behind[i]:
            count[s] -= 1
            if not count[s]:
                order.append(s)
    assert len(order) == n, [ops[i]["lab"] for i in range(n) if count[i]][:12]
    for i in reversed(order):
        tail[i] = dur[i] + max([la + tail[s] for s, la in behind[i]], default=0.0)
    start = one_pass(res, dur, behind, left, [-x for x in tail], r0)
    rng = np.random.RandomState(SEED)
    for steps, heat, rounds in STEPS:
        mates = [[i] if rounds is None or ops[i]["rnd"] in rounds else [] for i in range(n)]
        if rounds is None:
            for l in alike.values():
                for i in l:
                    mates[i] = l
        end, start = improve(res, dur, succ, npre, r0, list(start), mates, steps, heat, rng)
    order = sorted(range(n), key=lambda i: (start[i], i))
    first = [i for i in order if ops[i]["kind"] == "dma" and not any(ops[i]["pre"].values())]
    return first + [i for i in order if i not in set(first)], (end, order, start)


def emit(g, T, ops, order):
    Q = {"v": g.vector, "s": g.scalar, "p": g.tensor, "g": g, "y": g.sync}
    at = {i: k for k, i in enumerate(order)}
    known = {q: {} for q in Q}

    def sem_of(p):
        return p["sem"] if p["kind"] != "c" else "c" + p["q"]

    for i in order:
        o = ops[i]
        if o["kind"] == "ext":
            o["clock"] = {o["sem"]: at[i]}
            continue
        kn = known[o["q"]]
        waits = {}
        need = [j for j, w in o["pre"].items() if w and not (ops[j]["q"] == "p" and o["q"] == "p")]
        for j in sorted(need, key=lambda j: -at[j]):
            p = ops[j]
            if kn.get(sem_of(p), -1) >= at[j]:
                continue
            waits[sem_of(p)] = j
            p["mark"] = True
            for s2, k2 in p["clock"].items():
                kn[s2] = max(kn.get(s2, -1), k2)
        o["waits"] = waits
        o["clock"] = dict(kn)
        if o["kind"] != "rem":
            o["clock"][sem_of(o)] = at[i]
    count = {}
    for i in order:
        o = ops[i]
        if o["kind"] == "c" and o.get("mark"):
            count[o["q"]] = count.get(o["q"], 0) + 1
            o["val"] = count[o["q"]]
        elif o["kind"] != "c":
            o["val"] = o["cnt"]
    for i in order:
        o = ops[i]
        if o["kind"] == "ext":
            continue
        for s, j in o["waits"].items():
            Q[o["q"]].wait_ge(T.sem[s], ops[j]["val"])
        ins = o["fn"]()
        if o["kind"] == "dma":
            ins.then_inc(T.sem[o["sem"]], 16)
        elif o["kind"] == "c" and o.get("mark"):
            ins.then_inc(T.sem["c" + o["q"]], 1)
    for o in ops:
        if o["kind"] in ("dma", "ext") and not o.get("mark"):
            g.wait_ge(T.sem[o["sem"]], o["cnt"])


ORDER = []
GRAPH = []


def rank_program(g, core, T, topo):
    if T.rank_of(core) is None:
        return
    ops = build(g, core, T, topo)
    hazards(ops)
    if not ORDER:
        ORDER.extend(schedule(ops)[0])
    emit(g, T, ops, ORDER)
